import numpy as np, ml_dtypes
CORES = [16,17,18,19,150,151]
N = 6
BF = ml_dtypes.bfloat16
def gentries(a):
    return np.ascontiguousarray(a.reshape(8, 16, -1).transpose(0, 2, 1)).reshape(8, -1)
def gtable(e):
    e = np.asarray(e); return np.ascontiguousarray(e.reshape(8, -1, 16).transpose(0, 2, 1)).reshape(128, -1).astype(np.int32)
W, NB, T, CA, LV, LI, LG = 4096, 4096, 4, 5, 7, 2, 1
P, S = NB // 16, W // (NB // 16)
def parts(rng):
    return rng.integers(0, 256, (N, 8, 16, W)), rng.integers(0, 256, (N, 8, 16, P)), rng.integers(0, 16, (N, 8, 16)), rng.integers(0, W, (N, 8, NB)), rng.integers(0, W, (N, 8, NB))
def pack(x, z, w, a, b):
    return {"xt": np.reshape(x, (N, 128, W)).astype(np.float32).astype(BF), "zp": np.reshape(z, (N, 128, P)).astype(np.float32).astype(BF), "wl": np.reshape(w, (N, 128, 1)).astype(np.float32).astype(BF),
            "ba": np.stack([gtable(v) for v in a]), "bb": np.stack([gtable(v) for v in b])}
def setup_inputs(rng):
    x, z, w, a, b = parts(rng)
    return pack(x, z, w, a, np.where(rng.random(b.shape) < 0.125, a, b))
def setup_inputs_corners(rng):
    x, z, w, a, b = parts(rng); pol = 255 * (np.arange(8) & 1)
    good = rng.random((N, 8, W)) < 0.5; good[..., W - 4:W - 1] = False
    far = np.abs(pol[None, :, None, None] - rng.integers(128, 256, x.shape))
    x = np.where(good[:, :, None, :], pol[None, :, None, None], far)
    z = np.broadcast_to(pol[None, :, None, None], z.shape).copy()
    o = np.argsort(rng.random((N, 8, 16)), axis=-1); v = rng.choice(np.array([128, 200]), (N, 8, 16))
    x[..., W - 4] = 128; x[..., W - 3] = np.where(o < LV, v, 60); x[..., W - 2] = np.where(o < LV - 1, v, 60)
    own = np.arange(NB).reshape(P, 16)
    for q in range(N):
        for g in range(8):
            pa, pb = rng.integers(0, W, 8192), rng.integers(0, W, 8192); pc = ((pa * pb >> 5) + pa + 37 * pb) & (W - 1); k = good[q, g]
            yes = np.flatnonzero(~k[pa] & ~k[pb] & k[pc] & (pa != pb)); no = np.flatnonzero((k[pa] | k[pb]) & (pa != pb))
            n = rng.choice(np.array([0, 1, CA - 1, CA, CA + 1, 16]), P); n[P - 1] = CA; n[0] = 16; n[2] = CA + 1
            m = np.argsort(rng.random((P, 16)), axis=1) < n[:, None]
            i = np.where(m, yes[rng.integers(0, len(yes), (P, 16))], no[rng.integers(0, len(no), (P, 16))]); aa, bb = pa[i], pb[i]
            kp = rng.integers(0, 12, P); kp[0] = 9; kp[P - 1] = 9; kp[2] = 9; kp[1] = 2; kp[P - 2] = 3; kp[3] = 0; kp[P - 3] = 1
            s = (kp == 0) | (kp == 2) | (kp == 3); aa[s] = own[s]; bb[s] = own[s]
            e = (W - 1) * rng.integers(0, 2, (P, 16)); aa[kp == 1] = e[kp == 1]; bb[kp == 1] = e[kp == 1]
            aa[kp == 4] = e[kp == 4]; bb[kp == 4] = W - 1 - e[kp == 4]
            slot = rng.integers(0, 16, P)
            for c, col in ((2, W - 3), (3, W - 2)):
                r = np.flatnonzero(kp == c); aa[r, slot[r]] = W - 4; bb[r, slot[r]] = col; z[q, g][:, r] = x[q, g, :, col][:, None]
            a[q, g] = aa.reshape(-1); b[q, g] = bb.reshape(-1)
    b[1] = a[1]
    w[:, 0] = 0; w[:, 1] = 15; w[:, 2] = 0; w[:, 2, 15] = 15; w[:, 3] = 15 * rng.integers(0, 2, (N, 16))
    return pack(x, z, w, a, b)
def setup_inputs_ends(rng):
    kind = rng.integers(0, 4, (N, 8, 1, W)); x = 255 * np.where(kind > 1, rng.integers(0, 2, (N, 8, 16, W)), kind)
    x = np.where((kind == 3) & (rng.random(x.shape) < 0.25), x ^ 1, x)
    hi = np.arange(8) & 1
    x[..., 0] = 255 * (1 - hi)[None, :, None]; x[..., W - 1] = 255 * hi[None, :, None]; x[0, ::2, :, W - 37] = 255
    cc = (((W - 1) * (W - 2) >> 5) + W - 1 + 37 * (W - 2)) & (W - 1)
    x[:, 1::2, :, W - 2] = 255; x[:, 1::2, :, cc] = 255
    zk = rng.integers(0, 3, (N, 8, 1, P)); z = 255 * np.where(zk == 2, rng.integers(0, 2, (N, 8, 16, P)), zk)
    w = 15 * rng.integers(0, 2, (N, 8, 16)); w[:, 1] = 15; w[:, 7] = 15; w[:, 2] = 0
    sh = (N, 8, NB)
    a = np.where(rng.random(sh) < 0.8, (W - 1) * rng.integers(0, 2, sh), rng.integers(0, W, sh))
    b = np.where(rng.random(sh) < 0.8, (W - 1) * rng.integers(0, 2, sh), rng.integers(0, W, sh))
    n = rng.integers(10, 17, (8, P, 1)); n[:, 0] = 16; n[:, P - 1] = 16
    m = (np.argsort(rng.random((8, P, 16)), axis=-1) < n).reshape(8, NB); top = ((W - 1) * hi)[:, None]
    a[0] = np.where(m, top, a[0]); b[0] = np.where(m, W - 1 - top, b[0])
    z[0] = 255 * (np.argsort(rng.random((8, 16, P)), axis=1) < rng.integers(0, 7, (8, 1, P)))
    for q in range(1, N):
        for g in (1, 7):
            for i, va, vb, vz in ((0, 0, W - 1, 255), (P - 1, 0, W - 1, 255), (1, W - 1, 0, 0), (P - 2, W - 1, 0, 0), (2, W - 1, W - 2, 0), (P - 3, W - 1, W - 2, 0)):
                a[q, g, 16 * i:16 * i + 16] = va; b[q, g, 16 * i:16 * i + 16] = vb; z[q, g, :, i] = vz
    return pack(x, z, w, a, b)
def setup_inputs_spread(rng):
    x, z, w, a, b = parts(rng)
    x = (np.exp2(8 * rng.random((N, 8, 1, W))) * rng.random(x.shape)).astype(np.int64)
    z = (np.exp2(8 * rng.random((N, 8, 1, P))) * rng.random(z.shape)).astype(np.int64)
    w = w >> rng.integers(0, 5, w.shape)
    a = (W * rng.random(a.shape) ** rng.integers(1, 5, (N, 8, 1))).astype(np.int64); b = (W * rng.random(b.shape) ** rng.integers(1, 5, (N, 8, 1))).astype(np.int64)
    return pack(x, z, w, np.minimum(a, W - 1), np.minimum(b, W - 1))
def setup_inputs_ties(rng):
    x, z, w, a, b = parts(rng)
    base = rng.integers(0, 256, (N, 8, 16, 6)); base[:, ::2] = rng.choice(np.array([0, 1, 128, 254, 255]), (N, 4, 16, 6))
    x = np.take_along_axis(base, rng.integers(0, 6, (N, 8, 1, W)), 3)
    z = np.where(rng.random((N, 8, 1, P)) < 0.75, np.take_along_axis(base, rng.integers(0, 6, (N, 8, 1, P)), 3), z)
    m = rng.random((N, 8, P, 1)) < 0.25
    a = a.reshape(N, 8, P, 16); b = b.reshape(N, 8, P, 16); b = np.where(rng.random(b.shape) < 0.125, a, b)
    a = np.where(m, a[..., :1], a).reshape(N, 8, NB); b = np.where(m, b[..., :1], b).reshape(N, 8, NB)
    return pack(x, z, w, a, b)
def check_inputs(d):
    bad = []
    for k, lo, hi in (("xt", 0, 255), ("zp", 0, 255), ("wl", 0, 15), ("ba", 0, W - 1), ("bb", 0, W - 1)):
        v = np.asarray(d[k]).astype(np.float64)
        if not np.all((v >= lo) & (v <= hi) & (v == np.floor(v))): bad.append("range of " + k)
    return bad
def reference(xt, zp, wl, ba, bb):
    X = xt.astype(np.float32).astype(np.int32).reshape(N, 8, 16, W); z = zp.astype(np.float32).astype(np.int32).reshape(N, 8, 16, P)
    w = wl.astype(np.float32).astype(np.int32).reshape(N, 8, 16, 1)
    L = [np.stack([gentries(v) for v in m]).astype(np.int32) for m in (ba, bb)]
    I = np.zeros((N, 8, NB), np.int32); G = np.zeros((N, 8, NB), np.int32); rej = [0] * N
    def before(m):
        m = m.astype(np.int32).reshape(8, P, 16)
        return (np.add.accumulate(m, axis=2) - m).reshape(8, NB)
    for t in range(T):
        now = [0] * N
        for q in range(N):
            s = (q + t) % N
            H = L[t % 2][q]; O = L[1 - t % 2][q]; C = ((H * O >> 5) + H + 37 * O) & (W - 1)
            h, o, c = [np.take_along_axis(X[s], v[:, None, :], 2) for v in (H, O, C)]
            zz = np.repeat(z[q], 16, axis=2); dh, do, dc = [np.add.reduce(np.abs(v - zz), axis=1) for v in (h, o, c)]
            live = H != O
            rec = live & (do <= np.minimum(dh, dc))
            want = live & ~rec & (dc < dh) & (G[q] < LG); am = want & (before(want) < CA)
            ins = live & ~rec & ~am
            ch = np.where(rec[:, None, :], o, np.where(am[:, None, :], c, h))
            V = np.add.reduce((ch - h).reshape(8, 16, P, 16), axis=3)
            ok = np.add.reduce((V >= 0).astype(np.int32), axis=1) >= LV
            now[s] = int(np.add.reduce((~ok).astype(np.int64), axis=None)); yes = np.repeat(ok, 16, axis=1)
            I[q] += ins | ((rec | am) & ~yes); G[q] += am & yes
            H2 = np.where(yes & rec, O, np.where(yes & am, C, H))
            sp = I[q] >= LI; v = np.where((before(sp) & 1) == 1, C, H)
            H2 = np.where(sp, v, H2); O2 = np.where(sp, v, O); I[q] = np.where(sp, 0, I[q])
            M = np.maximum.reduce(ch.reshape(8, 16, P, 16), axis=3); u = np.add.reduce(w[s] * M, axis=1) & (W - 1)
            O2 = np.where(live, O2, ((H * np.repeat(u, 16, axis=1) >> 5) + H + rej[s]) & (W - 1))
            L[t % 2][q] = H2; L[1 - t % 2][q] = O2
            if t < T - 1:
                z[q] = np.abs(z[q] - M)
                at = (S * np.arange(P)[None, :] + (u & (S - 1)))[:, None, :]
                np.put_along_axis(X[s], at, (np.take_along_axis(X[s], at, 2) + M) >> 1, 2)
        rej = now
    home = [(s - (T - 1)) % N for s in range(N)]
    ya, yb, yi, yg = [np.stack([gtable(m[q]) for q in home]).astype(np.float32) for m in (L[0], L[1], I, G)]
    return {"ya": ya, "yb": yb, "yi": yi, "yg": yg}

@@ -1,0 +1,628 @@
+from concourse.mybir import dt, AluOpType as ALU, ActivationFunctionType as ACT
+
+CH = [96, 96, 64]
+NCH = len(CH)
+OFF = [sum(CH[:j]) for j in range(NCH)]
+NM = max(CH)
+NB = 3
+READS = 4
+NENG = 8
+RELU = [(), (), ()]
+PH, PD, PC, DHV = 48, 48, 48, True
+
+SCRATCH = {
+    "X": ("sbuf", [128, 4096], "bfloat16"),
+    "li": ("sbuf", [128, 512], "int32"),
+    "wcol": ("sbuf", [128, 1], "bfloat16"),
+    "Eb": ("sbuf", [128, 144], "bfloat16"), "Ew": ("sbuf", [128, 144], "bfloat16"),
+    "GBb": ("sbuf", [128, 128], "bfloat16"), "Ib": ("sbuf", [128, 128], "bfloat16"),
+    "Ibn": ("sbuf", [128, 128], "bfloat16"), "Ib128": ("sbuf", [128, 128], "bfloat16"),
+    "Ibh": ("sbuf", [128, 128], "bfloat16"), "TrS": ("sbuf", [128, 128], "bfloat16"),
+    "Tr1": ("sbuf", [128, 128], "bfloat16"), "ones": ("sbuf", [128, 144], "bfloat16"),
+    "tmpw": ("sbuf", [128, 144], "bfloat16"), "tmpw2": ("sbuf", [128, 144], "bfloat16"),
+    "tmpt": ("sbuf", [128, 128], "bfloat16"),
+    "H1": ("sbuf", [128, 128], "float16"), "Hn": ("sbuf", [128, 128], "float16"),
+    "H2080": ("sbuf", [128, 128], "float16"), "H3232": ("sbuf", [128, 128], "float16"),
+    "H32": ("sbuf", [128, 128], "float16"), "m96": ("sbuf", [128, NM], "float16"),
+    "F32": ("sbuf", [128, 128], "float32"), "F32n": ("sbuf", [128, 128], "float32"),
+    "H2048": ("sbuf", [128, 128], "float16"), "H256": ("sbuf", [128, 128], "float16"),
+    "HK": ("sbuf", [128, 128], "float16"), "on16": ("sbuf", [128, NM], "float16"),
+    "F1": ("sbuf", [128, 128], "float32"), "FK": ("sbuf", [128, 128], "float32"),
+    "E2": ("sbuf", [128, 144], "bfloat16"), "En": ("sbuf", [128, 144], "bfloat16"),
+    "Wb": ("sbuf", [128, 128], "bfloat16"),
+    "bi": ("sbuf", [128, 32], "int32"), "base": ("sbuf", [128, 16], "int32"),
+    "RST": ("sbuf", [128, 16 * NM], "bfloat16"),
+    "kacc": ("sbuf", [128, 16], "float32"), "kcol": ("sbuf", [128, 1], "float32"),
+    "junk": ("sbuf", [128, NM], "bfloat16"),
+    "ul": ("sbuf", [128, 32], "int32"),
+    "nl": ("sbuf", [128, 32], "uint16"), "xv": ("sbuf", [128, 256], "int32"),
+    "oya": ("sbuf", [128, 256], "float32"), "oyb": ("sbuf", [128, 256], "float32"),
+    "oyi": ("sbuf", [128, 256], "float32"), "oyg": ("sbuf", [128, 256], "float32"),
+}
+for _t in range(READS):
+    SCRATCH["lu%d" % _t] = ("sbuf", [128, 512], "uint16")
+    SCRATCH["mz%d" % _t] = ("sbuf", [128, 768], "bfloat16")
+    if _t < READS - 1:
+        SCRATCH["su%d" % _t] = ("sbuf", [128, 512], "uint16")
+        SCRATCH["sz%d" % _t] = ("sbuf", [128, 768], "bfloat16")
+for _p in range(2):
+    SCRATCH["zs%d" % _p] = ("sbuf", [128, 16 * NM], "bfloat16")
+for _p in range(NB):
+    for _n in ("zr", "h", "do", "dc", "ah", "ao", "ac", "ch", "rm"):
+        SCRATCH["%s%d" % (_n, _p)] = ("sbuf", [128, 16 * NM], "bfloat16")
+    SCRATCH["f%d" % _p] = ("sbuf", [128, 8 * NM], "float32")
+    SCRATCH["b%d" % _p] = ("sbuf", [128, 9 * NM], "bfloat16")
+    SCRATCH["s%d" % _p] = ("sbuf", [128, 4 * NM], "float16")
+    SCRATCH["i%d" % _p] = ("sbuf", [128, 3 * NM], "int32")
+    SCRATCH["u%d" % _p] = ("sbuf", [128, 2 * NM], "uint16")
+for _p in range(8):
+    SCRATCH["p%d" % _p] = ("psum", [128, 512], "float32")
+
+SEMAPHORES = ["qv", "qt", "qa", "qg", "left"]
+SEMAPHORES += ["x%d" % k for k in range(4)] + ["la%d" % k for k in range(NCH)] + ["lz", "lw"]
+SEMAPHORES += ["rl%d_%d" % (t, j) for t in range(1, READS) for j in range(NCH)]
+SEMAPHORES += ["rz%d_%d" % (t, j) for t in range(1, READS) for j in range(NCH)]
+SEMAPHORES += ["out%d" % k for k in range(4 * NCH)]
+
+EST = {"cy": 1.0, "gam": 1.56, "scat": 3.0, "pec": 0.5, "fv": 0.0, "fa": 0.0, "ft": 0.0, "wake": 80.0, "net": 6500.0, "dma": 2000.0, "iss": 500.0}
+SHIFT = {'s12': '5:-56 16:123 13:-23 3:-20 8:-37 9:102 14:-23 2:-20 x:-8 6:25 4:4 15:20', 's11': '9:-22 12:208 10:-58 18:36 14:-14 6:-7 13:-23 1:-35 7:12 17:45 0:-12 5:-8 11:12 16:-1 x:-1 15:19 8:-24', 'ch2': '2:-22 13:111 x:-159 12:57 5:-37 0:-40 4:-12 1:-8 11:76 8:17 14:15 3:-53 9:-5', 'vo0': '10:-47 11:139 13:-44 2:69 8:39 12:43 0:-144 15:-6 3:5 9:9 6:20 5:6 7:1 x:1 1:33', 'vo2': '1:40 10:129 14:-103 0:93 8:-32 11:-46 12:16 3:98 15:-43 2:6 5:4 13:-5 7:15 6:-5 9:-7 4:-27', 'ch1': 'x:1 12:5 1:115 0:38 13:-66 6:-51 14:16 5:-35 9:-31 8:-12 4:15 7:17 3:36 11:7', 'ch0': '13:22 14:1 1:84 0:1 6:16 12:213 8:72 x:9 4:39 3:-7 7:16 9:-2', 'c': '19:24 5:22 27:51 26:-14 40:23 37:128 43:22 1:-71 39:94 9:-65 25:-18 4:55 38:-36 30:22 33:-73 42:-17 29:-154 10:60 12:80 23:-11 2:132 0:-95 17:-13 11:11 41:1 7:-21 49:20 6:32 15:19 14:4 48:35 28:1 45:-15 20:36 3:-24 44:-8 8:29 18:-13 22:-26', 'kc0': '2:-2 1:-8 x:-286 0:-23', 'pre0': '13:-16 12:48 5:-12 3:128 8:-3 10:-34 1:-44 x:-1 0:-29', 'pre2': '7:-64 12:-19 2:-21 8:-43 6:-2 1:27 0:-22 x:-4 10:-14 3:-12 13:-8', 'up2': '7:29 6:-8 x:24 8:-33 1:-21 9:-150 0:-12 10:-75 12:-11 3:15 4:26 14:10 5:-7', 'up1': '10:4 14:-122 x:101 1:164 4:-110 6:-25 12:46 11:2 9:-36 3:-6 8:-11 0:5 2:33', 'up0': '14:-82 9:10 2:28 5:-45 8:-91 0:-6 6:-132 13:25 3:-29 11:107 12:-7', 'po0': '6:-12 0:54 8:-23 5:-10 7:57 4:40 9:-38 10:54 3:35 x:14', 'pre1': '1:-16 7:4 4:4 5:71 12:42 9:1 3:1 11:-1 0:-15', 'vo1': '15:-72 x:54 11:-15 13:20 12:-52 14:-37 8:-43 9:132 4:-102 0:-55 10:-24 7:12 6:-35 1:-32 2:-52 5:51 3:19', 'po1': '0:33 9:63 7:23 1:12 5:-78 3:-3 x:3 4:-24 8:-6 10:-46 2:16', 's10': '5:118 0:110 13:40 3:-30 2:-12 12:-15 16:62 11:-7 15:-7 9:3 17:-35 6:-99 7:4 14:59', 'po2': '5:11 2:-4 7:25 10:-50 6:-55 x:29 4:41 9:11 1:-16 3:22 8:74 0:2', 'sc192': '0:88 x:4', 'sc0': '0:-11 x:-10'}
+BONUS = {}
+for _p, _s in SHIFT.items():
+    for _e in _s.split():
+        _i, _v = _e.split(":")
+        BONUS[_p if _i == "x" else _p + ":" + _i] = 100.0 * int(_v)
+
+
+def price(w, E):
+    k, n = w[0], w[1]
+    if k == "v":
+        return E["fv"] + E["cy"] * max(64.0, n)
+    if k == "vg":
+        return 50.0 + E["cy"] * E["gam"] * n
+    if k == "vs":
+        return 50.0 + E["cy"] * E["scat"] * n
+    if k == "a":
+        return E["fa"] + E["cy"] * n
+    if k == "ag":
+        return 65.0 + E["cy"] * E["gam"] * n
+    if k == "t":
+        return E["pec"] * n + E["ft"] * w[2]
+    return E[k] if k in E else n
+
+
+def cv(n, f=1.0):
+    return ("v", n * f)
+
+
+def ca(n, f=1.0):
+    return ("a", n) if f == 1.0 else ("ag", n)
+
+
+def schedule(ops, E, bonus):
+    N = len(ops)
+    W = E["wake"]
+    cost = [price(o["w"], E) for o in ops]
+    succ = [[] for _ in range(N)]
+    for k in range(N):
+        for d in ops[k]["deps"]:
+            succ[d].append(k)
+    bot = [0.0] * N
+    for k in range(N - 1, -1, -1):
+        bot[k] = cost[k] + W + max([bot[s] for s in succ[k]] + [0.0])
+    pri = [bot[k] + bonus.get(ops[k]["tag"], 0.0) + bonus.get(ops[k]["tag"].split(":")[0], 0.0) for k in range(N)]
+    left = [len(o["deps"]) for o in ops]
+    ready, free, order = {}, {}, []
+    rt, fin = [0.0] * N, [0.0] * N
+    for k in range(N):
+        ready.setdefault(ops[k]["q"], [])
+        if left[k] == 0:
+            ready[ops[k]["q"]].append(k)
+    while len(order) < N:
+        best = None
+        for q, lst in ready.items():
+            if not lst:
+                continue
+            f = 0.0 if q == "n" else free.get(q, 0.0)
+            st = max(f, min([rt[k] for k in lst]))
+            if best is None or st < best[0]:
+                best = (st, q, lst)
+        st, q, lst = best
+        k = max([k for k in lst if rt[k] <= st + 1e-9], key=lambda k: pri[k])
+        lst.remove(k)
+        dma = q in ("s", "s2")
+        free[q] = st + (60.0 if dma else cost[k])
+        fin[k] = st + cost[k]
+        order.append(k)
+        for s in succ[k]:
+            left[s] -= 1
+            rt[s] = max(rt[s], fin[k] + (W if ops[s]["deps"][k] else 0.0))
+            if left[s] == 0:
+                ready[ops[s]["q"]].append(s)
+    return order, fin
+
+
+def rank_program(g, core, T, topo):
+    rank = T.rank_of(core)
+    if rank is None:
+        return
+    ops = []
+    hist = {}
+    cur = ["c", 0]
+
+    def phase(name, j):
+        cur[0], cur[1] = "%s%d" % (name, j), 0
+
+    def R(name, a, b):
+        return (name, a, b)
+
+    def add(q, fn, rd, wr, cost, sem=None, inc=1, after=()):
+        k = len(ops)
+        deps = {}
+        for isw, regs in ((False, rd), (True, wr)):
+            for (nm, a, b) in regs:
+                bank = nm[0] == "p" and nm[1:].isdigit()
+                for (d, da, db, dw) in hist.get(nm, ()):
+                    same = ops[d]["q"] == q
+                    over = a < db and da < b
+                    if bank and not same:
+                        deps[d] = True
+                    elif over and (isw or dw):
+                        deps[d] = deps.get(d, False) or dw or not same
+        for d in after:
+            deps[d] = True
+        for isw, regs in ((False, rd), (True, wr)):
+            for (nm, a, b) in regs:
+                lst = hist.setdefault(nm, [])
+                if isw:
+                    bank = nm[0] == "p" and nm[1:].isdigit()
+                    if not bank:
+                        lst = [e for e in lst if not (a <= e[1] and e[2] <= b)]
+                    else:
+                        lst = lst[-24:]
+                    hist[nm] = lst
+                lst.append((k, a, b, isw))
+        deps.pop(k, None)
+        w = ("dma", 0) if q in ("s", "s2") else cost if isinstance(cost, tuple) else ("x", cost)
+        ops.append({"q": q, "fn": fn, "deps": deps, "w": w, "sem": sem, "inc": inc, "tag": "%s:%d" % (cur[0], cur[1])})
+        cur[1] += 1
+        return k
+
+    def V(name, a, b, step=1):
+        return (name, a, b, step)
+
+    def ap(v):
+        if len(v) == 5:
+            o = v[4]
+            return T[v[0]][:, v[1]:v[2]].indirect(T[o[0]][:, o[1]:o[2]])
+        if v[3] == 1:
+            return T[v[0]][:, v[1]:v[2]]
+        return T[v[0]][:, v[1]:v[2]:v[3]]
+
+    def ind(win, off):
+        return (win[0], win[1], win[2], 1, off)
+
+    def regs(*vs):
+        r = []
+        for v in vs:
+            r.append((v[0], v[1], v[2]))
+            if len(v) == 5:
+                r.append((v[4][0], v[4][1], v[4][2]))
+        return r
+
+    def cnt(v):
+        if len(v) == 5:
+            return 16 * (v[4][2] - v[4][1])
+        return (v[2] - v[1] + v[3] - 1) // v[3]
+
+    two = ("bfloat16", "uint16", "float16")
+
+    def half(*vs):
+        return 0.5 if all(SCRATCH[v[0]][2] in two for v in vs) else 1.0
+
+    def tt(out, in0, in1, op):
+        n = cnt(out) if len(out) < 5 else cnt(in0)
+        if len(in0) == 5:
+            c = ("vg", n)
+        else:
+            c = cv(n, 1.0 if (in0[0][0] == "p" or in1[0][0] == "p") else 2.0)
+        return add("v", lambda: g.vector.tensor_tensor(ap(out), ap(in0), ap(in1), op), regs(in0, in1), regs(out), c)
+
+    def ts(out, in0, s1, op0, s2=None, op1=None):
+        rd = regs(in0) + [(s[0], s[1], s[2]) for s in (s1, s2) if isinstance(s, tuple)]
+
+        def emit():
+            a1 = ap(s1) if isinstance(s1, tuple) else s1
+            a2 = ap(s2) if isinstance(s2, tuple) else s2
+            if op1 is None:
+                return g.vector.tensor_scalar(ap(out), ap(in0), a1, None, op0)
+            return g.vector.tensor_scalar(ap(out), ap(in0), a1, a2, op0, op1)
+        return add("v", emit, rd, regs(out), cv(cnt(in0), half(out, in0)))
+
+    def cp(out, in_):
+        if len(out) == 5:
+            c = ("vs", cnt(in_))
+            return add("v", lambda: g.vector.tensor_copy(ap(out), ap(in_)), regs(in_) + [(out[4][0], out[4][1], out[4][2])], [(out[0], out[1], out[2])], c)
+        return add("v", lambda: g.vector.tensor_copy(ap(out), ap(in_)), regs(in_), regs(out), cv(cnt(in_), half(out, in_)))
+
+    def scan(out, d0, d1, o0, o1):
+        return add("v", lambda: g.vector.tensor_tensor_scan(ap(out), ap(d0), ap(d1), 0.0, o0, o1), regs(d0, d1), regs(out), cv(cnt(out), 0.5))
+
+    def fill(out, c):
+        return add("v", lambda: g.vector.memset(ap(out), c), [], regs(out), cv(cnt(out), half(out)))
+
+    def act(out, in_, func, bias=0.0, scale=1.0, acc=None):
+        n = cnt(out)
+        c = ca(n, 2.0 if len(in_) == 5 else 1.0)
+        wr = regs(out) + (regs(acc) if acc is not None else [])
+
+        def emit():
+            if acc is not None:
+                return g.scalar.activation(ap(out), ap(in_), func, bias=bias, scale=scale, accum_out=ap(acc))
+            return g.scalar.activation(ap(out), ap(in_), func, bias=bias, scale=scale)
+        return add("a", emit, regs(in_), wr, c)
+
+    def mm(groups, part=(True, True)):
+        first, final = part
+        rd, wr, c, m = [], [], 0.0, 0
+        for out, lst in groups:
+            wr += regs(out)
+            for l, r in lst:
+                rd += regs(l, r)
+                m += 1
+                c += max(64, cnt(r)) * (4 if SCRATCH[r[0]][2] == "float32" else 1)
+
+        def emit():
+            last = None
+            for out, lst in groups:
+                for k, (l, r) in enumerate(lst):
+                    last = g.tensor.matmul(ap(out), ap(l), ap(r), first and k == 0, final and k == len(lst) - 1)
+            return last
+        return add("t", emit, sorted(set(rd)), wr, ("t", c, m))
+
+    def gp(fn, rd, wr, c):
+        return add("g", fn, regs(*rd), regs(*wr), c)
+
+    def M128(name):
+        return V(name, 0, 128)
+
+    for k in range(4):
+        a, b = 1024 * k, 1024 * (k + 1)
+        add("s" if k % 2 else "s2", (lambda a=a, b=b, k=k: (g.sync if k % 2 else g.scalar).dma_start(T.X[:, a:b], T.xt[:, a:b])), [], [R("X", a, b)], 1500.0, "x%d" % k, 16)
+    for j in range(NCH):
+        o, n = OFF[j], CH[j]
+        add("s", (lambda o=o, n=n: g.sync.dma_start(T.li[:, 2 * o:2 * o + n], T.ba[:, o:o + n])), [], [R("li", 2 * o, 2 * o + n)], 1500.0, "la%d" % j, 16)
+        add("s", (lambda o=o, n=n: g.sync.dma_start(T.li[:, 2 * o + n:2 * o + 2 * n], T.bb[:, o:o + n])), [], [R("li", 2 * o + n, 2 * o + 2 * n)], 1500.0, "la%d" % j, 16)
+        add("s", (lambda o=o, n=n: g.sync.dma_start(T.mz0[:, 3 * o:3 * o + n], T.zp[:, o:o + n])), [], [R("mz0", 3 * o, 3 * o + n)], 1500.0, "la%d" % j, 16)
+    add("s", lambda: g.sync.dma_start(T.wcol[:], T.wl[:]), [], [R("wcol", 0, 1)], 1500.0, "lw", 16)
+    for k in ops:
+        if k["sem"] is not None and k["sem"].startswith("la"):
+            k["need"] = 48
+
+    fill(V("ones", 0, 144), 1.0)
+    gp(lambda: g.iota(T.bi[:, 0:16], [[0, 16]], 0, 16), [], [V("bi", 0, 16)], 200.0)
+    gp(lambda: g.iota(T.bi[:, 16:32], [[256, 16]], 0, 0), [], [V("bi", 16, 32)], 200.0)
+    W9 = V("ones", 0, 144)
+    gp(lambda: g.affine_select(T.tmpw[:], T.ones[:], [[-16, 9], [0, 16]], ALU.is_ge, 0.0, 0, 1), [W9], [V("tmpw", 0, 144)], 450.0)
+    gp(lambda: g.affine_select(T.tmpw2[:], T.tmpw[:], [[16, 9], [0, 16]], ALU.is_ge, 0.0, 15, -1), [V("tmpw", 0, 144)], [V("tmpw2", 0, 144)], 450.0)
+    cp(M128("GBb"), V("tmpw2", 0, 128))
+    gp(lambda: g.affine_select(T.Ib[:], T.GBb[:], [[1, 128]], ALU.is_equal, 0.0, 0, -1), [M128("GBb")], [M128("Ib")], 450.0)
+    gp(lambda: g.affine_select(T.Eb[:], T.tmpw2[:], [[0, 9], [1, 16]], ALU.is_equal, 0.0, -15, 0), [V("tmpw2", 0, 144)], [V("Eb", 0, 144)], 450.0)
+    gp(lambda: g.affine_select(T.Tr1[:], T.GBb[:], [[1, 128]], ALU.is_ge, 0.0, -1, -1), [M128("GBb")], [M128("Tr1")], 450.0)
+    for nm, c in (("H1", 1.0), ("Hn", -1.0), ("H2080", 2080.0), ("H3232", 3232.0), ("H32", 32.0), ("F32", 32.0), ("F32n", -32.0), ("H2048", 2048.0), ("Ibn", -1.0), ("Ib128", 128.0), ("Ibh", 0.5), ("H256", 256.0), ("F1", 1.0)):
+        ts(M128(nm), M128("Ib"), c, ALU.mult)
+    ts(M128("TrS"), M128("Tr1"), 0.21875, ALU.mult)
+    cp(V("on16", 0, NM), V("ones", 0, NM))
+    ts(V("m96", 0, NM), V("ones", 0, NM), -96.0, ALU.mult)
+    fill(V("RST", 0, 16 * NM), 1.0)
+    add("v", lambda: g.vector.memset(T.RST[:, 0:16 * NM:16], 0.0), [], [R("RST", 0, 16 * NM)], cv(NM))
+    for p in range(2):
+        act(V("zs%d" % p, 0, 16 * NM), V("RST", 0, 16 * NM), ACT.Copy, scale=0.0)
+    ts(V("Ew", 0, 144), V("Eb", 0, 144), V("wcol", 0, 1), ALU.mult)
+    ts(V("E2", 0, 144), V("Eb", 0, 144), 2.0, ALU.mult)
+    ts(V("En", 0, 144), V("Eb", 0, 144), -1.0, ALU.mult)
+    fill(M128("FK"), -0.5)
+    ts(M128("Wb"), M128("GBb"), V("wcol", 0, 1), ALU.mult)
+    ts(V("bi", 0, 16), V("bi", 0, 16), 255, ALU.bitwise_and)
+    tt(V("base", 0, 16), V("bi", 0, 16), V("bi", 16, 32), ALU.add)
+
+    def E(b, nm="Eb"):
+        return V(nm, 15 - b, 15 - b + 128)
+
+    nxt, prv = T.cores[(rank + 1) % len(T.cores)], T.cores[(rank - 1) % len(T.cores)]
+    sends = {}
+    X = V("X", 0, 4096)
+
+    def names(t, j):
+        q = t * NCH + j
+        p, o, n = q % NB, OFF[j], CH[j]
+        e = 16 * n
+        D = {"q": q, "p": p, "o": o, "n": n, "e": e}
+        for nm in ("zr", "h", "do", "dc", "ah", "ao", "ac", "ch", "rm"):
+            D[nm] = V("%s%d" % (nm, p), 0, e)
+
+        def slot(base, k, w=None):
+            return V("%s%d" % (base, p), k * NM, k * NM + (w or n))
+        for k, nm in enumerate(("dhs", "m1", "t1", "De", "jd", "sOm", "sO", "chf")):
+            D[nm] = slot("f", k)
+        for k, nm in enumerate(("rec", "w0", "wa", "am", "sg", "J", "sp", "nIo", "Gno")):
+            D[nm] = slot("b", k)
+        D["HO"] = V("s%d" % p, 0, 2 * n)
+        D["Hc"], D["Oc"] = V("s%d" % p, 0, n), V("s%d" % p, n, 2 * n)
+        D["stl"], D["Cc"] = slot("s", 2), slot("s", 3)
+        D["pm"], D["r"], D["p2"] = slot("i", 0), slot("i", 1), slot("i", 2)
+        D["Cu"], D["chu"] = slot("u", 0), slot("u", 1)
+        lu, mz = "lu%d" % t, "mz%d" % t
+        D["LU"] = V(lu, 2 * o, 2 * o + 2 * n)
+        D["Hu"], D["Ou"] = V(lu, 2 * o, 2 * o + n), V(lu, 2 * o + n, 2 * o + 2 * n)
+        D["z"], D["nI"], D["G"] = [V(mz, 3 * o + k * n, 3 * o + (k + 1) * n) for k in range(3)]
+        if t < READS - 1:
+            su, sz = "su%d" % t, "sz%d" % t
+            D["Hs"], D["Os"] = V(su, 2 * o + n, 2 * o + 2 * n), V(su, 2 * o, 2 * o + n)
+            D["zn"], D["nIn"], D["Gn"] = [V(sz, 3 * o + k * n, 3 * o + (k + 1) * n) for k in range(3)]
+            if t == 0:
+                D["J"] = D["nIn"]
+        else:
+            D["nIn"] = D["nIo"]
+            D["Gn"] = D["Gno"]
+
+        def ps(bk, k):
+            return V("p%d" % bk, k * n, k * n + n)
+        lb, db = 4 + q % 3, 2 + q % 2
+        for nm, k in (("OmH", 0), ("CmH", 1), ("Op", 2), ("HS", 2), ("S", 3), ("Y", 3), ("bp", 3), ("Hr", 4)):
+            D[nm] = ps(lb, k)
+        for nm, k in (("dh", 0), ("ddo", 1), ("ddc", 2), ("RG", 3), ("pf", 4), ("cp", 1), ("up", 2), ("zM", 3)):
+            D[nm] = ps(db, k)
+        D["UL"] = V("p%d" % db, 480, 480 + n // 16)
+        for nm, k in (("Vp", 0), ("X1", 1), ("X2", 2), ("sc", 3), ("H2", 3), ("S2", 4)):
+            D[nm] = ps(7, k)
+        return D
+
+    I1, In, F1 = M128("Ib"), M128("Ibn"), M128("F1")
+    H1, Hn = M128("H1"), M128("Hn")
+
+    def cut(n, w):
+        m = max(1, (n + w - 1) // w)
+        s = [2 * (n // 2 * i // m) for i in range(m + 1)]
+        return list(zip(s[:-1], s[1:]))
+
+    def sub(v, a, b, k=1):
+        return V(v[0], v[1] + k * a, v[1] + k * b)
+
+    def pre(t, j):
+        phase("pre", j)
+        D = names(t, j)
+        n = D["n"]
+        if t == 0:
+            li = V("li", 2 * D["o"], 2 * D["o"] + 2 * n)
+            cp(D["LU"], li)
+            ts(D["HO"], li, -2048.0, ALU.add)
+        else:
+            for nm, v in (("rl", D["LU"]), ("rz", V(D["z"][0], 3 * D["o"], 3 * D["o"] + 3 * n))):
+                k = add("n", None, [], regs(v), ("net", 0), "%s%d_%d" % (nm, t, j), NENG, after=[sends[(nm, t - 1, j)]])
+                ops[k]["soft"] = True
+            ts(D["HO"], D["LU"], -2048.0, ALU.add)
+        on = V("on16", 0, n)
+        mm([(D["Op"], [(H1, D["Oc"])]), (D["S"], [(M128("H2080"), D["Hc"]), (M128("H3232"), D["Oc"])]),
+            (D["OmH"], [(H1, D["Oc"]), (Hn, D["Hc"])]), (D["Hr"], [(H1, D["Hc"]), (M128("H2048"), on)])])
+        tt(D["pm"], D["Hc"], D["Op"], ALU.mult)
+        tt(D["pm"], D["pm"], D["S"], ALU.add)
+        ts(D["pm"], D["pm"], 5, ALU.arith_shift_right, 4095, ALU.bitwise_and)
+        cp(D["Cu"], D["pm"])
+        ts(D["stl"], D["OmH"], 0.0, ALU.is_equal)
+        tt(D["HS"], D["stl"], D["Hr"], ALU.mult)
+        tt(D["CmH"], D["pm"], D["Hr"], ALU.subtract)
+        zs = "zs%d" % (D["q"] % 2)
+        add("v", lambda: g.vector.tensor_copy(T[zs][:, 0:D["e"]:16], ap(D["z"])), regs(D["z"]), [R(zs, 0, D["e"])], cv(n, 0.5))
+        for a in range(0, D["e"], 512):
+            scan(V(D["zr"][0], a, a + 512), V("RST", a, a + 512), V(zs, a, a + 512), ALU.mult, ALU.add)
+
+    def s1(t, j):
+        D = names(t, j)
+        n, e = D["n"], D["e"]
+        phase("s1", j)
+        for a, b in cut(n, PH):
+            act(sub(D["h"], a, b, 16), ind(X, sub(D["Hu"], a, b)), ACT.Copy)
+        for dst, lst in (("do", "Ou"), ("dc", "Cu")):
+            for a, b in cut(n, PD):
+                tt(sub(D[dst], a, b, 16), ind(X, sub(D[lst], a, b)), sub(D["zr"], a, b, 16), ALU.subtract)
+        for k in range(n // 32):
+            a, b = 512 * k, 512 * k + 512
+            bk = V("p%d" % (k % 2), 0, 512)
+            mm([(bk, [(I1, V(D["h"][0], a, b)), (In, V(D["zr"][0], a, b))])])
+            act(V(D["ah"][0], a, b), bk, ACT.Abs)
+        for src, dst in (("do", "ao"), ("dc", "ac")):
+            for a, b in cut(n, PD):
+                if src in RELU[j]:
+                    ts(sub(D[dst], a, b, 16), sub(D[src], a, b, 16), 0.0, ALU.max)
+                else:
+                    act(sub(D[dst], a, b, 16), sub(D[src], a, b, 16), ACT.Abs)
+        for raw, src, dst in ((None, "ah", "dh"), ("do", "ao", "ddo"), ("dc", "ac", "ddc")):
+            if raw in RELU[j]:
+                mm([(D[dst], [(E(b, "En"), V(D[raw][0], b, e, 16)) for b in range(16)] +
+                     [(E(b, "E2"), V(D[src][0], b, e, 16)) for b in range(16)])])
+            else:
+                mm([(D[dst], [(E(b), V(D[src][0], b, e, 16)) for b in range(16)])])
+
+    def choice(t, j):
+        D = names(t, j)
+        n, e = D["n"], D["e"]
+        phase("ch", j)
+        cp(D["dhs"], D["dh"]) if DHV else act(D["dhs"], D["dh"], ACT.Copy)
+        tt(D["m1"], D["dhs"], D["ddc"], ALU.min)
+        tt(D["rec"], D["m1"], D["ddo"], ALU.is_ge)
+        tt(D["w0"], D["dhs"], D["ddc"], ALU.is_gt)
+        hb = M128("Ibh")
+        mm([(D["RG"], [(H1, D["stl"])] + ([(hb, D["G"]), (hb, V("ones", 0, n))] if t else []) + [(I1, D["rec"])])])
+        tt(D["t1"], D["rec"], D["OmH"], ALU.mult)
+        tt(D["wa"], D["w0"], D["RG"], ALU.is_gt)
+        mm([(D["pf"], [(M128("TrS"), D["wa"])])])
+        tt(D["am"], D["wa"], D["pf"], ALU.is_gt)
+        tt(D["cp"], D["am"], D["CmH"], ALU.mult)
+        tt(D["De"], D["t1"], D["cp"], ALU.add)
+        tt(D["chf"], D["De"], D["Hr"], ALU.add)
+        cp(D["chu"], D["chf"])
+        for a, b in cut(n, PC):
+            act(sub(D["ch"], a, b, 16), ind(X, sub(D["chu"], a, b)), ACT.Copy)
+
+    def upd(t, j):
+        D = names(t, j)
+        n, e, o = D["n"], D["e"], D["o"]
+        phase("up", j)
+        for a, b in cut(n, PC):
+            scan(sub(D["rm"], a, b, 16), V("RST", 16 * a, 16 * b), sub(D["ch"], a, b, 16), ALU.mult, ALU.max)
+        k = n // 16
+        c0 = o // 16
+        U0, U1 = V("ul", c0, c0 + k), V("ul", 16 + c0, 16 + c0 + k)
+        nl = V("nl", c0, c0 + k)
+        if t < READS - 1:
+            mm([(D["UL"], [(E(r, "Ew"), V(D["rm"][0], 16 * r + 15, e, 256)) for r in range(16)])])
+            cp(U0, D["UL"])
+            ts(U1, U0, 15, ALU.bitwise_and)
+            tt(U1, U1, V("base", c0, c0 + k), ALU.add)
+            cp(nl, U1)
+            xv = V("xv", o, o + n)
+            tt(xv, ind(X, nl), V(D["rm"][0], 15, e, 16), ALU.add)
+            ts(xv, xv, 1, ALU.arith_shift_right)
+            mm([(D["zM"], [(I1, D["z"]), (In, V(D["rm"][0], 15, e, 16))])])
+            act(D["zn"], D["zM"], ACT.Abs)
+        mm([(D["up"], [(M128("Wb"), V(D["rm"][0], 15, e, 16))])])
+        cp(D["p2"], D["up"])
+        ts(D["p2"], D["p2"], 4095, ALU.bitwise_and)
+        tt(D["p2"], D["p2"], D["HS"], ALU.mult)
+
+    def scat(t, o, n):
+        phase("sc", o)
+        cp(ind(X, V("nl", o // 16, (o + n) // 16)), V("xv", o, o + n))
+
+    def vote(t, j):
+        D = names(t, j)
+        n, e, o = D["n"], D["e"], D["o"]
+        phase("vo", j)
+        mm([(D["Vp"], [(In, V(D["h"][0], b, e, 16)) for b in range(16)])], (True, False))
+        mm([(D["Vp"], [(I1, V(D["ch"][0], b, e, 16)) for b in range(16)])], (False, True))
+        act(D["sg"], D["Vp"], ACT.Sign, bias=0.5)
+        GB = M128("GBb")
+        gr = [(D["X1"], [(GB, D["sg"]), (M128("Ib128"), D["rec"]), (M128("Ib128"), D["am"]), (M128("H256"), D["stl"])]),
+              (D["X2"], [(GB, D["sg"]), (M128("Ib128"), D["am"])] + ([(M128("Ib128"), D["G"])] if t else []))]
+        if t < READS - 1:
+            gr.append((D["sc"], [(GB, D["sg"])]))
+        mm(gr)
+        ts(D["J"], D["X1"], 126.0, ALU.is_ge)
+        act(D["Gn"], D["X2"], ACT.Sign, bias=3.0 if t else -125.0)
+        if t < READS - 1:
+            act(V("junk", 0, n), D["sc"], ACT.Sign, bias=3.0, acc=V("kacc", 8 * (t % 2) + j, 8 * (t % 2) + j + 1))
+        tt(D["jd"], D["J"], D["De"], ALU.mult)
+        if t:
+            mm([(D["Y"], [(I1, D["nI"]), (I1, D["J"])])])
+            act(D["sp"], D["Y"], ACT.Relu, bias=1.0, scale=-1.0)
+            act(D["nIn"], D["Y"], ACT.Square, bias=1.0, scale=-1.0)
+            mm([(D["bp"], [(M128("Tr1"), D["sp"])])])
+            tt(D["r"], D["sp"], D["bp"], ALU.mult)
+            ts(D["r"], D["r"], 1, ALU.bitwise_and)
+            tt(D["sO"], D["r"], D["CmH"], ALU.mult)
+            tt(D["sOm"], D["sp"], D["OmH"], ALU.mult)
+
+    def post(t, j):
+        D = names(t, j)
+        n, e, o = D["n"], D["e"], D["o"]
+        k, c0 = n // 16, o // 16
+        phase("po", j)
+        on = V("on16", 0, n)
+        L = [(H1, D["Hc"]), (F1, D["jd"])]
+        L2 = [(M128("H32"), D["Oc"]), (M128("H2048"), V("m96", 0, n))]
+        if t:
+            L += [(F1, D["sO"])]
+            L2 += [(M128("HK"), D["stl"]), (M128("HK"), D["stl"]), (M128("F32"), D["sO"]), (M128("F32n"), D["sOm"])]
+        mm([(D["H2"], L), (D["S2"], L2)])
+        if t < READS - 1:
+            ts(D["Hs"], D["H2"], 2048.0, ALU.add)
+        else:
+            ts(V("oyb", o, o + n), D["H2"], 2048.0, ALU.add)
+        tt(D["p2"], D["p2"], D["S2"], ALU.add)
+        ts(D["p2"], D["p2"], 5, ALU.arith_shift_right, 4095, ALU.bitwise_and)
+        if t < READS - 1:
+            cp(D["Os"], D["p2"])
+            su, sz = "su%d" % t, "sz%d" % t
+            rid, pid = topo.addr(nxt, core)
+            mask = sum(1 << x for x in topo.engines(core, nxt)[:NENG])
+            lu, mz = "lu%d" % (t + 1), "mz%d" % (t + 1)
+
+            def snd(src, dst, a, b, sem):
+                return lambda: g.remote_dma(T[dst][:, a:b], T[src][:, a:b], T.sem[sem], T.sem.left, pid, rid, mask)
+            sends[("rz", t, j)] = add("g", snd(sz, mz, 3 * o, 3 * o + 3 * n, "rz%d_%d" % (t + 1, j)), [R(sz, 3 * o, 3 * o + 3 * n)], [], 300.0, "left", NENG)
+            sends[("rl", t, j)] = add("g", snd(su, lu, 2 * o, 2 * o + 2 * n, "rl%d_%d" % (t + 1, j)), [R(su, 2 * o, 2 * o + 2 * n)], [], 300.0, "left", NENG)
+        else:
+            cp(V("oya", o, o + n), D["p2"])
+            act(V("oyi", o, o + n), D["nIn"], ACT.Identity, bias=1.0, scale=-1.0)
+            act(V("oyg", o, o + n), D["Gn"], ACT.Identity, bias=0.5, scale=0.5)
+            for m, (src, dst) in enumerate((("oya", "ya"), ("oyb", "yb"), ("oyi", "yi"), ("oyg", "yg"))):
+                add("s", (lambda src=src, dst=dst: g.sync.dma_start(T[dst][:, o:o + n], T[src][:, o:o + n])), [R(src, o, o + n)], [], 200.0, "out%d" % (4 * j + m), 16)
+
+    def kcalc(t):
+        phase("kc", 0)
+        b = 8 * (t % 2)
+        kb = "p%d" % (2 + (t * NCH + NCH - 1) % 2)
+        mm([(V(kb, 500, 501), [(M128("FK"), V("kacc", b + j, b + j + 1)) for j in range(NCH)])])
+        ts(V("kcol", 0, 1), V(kb, 500, 501), 16384.0, ALU.add)
+        ts(M128("HK"), M128("H1"), V("kcol", 0, 1), ALU.mult)
+
+    pre(0, 0)
+    for t in range(READS):
+        for j in range(NCH):
+            if t == 0 and j + 1 < NCH:
+                pre(0, j + 1)
+            s1(t, j)
+            if t and j + 1 < NCH:
+                pre(t, j + 1)
+            choice(t, j)
+            if j == NCH - 1 and t < READS - 1 and NCH > 1:
+                scat(t, 0, OFF[j])
+            upd(t, j)
+            if j == NCH - 1:
+                if t < READS - 1:
+                    scat(t, OFF[j], CH[j])
+                    pre(t + 1, 0)
+            vote(t, j)
+            post(t, j)
+        if t < READS - 1:
+            kcalc(t)
+
+    order, fin = schedule(ops, EST, BONUS)
+    N = len(ops)
+
+    eng = {"v": g.vector, "t": g.tensor, "a": g.scalar, "g": g, "s": g.sync, "s2": g.scalar}
+    own = {"v": "qv", "t": "qt", "a": "qa", "g": "qg"}
+    phys = {"s2": "a"}
+    total = {}
+    clk = {q: {} for q in ("v", "t", "a", "g", "s")}
+    val = [None] * N
+    opclk = [None] * N
+    for k in order:
+        o = ops[k]
+        q = phys.get(o["q"], o["q"])
+        if q == "n":
+            val[k] = (o["sem"], o["inc"])
+            opclk[k] = {o["sem"]: o["inc"]}
+            total[o["sem"]] = o["inc"]
+            continue
+        c = clk[q]
+        ds = [d for d, w in o["deps"].items() if w and ops[d]["sem"] != "left"]
+        ds.sort(key=lambda d: -fin[d])
+        for d in ds:
+            s, v = val[d]
+            if c.get(s, 0) < v:
+                eng[q].wait_ge(T.sem[s], v)
+                for s2, v2 in opclk[d].items():
+                    if c.get(s2, 0) < v2:
+                        c[s2] = v2
+        ins = o["fn"]()
+        s = o["sem"] or own[q]
+        total[s] = total.get(s, 0) + o["inc"]
+        if s != "left":
+            ins.then_inc(T.sem[s], o["inc"])
+        val[k] = (s, o.get("need", total[s]))
+        opclk[k] = dict(c)
+        if s != "left":
+            opclk[k][s] = val[k][1]
+    for s in sorted(total):
+        g.wait_ge(T.sem[s], total[s])

@@ -1,275 +1,426 @@
+import math
 from concourse.mybir import dt, AluOpType as ALU, ActivationFunctionType as ACT
 
-CH = [96, 96, 64]
-NCH = len(CH)
-OFF = [sum(CH[:j]) for j in range(NCH)]
-NM = max(CH)
+NM = 96
 NB = 3
 READS = 4
 NENG = 8
-RELU = [(), (), ()]
-PH, PD, PC, DHV = 48, 48, 48, True
+BIG = 16384.0
+CFG = {
+    "ch": [96, 96, 64],
+    "mode": ["PAA", "PRA", "PAA"],
+    "chq": ["aa", "aa", "av"],
+    "fast": [False, False, True],
+    "zq": ["vvv", "vvg", "vvg", "vvg"],
+    "tabs": [1, 2],
+    "rules": [],
+    "ps": [96, 96, 32], "nil": "v", "lists": "hoc",
+    "piece": 48, "pv": 32, "pabs": 48, "pt": 8, "dcq": "a", "uq": "a", "par": "a", "gj": "a", "zsq": "a", "rounds": 0,
+    "tries": 120000, "heat": 0.0007, "seed": 1, "auto": 2, "far": 1,
+}
+MAXCH = 4
+BANK = {"P": [0, 1], "C": [2, 3, 4], "L": [5, 6, 7]}
 
 SCRATCH = {
     "X": ("sbuf", [128, 4096], "bfloat16"),
     "li": ("sbuf", [128, 512], "int32"),
     "wcol": ("sbuf", [128, 1], "bfloat16"),
     "Eb": ("sbuf", [128, 144], "bfloat16"), "Ew": ("sbuf", [128, 144], "bfloat16"),
-    "GBb": ("sbuf", [128, 128], "bfloat16"), "Ib": ("sbuf", [128, 128], "bfloat16"),
-    "Ibn": ("sbuf", [128, 128], "bfloat16"), "Ib128": ("sbuf", [128, 128], "bfloat16"),
-    "Ibh": ("sbuf", [128, 128], "bfloat16"), "TrS": ("sbuf", [128, 128], "bfloat16"),
-    "Tr1": ("sbuf", [128, 128], "bfloat16"), "ones": ("sbuf", [128, 144], "bfloat16"),
-    "tmpw": ("sbuf", [128, 144], "bfloat16"), "tmpw2": ("sbuf", [128, 144], "bfloat16"),
-    "tmpt": ("sbuf", [128, 128], "bfloat16"),
-    "H1": ("sbuf", [128, 128], "float16"), "Hn": ("sbuf", [128, 128], "float16"),
-    "H2080": ("sbuf", [128, 128], "float16"), "H3232": ("sbuf", [128, 128], "float16"),
-    "H32": ("sbuf", [128, 128], "float16"), "m96": ("sbuf", [128, NM], "float16"),
-    "F32": ("sbuf", [128, 128], "float32"), "F32n": ("sbuf", [128, 128], "float32"),
-    "H2048": ("sbuf", [128, 128], "float16"), "H256": ("sbuf", [128, 128], "float16"),
-    "HK": ("sbuf", [128, 128], "float16"), "on16": ("sbuf", [128, NM], "float16"),
-    "F1": ("sbuf", [128, 128], "float32"), "FK": ("sbuf", [128, 128], "float32"),
-    "E2": ("sbuf", [128, 144], "bfloat16"), "En": ("sbuf", [128, 144], "bfloat16"),
-    "Wb": ("sbuf", [128, 128], "bfloat16"),
+    "E2": ("sbuf", [128, 144], "bfloat16"), "En": ("sbuf", [128, 144], "bfloat16"), "E2n": ("sbuf", [128, 144], "bfloat16"),
+    "ones": ("sbuf", [128, 144], "bfloat16"), "tmpw": ("sbuf", [128, 144], "bfloat16"), "tmpw2": ("sbuf", [128, 144], "bfloat16"),
+    "m96": ("sbuf", [128, NM], "float16"), "on16": ("sbuf", [128, NM], "float16"),
     "bi": ("sbuf", [128, 32], "int32"), "base": ("sbuf", [128, 16], "int32"),
     "RST": ("sbuf", [128, 16 * NM], "bfloat16"),
     "kacc": ("sbuf", [128, 16], "float32"), "kcol": ("sbuf", [128, 1], "float32"),
     "junk": ("sbuf", [128, NM], "bfloat16"),
+    "rm": ("sbuf", [128, 4096], "bfloat16"),
     "ul": ("sbuf", [128, 32], "int32"),
     "nl": ("sbuf", [128, 32], "uint16"), "xv": ("sbuf", [128, 256], "int32"),
     "oya": ("sbuf", [128, 256], "float32"), "oyb": ("sbuf", [128, 256], "float32"),
     "oyi": ("sbuf", [128, 256], "float32"), "oyg": ("sbuf", [128, 256], "float32"),
 }
+for _n in ("GBb", "Ib", "Ibn", "Ibh", "Ib128", "Ib256", "IbB", "IbBn", "IbH", "IbHn", "Ib4096n", "Ib144", "TrS", "Tr1", "Tr2", "Dm", "Wb", "GB15", "Ib16n"):
+    SCRATCH[_n] = ("sbuf", [128, 128], "bfloat16")
+for _n in ("H1", "Hn", "Hh", "H2080", "H3232", "H32", "H2048", "H256", "HK", "HB", "HBn"):
+    SCRATCH[_n] = ("sbuf", [128, 128], "float16")
+for _n in ("F1", "Fh", "F32", "F32n", "FK"):
+    SCRATCH[_n] = ("sbuf", [128, 128], "float32")
 for _t in range(READS):
     SCRATCH["lu%d" % _t] = ("sbuf", [128, 512], "uint16")
     SCRATCH["mz%d" % _t] = ("sbuf", [128, 768], "bfloat16")
     if _t < READS - 1:
         SCRATCH["su%d" % _t] = ("sbuf", [128, 512], "uint16")
-        SCRATCH["sz%d" % _t] = ("sbuf", [128, 768], "bfloat16")
+        SCRATCH["sz%d" % _t] = ("sbuf", [128, 1024], "bfloat16")
 for _p in range(2):
     SCRATCH["zs%d" % _p] = ("sbuf", [128, 16 * NM], "bfloat16")
 for _p in range(NB):
-    for _n in ("zr", "h", "do", "dc", "ah", "ao", "ac", "ch", "rm"):
+    for _n in ("zr", "xc", "xo", "xh", "mc", "mo", "mh"):
         SCRATCH["%s%d" % (_n, _p)] = ("sbuf", [128, 16 * NM], "bfloat16")
+    SCRATCH["ch%d" % _p] = ("sbuf", [128, 16 * NM], "bfloat16")
     SCRATCH["f%d" % _p] = ("sbuf", [128, 8 * NM], "float32")
-    SCRATCH["b%d" % _p] = ("sbuf", [128, 9 * NM], "bfloat16")
-    SCRATCH["s%d" % _p] = ("sbuf", [128, 4 * NM], "float16")
+    SCRATCH["b%d" % _p] = ("sbuf", [128, 10 * NM], "bfloat16")
+    SCRATCH["s%d" % _p] = ("sbuf", [128, 5 * NM], "float16")
     SCRATCH["i%d" % _p] = ("sbuf", [128, 3 * NM], "int32")
     SCRATCH["u%d" % _p] = ("sbuf", [128, 2 * NM], "uint16")
 for _p in range(8):
     SCRATCH["p%d" % _p] = ("psum", [128, 512], "float32")
 
 SEMAPHORES = ["qv", "qt", "qa", "qg", "left"]
-SEMAPHORES += ["x%d" % k for k in range(4)] + ["la%d" % k for k in range(NCH)] + ["lz", "lw"]
-SEMAPHORES += ["rl%d_%d" % (t, j) for t in range(1, READS) for j in range(NCH)]
-SEMAPHORES += ["rz%d_%d" % (t, j) for t in range(1, READS) for j in range(NCH)]
-SEMAPHORES += ["out%d" % k for k in range(4 * NCH)]
+SEMAPHORES += ["la0", "lb0", "lz0", "la1", "lb1", "lz1", "lx", "lw"]
+SEMAPHORES += ["rl%d_%d" % (t, j) for t in range(1, READS) for j in range(MAXCH)]
+SEMAPHORES += ["rz%d_%d" % (t, j) for t in range(1, READS) for j in range(MAXCH)]
+SEMAPHORES += ["out%d" % k for k in range(4 * MAXCH)]
 
-EST = {"cy": 1.0, "gam": 1.56, "scat": 3.0, "pec": 0.5, "fv": 0.0, "fa": 0.0, "ft": 0.0, "wake": 80.0, "net": 6500.0, "dma": 2000.0, "iss": 500.0}
-SHIFT = {'s12': '5:-56 16:123 13:-23 3:-20 8:-37 9:102 14:-23 2:-20 x:-8 6:25 4:4 15:20', 's11': '9:-22 12:208 10:-58 18:36 14:-14 6:-7 13:-23 1:-35 7:12 17:45 0:-12 5:-8 11:12 16:-1 x:-1 15:19 8:-24', 'ch2': '2:-22 13:111 x:-159 12:57 5:-37 0:-40 4:-12 1:-8 11:76 8:17 14:15 3:-53 9:-5', 'vo0': '10:-47 11:139 13:-44 2:69 8:39 12:43 0:-144 15:-6 3:5 9:9 6:20 5:6 7:1 x:1 1:33', 'vo2': '1:40 10:129 14:-103 0:93 8:-32 11:-46 12:16 3:98 15:-43 2:6 5:4 13:-5 7:15 6:-5 9:-7 4:-27', 'ch1': 'x:1 12:5 1:115 0:38 13:-66 6:-51 14:16 5:-35 9:-31 8:-12 4:15 7:17 3:36 11:7', 'ch0': '13:22 14:1 1:84 0:1 6:16 12:213 8:72 x:9 4:39 3:-7 7:16 9:-2', 'c': '19:24 5:22 27:51 26:-14 40:23 37:128 43:22 1:-71 39:94 9:-65 25:-18 4:55 38:-36 30:22 33:-73 42:-17 29:-154 10:60 12:80 23:-11 2:132 0:-95 17:-13 11:11 41:1 7:-21 49:20 6:32 15:19 14:4 48:35 28:1 45:-15 20:36 3:-24 44:-8 8:29 18:-13 22:-26', 'kc0': '2:-2 1:-8 x:-286 0:-23', 'pre0': '13:-16 12:48 5:-12 3:128 8:-3 10:-34 1:-44 x:-1 0:-29', 'pre2': '7:-64 12:-19 2:-21 8:-43 6:-2 1:27 0:-22 x:-4 10:-14 3:-12 13:-8', 'up2': '7:29 6:-8 x:24 8:-33 1:-21 9:-150 0:-12 10:-75 12:-11 3:15 4:26 14:10 5:-7', 'up1': '10:4 14:-122 x:101 1:164 4:-110 6:-25 12:46 11:2 9:-36 3:-6 8:-11 0:5 2:33', 'up0': '14:-82 9:10 2:28 5:-45 8:-91 0:-6 6:-132 13:25 3:-29 11:107 12:-7', 'po0': '6:-12 0:54 8:-23 5:-10 7:57 4:40 9:-38 10:54 3:35 x:14', 'pre1': '1:-16 7:4 4:4 5:71 12:42 9:1 3:1 11:-1 0:-15', 'vo1': '15:-72 x:54 11:-15 13:20 12:-52 14:-37 8:-43 9:132 4:-102 0:-55 10:-24 7:12 6:-35 1:-32 2:-52 5:51 3:19', 'po1': '0:33 9:63 7:23 1:12 5:-78 3:-3 x:3 4:-24 8:-6 10:-46 2:16', 's10': '5:118 0:110 13:40 3:-30 2:-12 12:-15 16:62 11:-7 15:-7 9:3 17:-35 6:-99 7:4 14:59', 'po2': '5:11 2:-4 7:25 10:-50 6:-55 x:29 4:41 9:11 1:-16 3:22 8:74 0:2', 'sc192': '0:88 x:4', 'sc0': '0:-11 x:-10'}
+EST = {"cy": 0.9, "gam": 1.56, "scat": 3.0, "pec": 0.46, "fv": 20.0, "fa": 20.0, "wake": 130.0, "net": 8000.0, "dma": 2000.0,
+       "big": 7500.0, "late": 9000.0, "iss": 600.0, "iss1": 4500.0}
+CASES = [{"cy": 0.9, "pec": 0.455, "fv": 15.0, "fa": 15.0, "wake": 140.0, "net": 5500.0},
+         {"cy": 0.95, "pec": 0.48, "gam": 1.15, "fv": 0.0, "fa": 0.0, "wake": 110.0, "net": 7000.0, "late": 11000.0, "dma": 3000.0},
+         {"cy": 1.1, "pec": 0.555, "gam": 2.0, "scat": 5.0, "fv": 15.0, "fa": 15.0, "wake": 170.0, "net": 6000.0, "big": 5500.0, "late": 6500.0}]
 BONUS = {}
-for _p, _s in SHIFT.items():
-    for _e in _s.split():
-        _i, _v = _e.split(":")
-        BONUS[_p if _i == "x" else _p + ":" + _i] = 100.0 * int(_v)
+RANK = {"c": -50, "zr0": 97, "pre0": 97, "s10": 0, "s10vg": -3, "ch0": 1, "top0": 2, "up0": 4, "vo0": 3, "po0": 2, "pre1": -0.5, "zr1": -0.5,
+        "s11": 6, "s11a": 5, "s11t": 5.7, "pre2": 5, "zr2": -2, "s12": 12, "ch1": 11, "ch1ag": 13, "ch1t": 15, "ch2": 12.5, "ch2t": 13.5,
+        "top2": 12.6, "tb192": 12.7, "sc0": 12.7, "sc192": 12.7, "top1": 13.1, "tb0": 6.2, "up1": 20, "vo1": 17, "po1": 20, "up2": 99,
+        "vo2": 91.7, "po2": 99, "kc0": 99.5}
+ORDER = {}
 
 
 def price(w, E):
-    k, n = w[0], w[1]
+    k, n = w
+    cy = E["cy"]
     if k == "v":
-        return E["fv"] + E["cy"] * max(64.0, n)
-    if k == "vg":
-        return 50.0 + E["cy"] * E["gam"] * n
-    if k == "vs":
-        return 50.0 + E["cy"] * E["scat"] * n
+        return E["fv"] + cy * max(64.0, n)
     if k == "a":
-        return E["fa"] + E["cy"] * n
-    if k == "ag":
-        return 65.0 + E["cy"] * E["gam"] * n
+        return E["fa"] + cy * n
     if k == "t":
-        return E["pec"] * n + E["ft"] * w[2]
-    return E[k] if k in E else n
+        return E["pec"] * n
+    if k == "g":
+        return 170.0 + 2 * cy * n
+    if k in ("vg", "ag"):
+        return (50.0 if k == "vg" else 65.0) + cy * E["gam"] * n
+    if k == "vs":
+        return 50.0 + cy * E["scat"] * n
+    return E[k]
 
 
-def cv(n, f=1.0):
-    return ("v", n * f)
-
-
-def ca(n, f=1.0):
-    return ("a", n) if f == 1.0 else ("ag", n)
-
-
-def schedule(ops, E, bonus):
-    N = len(ops)
-    W = E["wake"]
-    cost = [price(o["w"], E) for o in ops]
+def place(qs, pred, cost, hold, W, pri):
+    N = len(qs)
     succ = [[] for _ in range(N)]
     for k in range(N):
-        for d in ops[k]["deps"]:
-            succ[d].append(k)
-    bot = [0.0] * N
-    for k in range(N - 1, -1, -1):
-        bot[k] = cost[k] + W + max([bot[s] for s in succ[k]] + [0.0])
-    pri = [bot[k] + bonus.get(ops[k]["tag"], 0.0) + bonus.get(ops[k]["tag"].split(":")[0], 0.0) for k in range(N)]
-    left = [len(o["deps"]) for o in ops]
-    ready, free, order = {}, {}, []
+        for d, w in pred[k].items():
+            succ[d].append((k, W if w else 0.0))
+    left = [len(p) for p in pred]
+    ready, free, order = {q: [] for q in qs}, {q: 0.0 for q in qs}, []
     rt, fin = [0.0] * N, [0.0] * N
     for k in range(N):
-        ready.setdefault(ops[k]["q"], [])
         if left[k] == 0:
-            ready[ops[k]["q"]].append(k)
+            ready[qs[k]].append(k)
     while len(order) < N:
         best = None
         for q, lst in ready.items():
-            if not lst:
-                continue
-            f = 0.0 if q == "n" else free.get(q, 0.0)
-            st = max(f, min([rt[k] for k in lst]))
-            if best is None or st < best[0]:
-                best = (st, q, lst)
+            if lst:
+                st = max(free[q], min([rt[k] for k in lst]))
+                if best is None or st < best[0]:
+                    best = (st, q, lst)
         st, q, lst = best
         k = max([k for k in lst if rt[k] <= st + 1e-9], key=lambda k: pri[k])
         lst.remove(k)
-        dma = q in ("s", "s2")
-        free[q] = st + (60.0 if dma else cost[k])
+        free[q] = st + hold[k]
         fin[k] = st + cost[k]
         order.append(k)
-        for s in succ[k]:
+        for s, w in succ[k]:
             left[s] -= 1
-            rt[s] = max(rt[s], fin[k] + (W if ops[s]["deps"][k] else 0.0))
+            rt[s] = max(rt[s], fin[k] + w)
             if left[s] == 0:
-                ready[ops[s]["q"]].append(s)
+                ready[qs[s]].append(s)
     return order, fin
+
+
+def schedule(ops, E, rounds):
+    N = len(ops)
+    W = E["wake"]
+    qs = [o["q"] for o in ops]
+    cost = [price(o["w"], E) for o in ops]
+    hold = [0.0 if qs[k] == "n" else 60.0 if qs[k] in ("s", "s2") else cost[k] for k in range(N)]
+    pred = [o["deps"] for o in ops]
+    back = [{} for _ in range(N)]
+    for k in range(N):
+        for d, w in pred[k].items():
+            back[d][k] = w
+    bonus = [BONUS.get(o["tag"], 0.0) + BONUS.get(o["tag"].split(":")[0], 0.0) + BONUS.get(o["uid"], 0.0) + o.get("first", 0.0) for o in ops]
+    pri = [0.0] * N
+    for k in range(N - 1, -1, -1):
+        pri[k] = cost[k] + W + max([pri[s] for s in back[k]] + [0.0])
+    if RANK:
+        for k, o in enumerate(ops):
+            ph = o["tag"].split(":")[0]
+            pri[k] = -1e3 * (100 * o["t"] + RANK.get(ph + o["w"][0], RANK.get(ph, 0.0))) - k
+            bonus[k] = o.get("first", 0.0)
+    best = None
+    for r in range(rounds + 1):
+        order, fin = place(qs, pred, cost, hold, W, [pri[k] + bonus[k] for k in range(N)])
+        if best is None or max(fin) < max(best[1]):
+            best = (order, fin)
+        if r < rounds:
+            pri = place(qs, back, cost, hold, W, fin)[1]
+    return best
+
+
+def refine(ops, order, tries, heat):
+    N = len(ops)
+    q = ["vatgsn".find(o["q"][0] if o["q"] != "s2" else "a") for o in ops]
+    above, deps = [0] * N, []
+    for k in range(N):
+        keep = []
+        for d in sorted(ops[k]["deps"], reverse=True):
+            if not (above[k] >> d) & 1:
+                keep.append(d)
+            above[k] |= above[d] | (1 << d)
+        deps.append(keep)
+    cases = []
+    for c in CASES:
+        E = dict(EST, **c)
+        cost = [price(o["w"], E) for o in ops]
+        hold = [60.0 if o["q"] in ("s", "s2") else x for o, x in zip(ops, cost)]
+        cases.append((cost, hold, [[(d, E["wake"] if ops[k]["deps"][d] else 0.0) for d in deps[k]] for k in range(N)]))
+
+    def times(order, first, case, old, guess=None):
+        cost, hold, dw = case
+        fin, free = list(old), [None] * 5 + [0.0]
+        for k in reversed(order[:first]):
+            if free[q[k]] is None:
+                free[q[k]] = fin[k] - cost[k] + hold[k]
+                if None not in free[:4]:
+                    break
+        free = [f or 0.0 for f in free]
+        for j in range(first, N, 40):
+            for k in order[j:j + 40]:
+                x = q[k]
+                st = free[x]
+                for d, w in dw[k]:
+                    if fin[d] + w > st:
+                        st = fin[d] + w
+                fin[k] = st + cost[k]
+                if x < 5:
+                    free[x] = st + hold[k]
+            if guess is not None and j > guess + 80 and j + 40 < N:
+                gap = [fin[k] - old[k] for k in order[j - 80:j + 40]]
+                if max(gap) - min(gap) < 1e-3:
+                    if abs(gap[0]) > 1e-3:
+                        for k in order[j + 40:]:
+                            fin[k] += gap[0]
+                    break
+        return fin
+
+    def chain(order, case, fin):
+        cost, hold, dw = case
+        before, last = [None] * N, [None] * 6
+        for k in order:
+            before[k], last[q[k]] = last[q[k]], k
+        k, out = fin.index(max(fin)), []
+        while k is not None:
+            st, p = fin[k] - cost[k], None
+            for d, w in dw[k]:
+                if fin[d] + w >= st - 1e-6:
+                    p = d
+            if p is None and q[k] < 5 and st > 0:
+                p = before[k]
+                if p is not None:
+                    out.append((p, k))
+            k = p
+        return out
+
+    def shift(order, a, b, back):
+        seg = order[a:b + 1]
+        me = seg[-1] if back else seg[0]
+        take, mask, qs = {me}, above[me] if back else 1 << me, set()
+        for x in (reversed(seg[:-1]) if back else seg[1:]):
+            if ((mask >> x) & 1 if back else above[x] & mask) or q[x] in qs:
+                if q[x] == q[me]:
+                    return None
+                take.add(x)
+                mask |= above[x] if back else 1 << x
+                if q[x] < 5:
+                    qs.add(q[x])
+        return order[:a] + [x for x in seg if (x in take) == back] + [x for x in seg if (x in take) != back] + order[b + 1:]
+
+    seed = [CFG["seed"]]
+
+    def draw(n):
+        seed[0] = (seed[0] * 6364136223846793005 + 1442695040888963407) % 2 ** 64
+        return (seed[0] >> 33) % n
+
+    fins = [times(order, 0, c, [0.0] * N) for c in cases]
+    unit = [max(f) for f in fins]
+    now = 1.0
+    best = (now, order, fins[0])
+    done = 0
+    while done < tries:
+        i = draw(len(cases))
+        pairs = chain(order, cases[i], fins[i])
+        pos = [0] * N
+        for j, x in enumerate(order):
+            pos[x] = j
+        for _ in range(6):
+            done += 1
+            p, k = pairs[draw(len(pairs))]
+            a, b, back, more = pos[p], pos[k], draw(5) < 3, (0, 0, 1, 2, 3, 5, 8)[draw(7)]
+            j = a if back else b
+            ready = max([0.0] + [fins[i][d] + w for d, w in cases[i][2][k]]) if back and more > CFG["auto"] else None
+            while more and 0 < j < N - 1:
+                j += -1 if back else 1
+                x = order[j]
+                if q[x] == q[k]:
+                    if ready is not None and fins[i][x] - 0.5 * cases[i][0][x] < ready:
+                        break
+                    a, b, more = min(a, j), max(b, j), more - (ready is None)
+            if draw(10) < CFG["far"]:
+                run = {x: y for x, y in pairs} if not back else {y: x for x, y in pairs}
+                stops = [p if back else k]
+                while stops[-1] in run:
+                    stops.append(run[stops[-1]])
+                a, b, new = pos[p], pos[k], None
+                while new is None and stops:
+                    a, b = (pos[stops[-1]], b) if back else (a, pos[stops[-1]])
+                    new = shift(order, a, b, back)
+                    stops = stops[:len(stops) * 2 // 3]
+            else:
+                new = shift(order, a, b, back)
+            if new is None:
+                continue
+            room = -math.log((draw(10 ** 6) + 1) / 10 ** 6) * heat * 0.1 ** (done / tries) * len(unit)
+            lost, f2 = 0.0, list(fins)
+            for c in [i] + [c for c in range(len(unit)) if c != i]:
+                f2[c] = times(new, a, cases[c], fins[c], b)
+                lost += (max(f2[c]) - max(fins[c])) / unit[c]
+                if lost > room + 0.002:
+                    break
+            if lost <= room:
+                order, fins = new, f2 if draw(100) else [times(new, 0, c, f) for c, f in zip(cases, fins)]
+                s = now = sum(max(f) / u for f, u in zip(fins, unit)) / len(unit)
+                if s < best[0]:
+                    best = (s, order, fins[0])
+                break
+    return best[1:]
 
 
 def rank_program(g, core, T, topo):
     rank = T.rank_of(core)
     if rank is None:
         return
+    CH = CFG["ch"]
+    NCH = len(CH)
+    OFF = [sum(CH[:j]) for j in range(NCH)]
     ops = []
     hist = {}
-    cur = ["c", 0]
+    cur = ["c", 0, 0]
 
     def phase(name, j):
         cur[0], cur[1] = "%s%d" % (name, j), 0
 
-    def R(name, a, b):
-        return (name, a, b)
+    def meet(a, b):
+        if a[0] >= b[1] or b[0] >= a[1]:
+            return False
+        return not (a[2] == b[2] > 1 and a[0] % a[2] != b[0] % a[2])
 
-    def add(q, fn, rd, wr, cost, sem=None, inc=1, after=()):
+    def add(q, fn, rd, wr, w, sem=None, inc=1, after=()):
         k = len(ops)
         deps = {}
         for isw, regs in ((False, rd), (True, wr)):
-            for (nm, a, b) in regs:
-                bank = nm[0] == "p" and nm[1:].isdigit()
-                for (d, da, db, dw) in hist.get(nm, ()):
+            for r in regs:
+                bank = SCRATCH[r[0]][0] == "psum"
+                for (d, dr, dw) in hist.get(r[0], ()):
                     same = ops[d]["q"] == q
-                    over = a < db and da < b
                     if bank and not same:
                         deps[d] = True
-                    elif over and (isw or dw):
-                        deps[d] = deps.get(d, False) or dw or not same
+                    elif bank and q == "t":
+                        deps[d] = deps.get(d, False)
+                    elif (isw or dw) and meet(r[1:], dr):
+                        deps[d] = True
         for d in after:
             deps[d] = True
         for isw, regs in ((False, rd), (True, wr)):
-            for (nm, a, b) in regs:
-                lst = hist.setdefault(nm, [])
+            for r in regs:
+                lst = hist.setdefault(r[0], [])
                 if isw:
-                    bank = nm[0] == "p" and nm[1:].isdigit()
-                    if not bank:
-                        lst = [e for e in lst if not (a <= e[1] and e[2] <= b)]
+                    if SCRATCH[r[0]][0] == "psum":
+                        lst = lst[-30:]
                     else:
-                        lst = lst[-24:]
-                    hist[nm] = lst
-                lst.append((k, a, b, isw))
+                        lst = [e for e in lst if not (r[1] <= e[1][0] and e[1][1] <= r[2] and (r[3] == 1 or r[1:] == e[1]))]
+                    hist[r[0]] = lst
+                lst.append((k, r[1:], isw))
         deps.pop(k, None)
-        w = ("dma", 0) if q in ("s", "s2") else cost if isinstance(cost, tuple) else ("x", cost)
-        ops.append({"q": q, "fn": fn, "deps": deps, "w": w, "sem": sem, "inc": inc, "tag": "%s:%d" % (cur[0], cur[1])})
+        ops.append({"q": q, "fn": fn, "deps": deps, "w": w, "sem": sem, "inc": inc, "tag": "%s:%d" % (cur[0], cur[1]), "uid": k, "t": cur[2]})
         cur[1] += 1
         return k
 
     def V(name, a, b, step=1):
-        return (name, a, b, step)
+        return (name, a, b, step, (b - a + step - 1) // step, (slice(None), slice(a, b, step)), None)
 
     def ap(v):
-        if len(v) == 5:
-            o = v[4]
-            return T[v[0]][:, v[1]:v[2]].indirect(T[o[0]][:, o[1]:o[2]])
-        if v[3] == 1:
-            return T[v[0]][:, v[1]:v[2]]
-        return T[v[0]][:, v[1]:v[2]:v[3]]
+        if not isinstance(v, tuple):
+            return v
+        if v[6] is not None:
+            return T[v[0]][v[5]].indirect(ap(v[6]))
+        return T[v[0]][v[5]]
 
     def ind(win, off):
-        return (win[0], win[1], win[2], 1, off)
+        return win[:4] + (16 * off[4], win[5], off)
 
     def regs(*vs):
         r = []
         for v in vs:
-            r.append((v[0], v[1], v[2]))
-            if len(v) == 5:
-                r.append((v[4][0], v[4][1], v[4][2]))
+            if isinstance(v, tuple):
+                r.append(v[:4])
+                if v[6] is not None:
+                    r.append(v[6][:4])
         return r
 
-    def cnt(v):
-        if len(v) == 5:
-            return 16 * (v[4][2] - v[4][1])
-        return (v[2] - v[1] + v[3] - 1) // v[3]
-
-    two = ("bfloat16", "uint16", "float16")
+    def sub(v, a, b, k=1):
+        return V(v[0], v[1] + k * a, v[1] + k * b)
 
     def half(*vs):
-        return 0.5 if all(SCRATCH[v[0]][2] in two for v in vs) else 1.0
+        return 0.5 if all(SCRATCH[v[0]][2] in ("bfloat16", "uint16", "float16") for v in vs) else 1.0
 
     def tt(out, in0, in1, op):
-        n = cnt(out) if len(out) < 5 else cnt(in0)
-        if len(in0) == 5:
-            c = ("vg", n)
+        if in0[6] is not None:
+            c = ("vg", out[4])
         else:
-            c = cv(n, 1.0 if (in0[0][0] == "p" or in1[0][0] == "p") else 2.0)
+            c = ("v", out[4] * (1.0 if "psum" in (SCRATCH[in0[0]][0], SCRATCH[in1[0]][0]) else 2.0))
         return add("v", lambda: g.vector.tensor_tensor(ap(out), ap(in0), ap(in1), op), regs(in0, in1), regs(out), c)
 
     def ts(out, in0, s1, op0, s2=None, op1=None):
-        rd = regs(in0) + [(s[0], s[1], s[2]) for s in (s1, s2) if isinstance(s, tuple)]
-
         def emit():
-            a1 = ap(s1) if isinstance(s1, tuple) else s1
-            a2 = ap(s2) if isinstance(s2, tuple) else s2
             if op1 is None:
-                return g.vector.tensor_scalar(ap(out), ap(in0), a1, None, op0)
-            return g.vector.tensor_scalar(ap(out), ap(in0), a1, a2, op0, op1)
-        return add("v", emit, rd, regs(out), cv(cnt(in0), half(out, in0)))
+                return g.vector.tensor_scalar(ap(out), ap(in0), ap(s1), None, op0)
+            return g.vector.tensor_scalar(ap(out), ap(in0), ap(s1), ap(s2), op0, op1)
+        return add("v", emit, regs(in0, s1, s2), regs(out), ("v", out[4] * half(out, in0)))
 
     def cp(out, in_):
-        if len(out) == 5:
-            c = ("vs", cnt(in_))
-            return add("v", lambda: g.vector.tensor_copy(ap(out), ap(in_)), regs(in_) + [(out[4][0], out[4][1], out[4][2])], [(out[0], out[1], out[2])], c)
-        return add("v", lambda: g.vector.tensor_copy(ap(out), ap(in_)), regs(in_), regs(out), cv(cnt(in_), half(out, in_)))
+        fn = lambda: g.vector.tensor_copy(ap(out), ap(in_))
+        if out[6] is not None:
+            return add("v", fn, regs(in_, out[6]), [out[:4]], ("vs", in_[4]))
+        return add("v", fn, regs(in_), regs(out), ("vg", out[4]) if in_[6] is not None else ("v", out[4] * half(out, in_)))
 
     def scan(out, d0, d1, o0, o1):
-        return add("v", lambda: g.vector.tensor_tensor_scan(ap(out), ap(d0), ap(d1), 0.0, o0, o1), regs(d0, d1), regs(out), cv(cnt(out), 0.5))
+        return add("v", lambda: g.vector.tensor_tensor_scan(ap(out), ap(d0), ap(d1), 0.0, o0, o1), regs(d0, d1), regs(out), ("v", 0.5 * out[4]))
 
     def fill(out, c):
-        return add("v", lambda: g.vector.memset(ap(out), c), [], regs(out), cv(cnt(out), half(out)))
+        return add("v", lambda: g.vector.memset(ap(out), c), [], regs(out), ("v", out[4] * half(out)))
 
     def act(out, in_, func, bias=0.0, scale=1.0, acc=None):
-        n = cnt(out)
-        c = ca(n, 2.0 if len(in_) == 5 else 1.0)
-        wr = regs(out) + (regs(acc) if acc is not None else [])
-
         def emit():
             if acc is not None:
                 return g.scalar.activation(ap(out), ap(in_), func, bias=bias, scale=scale, accum_out=ap(acc))
             return g.scalar.activation(ap(out), ap(in_), func, bias=bias, scale=scale)
-        return add("a", emit, regs(in_), wr, c)
+        return add("a", emit, regs(in_), regs(out, acc), ("a" if in_[6] is None else "ag", out[4]))
 
-    def mm(groups, part=(True, True)):
-        first, final = part
-        rd, wr, c, m = [], [], 0.0, 0
+    def mm(groups, first=True, final=True):
+        rd, wr, c = [], [], 0.0
         for out, lst in groups:
             wr += regs(out)
             for l, r in lst:
                 rd += regs(l, r)
-                m += 1
-                c += max(64, cnt(r)) * (4 if SCRATCH[r[0]][2] == "float32" else 1)
+                c += max(64, r[4]) * (4 if SCRATCH[r[0]][2] == "float32" else 1)
 
         def emit():
             last = None
@@ -277,133 +428,149 @@ def rank_program(g, core, T, topo):
                 for k, (l, r) in enumerate(lst):
                     last = g.tensor.matmul(ap(out), ap(l), ap(r), first and k == 0, final and k == len(lst) - 1)
             return last
-        return add("t", emit, sorted(set(rd)), wr, ("t", c, m))
+        return add("t", emit, sorted(set(rd)), wr, ("t", c))
 
-    def gp(fn, rd, wr, c):
-        return add("g", fn, regs(*rd), regs(*wr), c)
+    def gp(fn, rd, wr):
+        return add("g", fn, regs(*rd), regs(*wr), ("g", wr[0][4]))
 
-    def M128(name):
+    def M(name):
         return V(name, 0, 128)
-
-    for k in range(4):
-        a, b = 1024 * k, 1024 * (k + 1)
-        add("s" if k % 2 else "s2", (lambda a=a, b=b, k=k: (g.sync if k % 2 else g.scalar).dma_start(T.X[:, a:b], T.xt[:, a:b])), [], [R("X", a, b)], 1500.0, "x%d" % k, 16)
-    for j in range(NCH):
-        o, n = OFF[j], CH[j]
-        add("s", (lambda o=o, n=n: g.sync.dma_start(T.li[:, 2 * o:2 * o + n], T.ba[:, o:o + n])), [], [R("li", 2 * o, 2 * o + n)], 1500.0, "la%d" % j, 16)
-        add("s", (lambda o=o, n=n: g.sync.dma_start(T.li[:, 2 * o + n:2 * o + 2 * n], T.bb[:, o:o + n])), [], [R("li", 2 * o + n, 2 * o + 2 * n)], 1500.0, "la%d" % j, 16)
-        add("s", (lambda o=o, n=n: g.sync.dma_start(T.mz0[:, 3 * o:3 * o + n], T.zp[:, o:o + n])), [], [R("mz0", 3 * o, 3 * o + n)], 1500.0, "la%d" % j, 16)
-    add("s", lambda: g.sync.dma_start(T.wcol[:], T.wl[:]), [], [R("wcol", 0, 1)], 1500.0, "lw", 16)
-    for k in ops:
-        if k["sem"] is not None and k["sem"].startswith("la"):
-            k["need"] = 48
-
-    fill(V("ones", 0, 144), 1.0)
-    gp(lambda: g.iota(T.bi[:, 0:16], [[0, 16]], 0, 16), [], [V("bi", 0, 16)], 200.0)
-    gp(lambda: g.iota(T.bi[:, 16:32], [[256, 16]], 0, 0), [], [V("bi", 16, 32)], 200.0)
-    W9 = V("ones", 0, 144)
-    gp(lambda: g.affine_select(T.tmpw[:], T.ones[:], [[-16, 9], [0, 16]], ALU.is_ge, 0.0, 0, 1), [W9], [V("tmpw", 0, 144)], 450.0)
-    gp(lambda: g.affine_select(T.tmpw2[:], T.tmpw[:], [[16, 9], [0, 16]], ALU.is_ge, 0.0, 15, -1), [V("tmpw", 0, 144)], [V("tmpw2", 0, 144)], 450.0)
-    cp(M128("GBb"), V("tmpw2", 0, 128))
-    gp(lambda: g.affine_select(T.Ib[:], T.GBb[:], [[1, 128]], ALU.is_equal, 0.0, 0, -1), [M128("GBb")], [M128("Ib")], 450.0)
-    gp(lambda: g.affine_select(T.Eb[:], T.tmpw2[:], [[0, 9], [1, 16]], ALU.is_equal, 0.0, -15, 0), [V("tmpw2", 0, 144)], [V("Eb", 0, 144)], 450.0)
-    gp(lambda: g.affine_select(T.Tr1[:], T.GBb[:], [[1, 128]], ALU.is_ge, 0.0, -1, -1), [M128("GBb")], [M128("Tr1")], 450.0)
-    for nm, c in (("H1", 1.0), ("Hn", -1.0), ("H2080", 2080.0), ("H3232", 3232.0), ("H32", 32.0), ("F32", 32.0), ("F32n", -32.0), ("H2048", 2048.0), ("Ibn", -1.0), ("Ib128", 128.0), ("Ibh", 0.5), ("H256", 256.0), ("F1", 1.0)):
-        ts(M128(nm), M128("Ib"), c, ALU.mult)
-    ts(M128("TrS"), M128("Tr1"), 0.21875, ALU.mult)
-    cp(V("on16", 0, NM), V("ones", 0, NM))
-    ts(V("m96", 0, NM), V("ones", 0, NM), -96.0, ALU.mult)
-    fill(V("RST", 0, 16 * NM), 1.0)
-    add("v", lambda: g.vector.memset(T.RST[:, 0:16 * NM:16], 0.0), [], [R("RST", 0, 16 * NM)], cv(NM))
-    for p in range(2):
-        act(V("zs%d" % p, 0, 16 * NM), V("RST", 0, 16 * NM), ACT.Copy, scale=0.0)
-    ts(V("Ew", 0, 144), V("Eb", 0, 144), V("wcol", 0, 1), ALU.mult)
-    ts(V("E2", 0, 144), V("Eb", 0, 144), 2.0, ALU.mult)
-    ts(V("En", 0, 144), V("Eb", 0, 144), -1.0, ALU.mult)
-    fill(M128("FK"), -0.5)
-    ts(M128("Wb"), M128("GBb"), V("wcol", 0, 1), ALU.mult)
-    ts(V("bi", 0, 16), V("bi", 0, 16), 255, ALU.bitwise_and)
-    tt(V("base", 0, 16), V("bi", 0, 16), V("bi", 16, 32), ALU.add)
 
     def E(b, nm="Eb"):
         return V(nm, 15 - b, 15 - b + 128)
 
-    nxt, prv = T.cores[(rank + 1) % len(T.cores)], T.cores[(rank - 1) % len(T.cores)]
+    def load(q, dst, src, sem, w="dma"):
+        add(q, lambda: (g.sync if q == "s" else g.scalar).dma_start(ap(dst), src), [], regs(dst), (w, 0), sem, 16)
+
+    for a, b in ((0, CH[0]), (CH[0], 256)):
+        w = "late" if a else "dma"
+        load("s", V("li", a, b), T.ba[:, a:b], "la%d" % min(a, 1), w)
+        load("s2" if a == 0 else "s", V("li", 256 + a, 256 + b), T.bb[:, a:b], "lb%d" % min(a, 1), w)
+        load("s", V("mz0", a, b), T.zp[:, a:b], "lz%d" % min(a, 1), w)
+        if a == 0:
+            load("s2", V("X", 0, 4096), T.xt[:], "lx", "big")
+    load("s", V("wcol", 0, 1), T.wl[:], "lw", "late")
+    for k in range(len(ops)):
+        ops[k]["first"] = 1e9 - 1e6 * k
+
+    fill(V("ones", 0, 144), 1.0)
+    gp(lambda: g.iota(T.bi[:, 0:16], [[0, 16]], 0, 16), [], [V("bi", 0, 16)])
+    gp(lambda: g.iota(T.bi[:, 16:32], [[256, 16]], 0, 0), [], [V("bi", 16, 32)])
+    gp(lambda: g.affine_select(T.tmpw[:], T.ones[:], [[-16, 9], [0, 16]], ALU.is_ge, 0.0, 0, 1), [V("ones", 0, 144)], [V("tmpw", 0, 144)])
+    gp(lambda: g.affine_select(T.tmpw2[:], T.tmpw[:], [[16, 9], [0, 16]], ALU.is_ge, 0.0, 15, -1), [V("tmpw", 0, 144)], [V("tmpw2", 0, 144)])
+    cp(M("GBb"), V("tmpw2", 0, 128))
+    gp(lambda: g.affine_select(T.Ib[:], T.GBb[:], [[1, 128]], ALU.is_equal, 0.0, 0, -1), [M("GBb")], [M("Ib")])
+    gp(lambda: g.affine_select(T.Eb[:], T.tmpw2[:], [[0, 9], [1, 16]], ALU.is_equal, 0.0, -15, 0), [V("tmpw2", 0, 144)], [V("Eb", 0, 144)])
+    gp(lambda: g.affine_select(T.Tr1[:], T.GBb[:], [[1, 128]], ALU.is_ge, 0.0, -1, -1), [M("GBb")], [M("Tr1")])
+    modes = "".join(CFG["mode"])
+    scaled = [("H1", 1.0), ("Hn", -1.0), ("H2080", 2080.0), ("H3232", 3232.0), ("H2048", 2048.0), ("Ibn", -1.0), ("H32", 32.0),
+              ("F32", 32.0), ("F32n", -32.0), ("Ib128", 128.0), ("Ib256", 256.0), ("H256", 256.0), ("F1", 1.0)]
+    scaled += [("IbBn", -BIG), ("HBn", -BIG)]
+    scaled += [("Ibh", 0.5), ("Hh", 0.5), ("Fh", 0.5), ("IbHn", -BIG / 2)] if CFG["gj"] == "a" else []
+    scaled += [("Ib4096n", -4096.0), ("Ib144", 144 * 4096.0)] if CFG["uq"] == "a" else []
+    for nm, c in scaled:
+        ts(M(nm), M("Ib"), c, ALU.mult)
+    ts(V("bi", 0, 16), V("bi", 0, 16), 255, ALU.bitwise_and)
+    if CFG["par"] == "a":
+        gp(lambda: g.affine_select(T.Tr2[:], T.GBb[:], [[1, 128]], ALU.is_ge, 0.0, 0, -1), [M("GBb")], [M("Tr2")])
+        gp(lambda: g.affine_select(T.tmpw[:, 0:128], T.GBb[:], [[1, 128]], ALU.is_equal, 0.0, -1, -1), [M("GBb")], [M("tmpw")])
+        ts(V("kcol", 0, 1), V("bi", 0, 1), 0.0, ALU.is_gt)
+        ts(M("Dm"), M("Ib"), V("kcol", 0, 1), ALU.mult)
+        tt(M("Dm"), M("Dm"), M("tmpw"), ALU.subtract)
+        ts(M("Dm"), M("Dm"), 0.5, ALU.mult)
+    ts(M("TrS"), M("Tr1"), 0.21875, ALU.mult)
+    cp(V("on16", 0, NM), V("ones", 0, NM))
+    ts(V("m96", 0, NM), V("ones", 0, NM), -96.0, ALU.mult)
+    fill(V("RST", 0, 16 * NM), 1.0)
+    fill(V("RST", 0, 16 * NM, 16), 0.0)
+    for p in range(2):
+        act(V("zs%d" % p, 0, 16 * NM), V("RST", 0, 16 * NM), ACT.Copy, scale=0.0)
+    ts(V("Ew", 0, 144), V("Eb", 0, 144), V("wcol", 0, 1), ALU.mult)
+    if "S" in modes:
+        ts(V("E2n", 0, 144), V("Eb", 0, 144), -2.0, ALU.mult)
+        tt(M("GB15"), M("GBb"), E(15), ALU.subtract)
+    if any(m[0] != "P" for m in CFG["mode"]):
+        ts(M("Ib16n"), M("Ib"), -16.0, ALU.mult)
+    if "R" in modes:
+        ts(V("E2", 0, 144), V("Eb", 0, 144), 2.0, ALU.mult)
+        ts(V("En", 0, 144), V("Eb", 0, 144), -1.0, ALU.mult)
+    fill(M("FK"), -0.5)
+    ts(M("Wb"), M("GBb"), V("wcol", 0, 1), ALU.mult)
+    tt(V("base", 0, 16), V("bi", 0, 16), V("bi", 16, 32), ALU.add)
+
+    nxt = T.cores[(rank + 1) % len(T.cores)]
     sends = {}
+    turn = [0]
     X = V("X", 0, 4096)
+    I1, In, F1, H1, Hn, GB = M("Ib"), M("Ibn"), M("F1"), M("H1"), M("Hn"), M("GBb")
 
     def names(t, j):
         q = t * NCH + j
         p, o, n = q % NB, OFF[j], CH[j]
-        e = 16 * n
-        D = {"q": q, "p": p, "o": o, "n": n, "e": e}
-        for nm in ("zr", "h", "do", "dc", "ah", "ao", "ac", "ch", "rm"):
-            D[nm] = V("%s%d" % (nm, p), 0, e)
+        D = {"q": q, "p": p, "o": o, "n": n}
+        for nm in ("zr", "xc", "xo", "xh", "mc", "mo", "mh"):
+            D[nm] = V("%s%d" % (nm, p), 0, 16 * n)
+        D["ch"] = V("ch%d" % p, 0, 16 * n)
+        D["M"] = V("rm", 16 * o + 15, 16 * (o + n), 16)
 
-        def slot(base, k, w=None):
-            return V("%s%d" % (base, p), k * NM, k * NM + (w or n))
-        for k, nm in enumerate(("dhs", "m1", "t1", "De", "jd", "sOm", "sO", "chf")):
-            D[nm] = slot("f", k)
-        for k, nm in enumerate(("rec", "w0", "wa", "am", "sg", "J", "sp", "nIo", "Gno")):
-            D[nm] = slot("b", k)
+        def slot(base, k):
+            return V("%s%d" % (base, p), k * NM, k * NM + n)
+        for base, lst in (("f", ("dhs", "m1", "jd", "sOm", "sO", "m2", "HS", "CmS")), ("b", ("rec", "uq", "wa", "am", "sg", "J", "sp", "R", "eo", "ec")),
+                          ("i", ("pm", "r", "p2")), ("u", ("Cu", "chu"))):
+            for k, nm in enumerate(lst):
+                D[nm] = slot(base, k)
         D["HO"] = V("s%d" % p, 0, 2 * n)
         D["Hc"], D["Oc"] = V("s%d" % p, 0, n), V("s%d" % p, n, 2 * n)
-        D["stl"], D["Cc"] = slot("s", 2), slot("s", 3)
-        D["pm"], D["r"], D["p2"] = slot("i", 0), slot("i", 1), slot("i", 2)
-        D["Cu"], D["chu"] = slot("u", 0), slot("u", 1)
+        D["stl"], D["x1"], D["chc"] = slot("s", 2), slot("s", 3), slot("s", 4)
         lu, mz = "lu%d" % t, "mz%d" % t
         D["LU"] = V(lu, 2 * o, 2 * o + 2 * n)
         D["Hu"], D["Ou"] = V(lu, 2 * o, 2 * o + n), V(lu, 2 * o + n, 2 * o + 2 * n)
-        D["z"], D["nI"], D["G"] = [V(mz, 3 * o + k * n, 3 * o + (k + 1) * n) for k in range(3)]
+        for k, nm in enumerate(("z", "G", "nI") if t == 1 else ("z", "nI", "G")):
+            D[nm] = V(mz, 3 * o + k * n, 3 * o + (k + 1) * n)
+        if t == 0:
+            D["z"] = V(mz, o, o + n)
         if t < READS - 1:
             su, sz = "su%d" % t, "sz%d" % t
             D["Hs"], D["Os"] = V(su, 2 * o + n, 2 * o + 2 * n), V(su, 2 * o, 2 * o + n)
-            D["zn"], D["nIn"], D["Gn"] = [V(sz, 3 * o + k * n, 3 * o + (k + 1) * n) for k in range(3)]
-            if t == 0:
-                D["J"] = D["nIn"]
-        else:
-            D["nIn"] = D["nIo"]
-            D["Gn"] = D["Gno"]
+            for k, nm in enumerate(("zn", "nIn", "Gn", "J") if t else ("zn", "Gn", "J")):
+                D[nm] = V(sz, 4 * o + k * n, 4 * o + (k + 1) * n)
+            D["GJ"] = V(sz, D["Gn"][1], D["J"][2])
 
-        def ps(bk, k):
-            return V("p%d" % bk, k * n, k * n + n)
-        lb, db = 4 + q % 3, 2 + q % 2
-        for nm, k in (("OmH", 0), ("CmH", 1), ("Op", 2), ("HS", 2), ("S", 3), ("Y", 3), ("bp", 3), ("Hr", 4)):
-            D[nm] = ps(lb, k)
-        for nm, k in (("dh", 0), ("ddo", 1), ("ddc", 2), ("RG", 3), ("pf", 4), ("cp", 1), ("up", 2), ("zM", 3)):
-            D[nm] = ps(db, k)
-        D["UL"] = V("p%d" % db, 480, 480 + n // 16)
-        for nm, k in (("Vp", 0), ("X1", 1), ("X2", 2), ("sc", 3), ("H2", 3), ("S2", 4)):
-            D[nm] = ps(7, k)
+        def ps(bk, k, w=1):
+            return V("p%d" % bk, k * n, (k + w) * n)
+        bank = {k: v[q % len(v)] for k, v in BANK.items()}
+        for bk, lst in (("L", (("OmH", 0), ("CmH", 1), ("Op", 2), ("S", 3), ("Hr", 4), ("t1", 3), ("cp", 4), ("De", 2), ("um", 3),
+                               ("Yw", 2), ("bp", 3), ("S2", 4))),
+                        ("C", (("dh", 0), ("do", 1), ("dc", 2), ("pf", 4), ("Vp", 0), ("zM", 1), ("sc", 2), ("Y", 0), ("bi", 1),
+                               ("H2", 2), ("up", 2), ("HSp", 3))),
+                        ("C" if CFG["gj"] == "a" else "L", (("X2", 3), ("X1", 4)))):
+            for nm, k in lst:
+                D[nm] = ps(bank[bk], k)
+        if CFG["uq"] == "v":
+            D["HS"] = D["HSp"]
+        D["X21"] = ps(bank["L"], 3, 2)
+        D["UB"] = "p%d" % bank["L"]
         return D
-
-    I1, In, F1 = M128("Ib"), M128("Ibn"), M128("F1")
-    H1, Hn = M128("H1"), M128("Hn")
 
     def cut(n, w):
         m = max(1, (n + w - 1) // w)
         s = [2 * (n // 2 * i // m) for i in range(m + 1)]
         return list(zip(s[:-1], s[1:]))
 
-    def sub(v, a, b, k=1):
-        return V(v[0], v[1] + k * a, v[1] + k * b)
-
     def pre(t, j):
         phase("pre", j)
         D = names(t, j)
-        n = D["n"]
+        n, o = D["n"], D["o"]
         if t == 0:
-            li = V("li", 2 * D["o"], 2 * D["o"] + 2 * n)
-            cp(D["LU"], li)
-            ts(D["HO"], li, -2048.0, ALU.add)
+            cp(D["Hu"], V("li", o, o + n))
+            cp(D["Ou"], V("li", 256 + o, 256 + o + n))
         else:
-            for nm, v in (("rl", D["LU"]), ("rz", V(D["z"][0], 3 * D["o"], 3 * D["o"] + 3 * n))):
-                k = add("n", None, [], regs(v), ("net", 0), "%s%d_%d" % (nm, t, j), NENG, after=[sends[(nm, t - 1, j)]])
-                ops[k]["soft"] = True
-            ts(D["HO"], D["LU"], -2048.0, ALU.add)
+            for nm, v in (("rl", D["LU"]), ("rz", V(D["z"][0], 3 * o, 3 * o + 3 * n))):
+                add("n", None, [], regs(v), ("net", 0), "%s%d_%d" % (nm, t, j), NENG, after=[sends[(nm, t - 1, j)]])
+        ts(D["HO"], D["LU"], -2048.0, ALU.add)
         on = V("on16", 0, n)
-        mm([(D["Op"], [(H1, D["Oc"])]), (D["S"], [(M128("H2080"), D["Hc"]), (M128("H3232"), D["Oc"])]),
-            (D["OmH"], [(H1, D["Oc"]), (Hn, D["Hc"])]), (D["Hr"], [(H1, D["Hc"]), (M128("H2048"), on)])])
+        mm([(D["Op"], [(H1, D["Oc"])]), (D["S"], [(M("H2080"), D["Hc"]), (M("H3232"), D["Oc"])]),
+            (D["OmH"], [(H1, D["Oc"]), (Hn, D["Hc"])]), (D["Hr"], [(H1, D["Hc"]), (M("H2048"), on)])])
         tt(D["pm"], D["Hc"], D["Op"], ALU.mult)
         tt(D["pm"], D["pm"], D["S"], ALU.add)
         ts(D["pm"], D["pm"], 5, ALU.arith_shift_right, 4095, ALU.bitwise_and)
@@ -411,195 +578,287 @@ def rank_program(g, core, T, topo):
         ts(D["stl"], D["OmH"], 0.0, ALU.is_equal)
         tt(D["HS"], D["stl"], D["Hr"], ALU.mult)
         tt(D["CmH"], D["pm"], D["Hr"], ALU.subtract)
-        zs = "zs%d" % (D["q"] % 2)
-        add("v", lambda: g.vector.tensor_copy(T[zs][:, 0:D["e"]:16], ap(D["z"])), regs(D["z"]), [R(zs, 0, D["e"])], cv(n, 0.5))
-        for a in range(0, D["e"], 512):
-            scan(V(D["zr"][0], a, a + 512), V("RST", a, a + 512), V(zs, a, a + 512), ALU.mult, ALU.add)
+        if t and CFG["par"] == "a":
+            act(D["CmS"], D["CmH"], ACT.Copy)
+        phase("zr", j)
+        if CFG["zq"][t][j] == "v":
+            zs = "zs%d" % (D["q"] % 2)
+            cp(V(zs, 0, 16 * n, 16), D["z"]) if CFG["zsq"] == "v" else act(V(zs, 0, 16 * n, 16), D["z"], ACT.Copy)
+            for a, b in cut(n, CFG["piece"]):
+                scan(sub(D["zr"], a, b, 16), V("RST", 16 * a, 16 * b), V(zs, 16 * a, 16 * b), ALU.mult, ALU.add)
+        else:
+            for k in range(16):
+                v = V(D["zr"][0], k, 16 * n, 16)
+                gp(lambda v=v: g.affine_select(ap(v), ap(D["z"]), [[0, n]], ALU.is_ge, 0.0, 0, 0), [D["z"]], [v])
 
     def s1(t, j):
         D = names(t, j)
-        n, e = D["n"], D["e"]
+        n = D["n"]
         phase("s1", j)
-        for a, b in cut(n, PH):
-            act(sub(D["h"], a, b, 16), ind(X, sub(D["Hu"], a, b)), ACT.Copy)
-        for dst, lst in (("do", "Ou"), ("dc", "Cu")):
-            for a, b in cut(n, PD):
-                tt(sub(D[dst], a, b, 16), ind(X, sub(D[lst], a, b)), sub(D["zr"], a, b, 16), ALU.subtract)
-        for k in range(n // 32):
-            a, b = 512 * k, 512 * k + 512
-            bk = V("p%d" % (k % 2), 0, 512)
-            mm([(bk, [(I1, V(D["h"][0], a, b)), (In, V(D["zr"][0], a, b))])])
-            act(V(D["ah"][0], a, b), bk, ACT.Abs)
-        for src, dst in (("do", "ao"), ("dc", "ac")):
-            for a, b in cut(n, PD):
-                if src in RELU[j]:
-                    ts(sub(D[dst], a, b, 16), sub(D[src], a, b, 16), 0.0, ALU.max)
+        for nm in CFG["lists"]:
+            lst, mode = nm.upper() + "u", CFG["mode"][j]["hoc".find(nm)]
+            x, m = D["x" + nm], D["m" + nm]
+            for a, b in cut(n, CFG["piece" if mode in "PS" else "pv"]):
+                src = ind(X, sub(D[lst], a, b))
+                if mode in "PS":
+                    act(sub(x, a, b, 16), src, ACT.Copy)
                 else:
-                    act(sub(D[dst], a, b, 16), sub(D[src], a, b, 16), ACT.Abs)
-        for raw, src, dst in ((None, "ah", "dh"), ("do", "ao", "ddo"), ("dc", "ac", "ddc")):
-            if raw in RELU[j]:
-                mm([(D[dst], [(E(b, "En"), V(D[raw][0], b, e, 16)) for b in range(16)] +
-                     [(E(b, "E2"), V(D[src][0], b, e, 16)) for b in range(16)])])
-            else:
-                mm([(D[dst], [(E(b), V(D[src][0], b, e, 16)) for b in range(16)])])
+                    tt(sub(x, a, b, 16), src, sub(D["zr"], a, b, 16), ALU.subtract)
+            for a, b in cut(n, CFG["ps"][j]) if mode == "S" else ():
+                end = V(x[0], 16 * a + 15, 16 * b, 16)
+                bk = V("p%d" % BANK["P"][turn[0] % len(BANK["P"])], 0, b - a)
+                turn[0] += 1
+                mm([(bk, [(In, sub(D["z"], a, b)), (I1, end)])])
+                if CFG["nil"] == "v":
+                    fill(end, 0.0)
+                elif CFG["nil"] == "a":
+                    act(end, sub(D["z"], a, b), ACT.Copy, scale=0.0)
+                else:
+                    gp(lambda end=end, a=a, b=b: g.affine_select(ap(end), ap(sub(D["z"], a, b)), [[0, b - a]], ALU.is_gt, 0.0, 0, 0), [sub(D["z"], a, b)], [end])
+                act(sub(D["e" + nm], a, b), bk, ACT.Abs)
+                scan(sub(m, a, b, 16), sub(D["zr"], a, b, 16), sub(x, a, b, 16), ALU.max, ALU.min)
+            for a, b in cut(n, CFG["pabs"]):
+                if mode == "A":
+                    act(sub(m, a, b, 16), sub(x, a, b, 16), ACT.Abs)
+                elif mode == "R":
+                    ts(sub(m, a, b, 16), sub(x, a, b, 16), 0.0, ALU.max)
+            col = lambda buf, e: [(E(b, e), V(buf[0], b, 16 * n, 16)) for b in range(16)]
+            d = D["d" + nm]
+            if mode == "P":
+                for a in range(0, 16 * n, 512):
+                    b = min(a + 512, 16 * n)
+                    bk = V("p%d" % BANK["P"][turn[0] % len(BANK["P"])], 0, b - a)
+                    turn[0] += 1
+                    mm([(bk, [(In, sub(D["zr"], a, b)), (I1, sub(x, a, b))])])
+                    act(sub(m, a, b), bk, ACT.Abs)
+            terms = col(x, "En") + col(m, "E2") if mode == "R" else col(m, "Eb")
+            if mode == "S":
+                terms = [(M("GB15"), D["z"])] + col(x, "Eb")[:15] + [(E(15), D["e" + nm])] + col(m, "E2n")[:15]
+            for a, b in cut(len(terms), CFG["pt"]):
+                mm([(d, terms[a:b])], a == 0, b == len(terms))
+            if nm == "h":
+                act(D["dhs"], d, ACT.Copy) if CFG["dcq"] == "a" else cp(D["dhs"], d)
+                if CFG["fast"][j]:
+                    mm([(D["Yw"], barred(D, t, "n"))])
+                else:
+                    mm([(D["Yw"], barred(D, t, "n") + [(F1, D["dhs"])])], True, False)
+            if nm == CFG["lists"][1] and CFG["fast"][j]:
+                tt(D["m2"], D["dhs"], D["do"], ALU.min)
+                tt(D["m2"], D["m2"], D["Yw"], ALU.add)
+
+    def barred(D, t, s):
+        if t and CFG["gj"] == "a":
+            return [(M("HB" + s), D["stl"]), (M("IbH" + s), D["G"]), (M("IbH" + s), V("ones", 0, D["n"]))]
+        return [(M("HB" + s), D["stl"])] + ([(M("IbB" + s), D["G"])] if t else [])
 
     def choice(t, j):
         D = names(t, j)
-        n, e = D["n"], D["e"]
+        n = D["n"]
         phase("ch", j)
-        cp(D["dhs"], D["dh"]) if DHV else act(D["dhs"], D["dh"], ACT.Copy)
-        tt(D["m1"], D["dhs"], D["ddc"], ALU.min)
-        tt(D["rec"], D["m1"], D["ddo"], ALU.is_ge)
-        tt(D["w0"], D["dhs"], D["ddc"], ALU.is_gt)
-        hb = M128("Ibh")
-        mm([(D["RG"], [(H1, D["stl"])] + ([(hb, D["G"]), (hb, V("ones", 0, n))] if t else []) + [(I1, D["rec"])])])
+        if CFG["fast"][j]:
+            tt(D["wa"], D["m2"], D["dc"], ALU.is_gt)
+        tt(D["m1"], D["dhs"], D["dc"], ALU.min)
+        tt(D["rec"], D["m1"], D["do"], ALU.is_ge)
+        if not CFG["fast"][j]:
+            mm([(D["Yw"], [(M("IbBn"), D["rec"])])], False, True)
+            tt(D["wa"], D["m1"], D["Yw"], ALU.is_lt)
+        mm([(D["pf"], [(M("TrS"), D["wa"])])])
         tt(D["t1"], D["rec"], D["OmH"], ALU.mult)
-        tt(D["wa"], D["w0"], D["RG"], ALU.is_gt)
-        mm([(D["pf"], [(M128("TrS"), D["wa"])])])
+        tt(D["x1"], D["Hc"], D["t1"], ALU.add)
         tt(D["am"], D["wa"], D["pf"], ALU.is_gt)
         tt(D["cp"], D["am"], D["CmH"], ALU.mult)
-        tt(D["De"], D["t1"], D["cp"], ALU.add)
-        tt(D["chf"], D["De"], D["Hr"], ALU.add)
-        cp(D["chu"], D["chf"])
-        for a, b in cut(n, PC):
-            act(sub(D["ch"], a, b, 16), ind(X, sub(D["chu"], a, b)), ACT.Copy)
+        tt(D["chc"], D["x1"], D["cp"], ALU.add)
+        ts(D["chu"], D["chc"], 2048.0, ALU.add)
+        for (a, b), q in zip(cut(n, n // len(CFG["chq"][j])), CFG["chq"][j]):
+            src = ind(X, sub(D["chu"], a, b))
+            act(sub(D["ch"], a, b, 16), src, ACT.Copy) if q == "a" else cp(sub(D["ch"], a, b, 16), src)
+        terms = [(In, V(D["xh"][0], b, 16 * n, 16)) for b in range(16)] + [(I1, V(D["ch"][0], b, 16 * n, 16)) for b in range(16)]
+        for a, b in cut(32, CFG["pt"]):
+            mm([(D["Vp"], ([(M("Ib16n"), D["z"])] if a == 0 and CFG["mode"][j][0] != "P" else []) + terms[a:b])], a == 0, b == 32)
+        act(D["sg"], D["Vp"], ACT.Sign, bias=0.5)
+        mm([(D["De"], [(H1, D["chc"]), (Hn, D["Hc"])])])
+
+    def top(t, j):
+        D = names(t, j)
+        phase("top", j)
+        for a, b in cut(D["n"], D["n"] // len(CFG["chq"][j])):
+            scan(V("rm", 16 * (D["o"] + a), 16 * (D["o"] + b)), V("RST", 16 * a, 16 * b), sub(D["ch"], a, b, 16), ALU.mult, ALU.max)
 
     def upd(t, j):
         D = names(t, j)
-        n, e, o = D["n"], D["e"], D["o"]
         phase("up", j)
-        for a, b in cut(n, PC):
-            scan(sub(D["rm"], a, b, 16), V("RST", 16 * a, 16 * b), sub(D["ch"], a, b, 16), ALU.mult, ALU.max)
-        k = n // 16
-        c0 = o // 16
-        U0, U1 = V("ul", c0, c0 + k), V("ul", 16 + c0, 16 + c0 + k)
-        nl = V("nl", c0, c0 + k)
         if t < READS - 1:
-            mm([(D["UL"], [(E(r, "Ew"), V(D["rm"][0], 16 * r + 15, e, 256)) for r in range(16)])])
-            cp(U0, D["UL"])
-            ts(U1, U0, 15, ALU.bitwise_and)
-            tt(U1, U1, V("base", c0, c0 + k), ALU.add)
-            cp(nl, U1)
-            xv = V("xv", o, o + n)
-            tt(xv, ind(X, nl), V(D["rm"][0], 15, e, 16), ALU.add)
-            ts(xv, xv, 1, ALU.arith_shift_right)
-            mm([(D["zM"], [(I1, D["z"]), (In, V(D["rm"][0], 15, e, 16))])])
+            mm([(D["zM"], [(I1, D["z"]), (In, D["M"])])])
             act(D["zn"], D["zM"], ACT.Abs)
-        mm([(D["up"], [(M128("Wb"), V(D["rm"][0], 15, e, 16))])])
-        cp(D["p2"], D["up"])
-        ts(D["p2"], D["p2"], 4095, ALU.bitwise_and)
-        tt(D["p2"], D["p2"], D["HS"], ALU.mult)
+        mm([(D["up"], [(M("Wb"), D["M"])])])
+        if CFG["uq"] == "a":
+            act(D["uq"], D["up"], ACT.Identity, bias=143.5 + 2.0 ** -13, scale=2.0 ** -12)
+            mm([(D["um"], [(M("Wb"), D["M"]), (M("Ib144"), V("ones", 0, D["n"])), (M("Ib4096n"), D["uq"])])])
+            tt(D["p2"], D["HS"], D["um"], ALU.mult)
+        else:
+            cp(D["p2"], D["up"])
+            ts(D["p2"], D["p2"], 4095, ALU.bitwise_and)
+            tt(D["p2"], D["p2"], D["HS"], ALU.mult)
 
-    def scat(t, o, n):
+    def table(bank, o, n):
+        phase("tb", o)
+        k, c0 = n // 16, o // 16
+        U0, U1, nl = V("ul", c0, c0 + k), V("ul", 16 + c0, 16 + c0 + k), V("nl", c0, c0 + k)
+        UL = V(bank, 480, 480 + k)
+        mm([(UL, [(E(r, "Ew"), V("rm", 16 * (o + r) + 15, 16 * (o + n), 256)) for r in range(16)])])
+        cp(U0, UL)
+        ts(U1, U0, 15, ALU.bitwise_and)
+        tt(U1, U1, V("base", c0, c0 + k), ALU.add)
+        cp(nl, U1)
+        xv = V("xv", o, o + n)
+        tt(xv, ind(X, nl), V("rm", 16 * o + 15, 16 * (o + n), 16), ALU.add)
+        ts(xv, xv, 1, ALU.arith_shift_right)
+
+    def scat(o, n):
         phase("sc", o)
         cp(ind(X, V("nl", o // 16, (o + n) // 16)), V("xv", o, o + n))
 
     def vote(t, j):
         D = names(t, j)
-        n, e, o = D["n"], D["e"], D["o"]
+        n, o = D["n"], D["o"]
         phase("vo", j)
-        mm([(D["Vp"], [(In, V(D["h"][0], b, e, 16)) for b in range(16)])], (True, False))
-        mm([(D["Vp"], [(I1, V(D["ch"][0], b, e, 16)) for b in range(16)])], (False, True))
-        act(D["sg"], D["Vp"], ACT.Sign, bias=0.5)
-        GB = M128("GBb")
-        gr = [(D["X1"], [(GB, D["sg"]), (M128("Ib128"), D["rec"]), (M128("Ib128"), D["am"]), (M128("H256"), D["stl"])]),
-              (D["X2"], [(GB, D["sg"]), (M128("Ib128"), D["am"])] + ([(M128("Ib128"), D["G"])] if t else []))]
-        if t < READS - 1:
-            gr.append((D["sc"], [(GB, D["sg"])]))
-        mm(gr)
-        ts(D["J"], D["X1"], 126.0, ALU.is_ge)
-        act(D["Gn"], D["X2"], ACT.Sign, bias=3.0 if t else -125.0)
-        if t < READS - 1:
+        sign = CFG["gj"] == "a"
+        more = t < READS - 1
+        x1 = (D["X1"], [(M("Ib128"), D["rec"]), (M("Ib128"), D["am"]), (M("H256"), D["stl"]), (GB, D["sg"])])
+        x2 = (D["X2"], [(M("Ib128"), D["am"])] + ([(M("Ib128" if sign else "Ib256"), D["G"])] if t else []) + [(GB, D["sg"])])
+        sc = (D["sc"], [(GB, D["sg"])])
+        if sign:
+            mm([x1, x2] + ([sc] if more else []))
+            act(D["J"], D["X1"], ACT.Sign, bias=-125.0)
+            if more:
+                act(D["Gn"], D["X2"], ACT.Sign, bias=3.0 if t else -125.0)
+        else:
+            mm([x1, x2])
+            if more:
+                mm([sc])
+                ts(D["GJ"], D["X21"], 126.0, ALU.is_ge)
+            else:
+                ts(D["J"], D["X1"], 126.0, ALU.is_ge)
+        if more:
             act(V("junk", 0, n), D["sc"], ACT.Sign, bias=3.0, acc=V("kacc", 8 * (t % 2) + j, 8 * (t % 2) + j + 1))
+        else:
+            ts(V("oyg", o, o + n), D["X2"], -2.5 if sign else 126.0, ALU.is_ge)
         tt(D["jd"], D["J"], D["De"], ALU.mult)
         if t:
-            mm([(D["Y"], [(I1, D["nI"]), (I1, D["J"])])])
-            act(D["sp"], D["Y"], ACT.Relu, bias=1.0, scale=-1.0)
-            act(D["nIn"], D["Y"], ACT.Square, bias=1.0, scale=-1.0)
-            mm([(D["bp"], [(M128("Tr1"), D["sp"])])])
-            tt(D["r"], D["sp"], D["bp"], ALU.mult)
-            ts(D["r"], D["r"], 1, ALU.bitwise_and)
-            tt(D["sO"], D["r"], D["CmH"], ALU.mult)
-            tt(D["sOm"], D["sp"], D["OmH"], ALU.mult)
+            one = 1.0 - (0.0 if not sign else 1.0 if t == 1 else 0.5)
+            mm([(D["Y"], [(M("Ibh") if sign and t == 1 else I1, D["nI"]), (M("Ibh") if sign else I1, D["J"])])])
+            act(D["sp"], D["Y"], ACT.Relu, bias=one, scale=-1.0)
+            if more:
+                act(D["nIn"], D["Y"], ACT.Square, bias=one, scale=-1.0)
+            else:
+                ts(V("oyi", o, o + n), D["Y"], one, ALU.is_equal)
+            if CFG["par"] == "a":
+                mm([(D["bi"], [(M("Tr2"), D["sp"])])])
+                act(D["R"], D["bi"], ACT.Identity, bias=271.5)
+                tt(D["sOm"], D["sp"], D["OmH"], ALU.mult)
+                mm([(D["bp"], [(M("Dm"), D["R"])])])
+                tt(D["sO"], D["CmS"], D["bp"], ALU.mult)
+            else:
+                mm([(D["bp"], [(M("Tr1"), D["sp"])])])
+                tt(D["r"], D["sp"], D["bp"], ALU.mult)
+                ts(D["r"], D["r"], 1, ALU.bitwise_and)
+                tt(D["sO"], D["r"], D["CmH"], ALU.mult)
+                tt(D["sOm"], D["sp"], D["OmH"], ALU.mult)
 
     def post(t, j):
         D = names(t, j)
-        n, e, o = D["n"], D["e"], D["o"]
-        k, c0 = n // 16, o // 16
+        n, o = D["n"], D["o"]
         phase("po", j)
-        on = V("on16", 0, n)
-        L = [(H1, D["Hc"]), (F1, D["jd"])]
-        L2 = [(M128("H32"), D["Oc"]), (M128("H2048"), V("m96", 0, n))]
-        if t:
-            L += [(F1, D["sO"])]
-            L2 += [(M128("HK"), D["stl"]), (M128("HK"), D["stl"]), (M128("F32"), D["sO"]), (M128("F32n"), D["sOm"])]
-        mm([(D["H2"], L), (D["S2"], L2)])
-        if t < READS - 1:
-            ts(D["Hs"], D["H2"], 2048.0, ALU.add)
+        if CFG["gj"] == "a":
+            L = [(M("Hh"), D["Hc"]), (M("Hh"), D["chc"]), (M("Fh"), D["jd"])]
         else:
-            ts(V("oyb", o, o + n), D["H2"], 2048.0, ALU.add)
+            L = [(H1, D["Hc"]), (F1, D["jd"])]
+        L2 = [(M("H32"), D["Oc"]), (M("H2048"), V("m96", 0, n))]
+        if t:
+            mm([(D["H2"], L)], True, False)
+            mm([(D["S2"], L2 + [(M("HK"), D["stl"]), (M("HK"), D["stl"]), (M("F32n"), D["sOm"])])], True, False)
+            mm([(D["S2"], [(M("F32"), D["sO"])])], False, True)
+            mm([(D["H2"], [(F1, D["sO"])])], False, True)
+        else:
+            mm([(D["S2"], L2)])
+            mm([(D["H2"], L)])
         tt(D["p2"], D["p2"], D["S2"], ALU.add)
+        ts(D["Hs"] if t < READS - 1 else V("oyb", o, o + n), D["H2"], 2048.0, ALU.add)
         ts(D["p2"], D["p2"], 5, ALU.arith_shift_right, 4095, ALU.bitwise_and)
         if t < READS - 1:
             cp(D["Os"], D["p2"])
-            su, sz = "su%d" % t, "sz%d" % t
             rid, pid = topo.addr(nxt, core)
             mask = sum(1 << x for x in topo.engines(core, nxt)[:NENG])
-            lu, mz = "lu%d" % (t + 1), "mz%d" % (t + 1)
-
-            def snd(src, dst, a, b, sem):
-                return lambda: g.remote_dma(T[dst][:, a:b], T[src][:, a:b], T.sem[sem], T.sem.left, pid, rid, mask)
-            sends[("rz", t, j)] = add("g", snd(sz, mz, 3 * o, 3 * o + 3 * n, "rz%d_%d" % (t + 1, j)), [R(sz, 3 * o, 3 * o + 3 * n)], [], 300.0, "left", NENG)
-            sends[("rl", t, j)] = add("g", snd(su, lu, 2 * o, 2 * o + 2 * n, "rl%d_%d" % (t + 1, j)), [R(su, 2 * o, 2 * o + 2 * n)], [], 300.0, "left", NENG)
+            for nm, src, dst in (("rz", V("sz%d" % t, 4 * o, 4 * o + 3 * n), V("mz%d" % (t + 1), 3 * o, 3 * o + 3 * n)),
+                                 ("rl", V("su%d" % t, 2 * o, 2 * o + 2 * n), V("lu%d" % (t + 1), 2 * o, 2 * o + 2 * n))):
+                fn = lambda nm=nm, src=src, dst=dst: g.remote_dma(ap(dst), ap(src), T.sem["%s%d_%d" % (nm, t + 1, j)], T.sem.left, pid, rid, mask)
+                sends[(nm, t, j)] = add("g", fn, regs(src), [], ("iss" if sends else "iss1", 0), "left", NENG)
         else:
             cp(V("oya", o, o + n), D["p2"])
-            act(V("oyi", o, o + n), D["nIn"], ACT.Identity, bias=1.0, scale=-1.0)
-            act(V("oyg", o, o + n), D["Gn"], ACT.Identity, bias=0.5, scale=0.5)
-            for m, (src, dst) in enumerate((("oya", "ya"), ("oyb", "yb"), ("oyi", "yi"), ("oyg", "yg"))):
-                add("s", (lambda src=src, dst=dst: g.sync.dma_start(T[dst][:, o:o + n], T[src][:, o:o + n])), [R(src, o, o + n)], [], 200.0, "out%d" % (4 * j + m), 16)
+            for m, nm in enumerate(("yg", "yi", "yb", "ya")):
+                fn = lambda nm=nm: g.sync.dma_start(T[nm][:, o:o + n], T["o" + nm][:, o:o + n])
+                add("s", fn, regs(V("o" + nm, o, o + n)), [], ("dma", 0), "out%d" % (4 * j + m), 16)
 
     def kcalc(t):
         phase("kc", 0)
         b = 8 * (t % 2)
-        kb = "p%d" % (2 + (t * NCH + NCH - 1) % 2)
-        mm([(V(kb, 500, 501), [(M128("FK"), V("kacc", b + j, b + j + 1)) for j in range(NCH)])])
-        ts(V("kcol", 0, 1), V(kb, 500, 501), 16384.0, ALU.add)
-        ts(M128("HK"), M128("H1"), V("kcol", 0, 1), ALU.mult)
+        kb = V(names(t, NCH - 1)["UB"], 500, 501)
+        mm([(kb, [(M("FK"), V("kacc", b + j, b + j + 1)) for j in range(NCH)])])
+        ts(V("kcol", 0, 1), kb, 16384.0, ALU.add)
+        ts(M("HK"), H1, V("kcol", 0, 1), ALU.mult)
 
     pre(0, 0)
     for t in range(READS):
+        more = t < READS - 1
+        cur[2] = t
         for j in range(NCH):
-            if t == 0 and j + 1 < NCH:
-                pre(0, j + 1)
+            if j:
+                pre(t, j)
             s1(t, j)
-            if t and j + 1 < NCH:
-                pre(t, j + 1)
+        for j in range(NCH):
+            last = j == NCH - 1
             choice(t, j)
-            if j == NCH - 1 and t < READS - 1 and NCH > 1:
-                scat(t, 0, OFF[j])
-            upd(t, j)
-            if j == NCH - 1:
-                if t < READS - 1:
-                    scat(t, OFF[j], CH[j])
+            top(t, j)
+            if more and j in CFG["tabs"]:
+                o = max([0] + [OFF[i] + CH[i] for i in CFG["tabs"] if i < j])
+                if last and o:
+                    scat(0, o)
+                table(names(t, j)["UB"], o, OFF[j] + CH[j] - o)
+                if last:
+                    scat(o, 256 - o)
                     pre(t + 1, 0)
+            upd(t, j)
             vote(t, j)
             post(t, j)
-        if t < READS - 1:
+        if more:
             kcalc(t)
 
-    order, fin = schedule(ops, EST, BONUS)
-    N = len(ops)
+    for early, late in CFG["rules"]:
+        seen = []
+        for k, o in enumerate(ops):
+            if (o["tag"].split(":")[0], o["w"][0]) == early:
+                seen.append(k)
+        for k, o in enumerate(ops):
+            if (o["tag"].split(":")[0], o["w"][0]) == late:
+                for d in seen:
+                    if o["t"] == ops[d]["t"]:
+                        o["deps"].setdefault(d, False)
 
-    eng = {"v": g.vector, "t": g.tensor, "a": g.scalar, "g": g, "s": g.sync, "s2": g.scalar}
+    if "it" not in ORDER:
+        ORDER["it"] = schedule(ops, EST, CFG["rounds"])
+        if CFG["tries"]:
+            ORDER["it"] = refine(ops, ORDER["it"][0], CFG["tries"], CFG["heat"])
+    order, fin = ORDER["it"]
+
+    eng = {"v": g.vector, "t": g.tensor, "a": g.scalar, "g": g, "s": g.sync}
     own = {"v": "qv", "t": "qt", "a": "qa", "g": "qg"}
-    phys = {"s2": "a"}
     total = {}
-    clk = {q: {} for q in ("v", "t", "a", "g", "s")}
-    val = [None] * N
-    opclk = [None] * N
+    clk = {q: {} for q in eng}
+    val = [None] * len(ops)
+    opclk = [None] * len(ops)
     for k in order:
         o = ops[k]
-        q = phys.get(o["q"], o["q"])
+        q = "a" if o["q"] == "s2" else o["q"]
         if q == "n":
             val[k] = (o["sem"], o["inc"])
             opclk[k] = {o["sem"]: o["inc"]}

@@ -1,104 +1,87 @@
 import math
 from concourse.mybir import dt, AluOpType as ALU, ActivationFunctionType as ACT
 
-NM = 96
-NB = 3
+n = 128
 READS = 4
 NENG = 8
-BIG = 16384.0
+EPS = 2.0 ** -12
 CFG = {
-    "ch": [96, 96, 64],
-    "mode": ["PAA", "PRA", "PAA"],
-    "chq": ["aa", "aa", "av"],
-    "fast": [False, False, True],
-    "zq": ["vvv", "vvg", "vvg", "vvg"],
-    "tabs": [1, 2],
-    "rules": [],
-    "ps": [96, 96, 32], "nil": "v", "lists": "hoc",
-    "piece": 48, "pv": 32, "pabs": 48, "pt": 8, "dcq": "a", "uq": "a", "par": "a", "gj": "a", "zsq": "a", "rounds": 0,
-    "tries": 120000, "heat": 0.0007, "seed": 1, "auto": 2, "far": 1,
+    "ph": [0, 32, 64, 96, 128],
+    "po": [0, 64, 128], "pc": [0, 64, 128], "pg": 32,
+    "pch": [(0, 32, "a"), (32, 64, "a"), (64, 96, "a"), (96, 128, "v")], "pm": [0, 64, 128],
+    "zg": [[0, 8], [10, 10], [10, 10], [10, 10]],
+    "a2": "a", "am": "p", "nil": "v", "pt": 8, "outq": "v",
+    "argD": False, "lead": 9000.0, "rounds": 6, "tries": 120000, "heat": 0.0007, "seed": 1, "auto": 2, "far": 1,
 }
-MAXCH = 4
-BANK = {"P": [0, 1], "C": [2, 3, 4], "L": [5, 6, 7]}
 
 SCRATCH = {
-    "X": ("sbuf", [128, 4096], "bfloat16"),
-    "li": ("sbuf", [128, 512], "int32"),
-    "wcol": ("sbuf", [128, 1], "bfloat16"),
-    "Eb": ("sbuf", [128, 144], "bfloat16"), "Ew": ("sbuf", [128, 144], "bfloat16"),
-    "E2": ("sbuf", [128, 144], "bfloat16"), "En": ("sbuf", [128, 144], "bfloat16"), "E2n": ("sbuf", [128, 144], "bfloat16"),
+    "wcol": ("sbuf", [128, 16], "bfloat16"),
+    "Eb": ("sbuf", [128, 144], "bfloat16"),
     "ones": ("sbuf", [128, 144], "bfloat16"), "tmpw": ("sbuf", [128, 144], "bfloat16"), "tmpw2": ("sbuf", [128, 144], "bfloat16"),
-    "m96": ("sbuf", [128, NM], "float16"), "on16": ("sbuf", [128, NM], "float16"),
-    "bi": ("sbuf", [128, 32], "int32"), "base": ("sbuf", [128, 16], "int32"),
-    "RST": ("sbuf", [128, 16 * NM], "bfloat16"),
-    "kacc": ("sbuf", [128, 16], "float32"), "kcol": ("sbuf", [128, 1], "float32"),
-    "junk": ("sbuf", [128, NM], "bfloat16"),
-    "rm": ("sbuf", [128, 4096], "bfloat16"),
-    "ul": ("sbuf", [128, 32], "int32"),
-    "nl": ("sbuf", [128, 32], "uint16"), "xv": ("sbuf", [128, 256], "int32"),
-    "oya": ("sbuf", [128, 256], "float32"), "oyb": ("sbuf", [128, 256], "float32"),
-    "oyi": ("sbuf", [128, 256], "float32"), "oyg": ("sbuf", [128, 256], "float32"),
+    "m96": ("sbuf", [128, n], "float16"), "on16": ("sbuf", [128, n], "float16"),
+    "bi": ("sbuf", [128, 64], "int32"), "base": ("sbuf", [128, 16], "bfloat16"),
+    "RST": ("sbuf", [128, 16 * 64], "bfloat16"), "CAP": ("sbuf", [128, 128], "bfloat16"),
+    "kacc": ("sbuf", [128, 8], "float32"), "kcol": ("sbuf", [128, 4], "float32"),
+    "RG": ("sbuf", [128, 144], "bfloat16"),
+    "ZR": ("sbuf", [128, 384], "bfloat16"), "CR": ("sbuf", [128, 384], "bfloat16"),
+    "XR": ("sbuf", [128, 384], "bfloat16"), "XA": ("sbuf", [128, 384], "bfloat16"),
 }
-for _n in ("GBb", "Ib", "Ibn", "Ibh", "Ib128", "Ib256", "IbB", "IbBn", "IbH", "IbHn", "Ib4096n", "Ib144", "TrS", "Tr1", "Tr2", "Dm", "Wb", "GB15", "Ib16n"):
+for _n in ("GBb", "Ib", "Ibn", "Ibh", "Swh", "Sw", "Ib2n", "Ib8", "Ib256", "Ib512", "Ib4096n", "Ib144", "Ib16n", "TrH", "Dp", "Dn"):
     SCRATCH[_n] = ("sbuf", [128, 128], "bfloat16")
-for _n in ("H1", "Hn", "Hh", "H2080", "H3232", "H32", "H2048", "H256", "HK", "HB", "HBn"):
+for _n in ("H1", "Hn", "Hh", "Hhn", "H2n", "H2080", "H3232", "H32", "H2048", "H256", "HK0", "HK1"):
     SCRATCH[_n] = ("sbuf", [128, 128], "float16")
-for _n in ("F1", "Fh", "F32", "F32n", "FK"):
+for _n in ("F1", "Fhn", "FK"):
     SCRATCH[_n] = ("sbuf", [128, 128], "float32")
 for _t in range(READS):
     SCRATCH["lu%d" % _t] = ("sbuf", [128, 512], "uint16")
     SCRATCH["mz%d" % _t] = ("sbuf", [128, 768], "bfloat16")
+    SCRATCH["sz%d" % _t] = ("sbuf", [128, 1024], "bfloat16")
     if _t < READS - 1:
         SCRATCH["su%d" % _t] = ("sbuf", [128, 512], "uint16")
-        SCRATCH["sz%d" % _t] = ("sbuf", [128, 1024], "bfloat16")
 for _p in range(2):
-    SCRATCH["zs%d" % _p] = ("sbuf", [128, 16 * NM], "bfloat16")
-for _p in range(NB):
-    for _n in ("zr", "xc", "xo", "xh", "mc", "mo", "mh"):
-        SCRATCH["%s%d" % (_n, _p)] = ("sbuf", [128, 16 * NM], "bfloat16")
-    SCRATCH["ch%d" % _p] = ("sbuf", [128, 16 * NM], "bfloat16")
-    SCRATCH["f%d" % _p] = ("sbuf", [128, 8 * NM], "float32")
-    SCRATCH["b%d" % _p] = ("sbuf", [128, 10 * NM], "bfloat16")
-    SCRATCH["s%d" % _p] = ("sbuf", [128, 5 * NM], "float16")
-    SCRATCH["i%d" % _p] = ("sbuf", [128, 3 * NM], "int32")
-    SCRATCH["u%d" % _p] = ("sbuf", [128, 2 * NM], "uint16")
+    SCRATCH["X%d" % _p] = ("sbuf", [128, 4096], "bfloat16")
+    SCRATCH["li%d" % _p] = ("sbuf", [128, 256], "int32")
+    SCRATCH["Ew%d" % _p] = ("sbuf", [128, 144], "bfloat16")
+    SCRATCH["Wb%d" % _p] = ("sbuf", [128, 128], "bfloat16")
+    for _n in ("zr", "xc", "xo", "xh", "mc", "mo", "mh", "ch", "rm"):
+        SCRATCH["%s%d" % (_n, _p)] = ("sbuf", [128, 16 * n], "bfloat16")
+    SCRATCH["f%d" % _p] = ("sbuf", [128, 8 * n], "float32")
+    SCRATCH["b%d" % _p] = ("sbuf", [128, 13 * n], "bfloat16")
+    SCRATCH["s%d" % _p] = ("sbuf", [128, 6 * n], "float16")
+    SCRATCH["i%d" % _p] = ("sbuf", [128, 5 * n], "int32")
+    SCRATCH["u%d" % _p] = ("sbuf", [128, 3 * n], "uint16")
+    SCRATCH["oy%d" % _p] = ("sbuf", [128, 4 * n], "float32")
 for _p in range(8):
     SCRATCH["p%d" % _p] = ("psum", [128, 512], "float32")
 
 SEMAPHORES = ["qv", "qt", "qa", "qg", "left"]
-SEMAPHORES += ["la0", "lb0", "lz0", "la1", "lb1", "lz1", "lx", "lw"]
-SEMAPHORES += ["rl%d_%d" % (t, j) for t in range(1, READS) for j in range(MAXCH)]
-SEMAPHORES += ["rz%d_%d" % (t, j) for t in range(1, READS) for j in range(MAXCH)]
-SEMAPHORES += ["out%d" % k for k in range(4 * MAXCH)]
+SEMAPHORES += ["l%s%d" % (k, s) for k in "abzxw" for s in range(2)]
+SEMAPHORES += ["r%s%d_%d" % (k, t, s) for k in "lzg" for t in range(1, READS) for s in range(2)]
+SEMAPHORES += ["out%d" % k for k in range(8)]
 
-EST = {"cy": 0.9, "gam": 1.56, "scat": 3.0, "pec": 0.46, "fv": 20.0, "fa": 20.0, "wake": 130.0, "net": 8000.0, "dma": 2000.0,
-       "big": 7500.0, "late": 9000.0, "iss": 600.0, "iss1": 4500.0}
-CASES = [{"cy": 0.9, "pec": 0.455, "fv": 15.0, "fa": 15.0, "wake": 140.0, "net": 5500.0},
-         {"cy": 0.95, "pec": 0.48, "gam": 1.15, "fv": 0.0, "fa": 0.0, "wake": 110.0, "net": 7000.0, "late": 11000.0, "dma": 3000.0},
-         {"cy": 1.1, "pec": 0.555, "gam": 2.0, "scat": 5.0, "fv": 15.0, "fa": 15.0, "wake": 170.0, "net": 6000.0, "big": 5500.0, "late": 6500.0}]
-BONUS = {}
-RANK = {"c": -50, "zr0": 97, "pre0": 97, "s10": 0, "s10vg": -3, "ch0": 1, "top0": 2, "up0": 4, "vo0": 3, "po0": 2, "pre1": -0.5, "zr1": -0.5,
-        "s11": 6, "s11a": 5, "s11t": 5.7, "pre2": 5, "zr2": -2, "s12": 12, "ch1": 11, "ch1ag": 13, "ch1t": 15, "ch2": 12.5, "ch2t": 13.5,
-        "top2": 12.6, "tb192": 12.7, "sc0": 12.7, "sc192": 12.7, "top1": 13.1, "tb0": 6.2, "up1": 20, "vo1": 17, "po1": 20, "up2": 99,
-        "vo2": 91.7, "po2": 99, "kc0": 99.5}
+EST = {"cy": 0.9, "gam": 1.56, "scat": 3.0, "pec": 0.46, "fv": 20.0, "fa": 20.0, "wake": 130.0, "net": 5500.0, "dma": 2000.0,
+       "big": 7500.0, "late": 9000.0, "big2": 12000.0, "iss": 600.0, "iss1": 4500.0}
+CASES = [{"cy": 0.9, "pec": 0.455, "fv": 15.0, "fa": 15.0, "wake": 140.0, "net": 5000.0},
+         {"cy": 0.95, "pec": 0.48, "gam": 1.15, "fv": 0.0, "fa": 0.0, "wake": 110.0, "net": 6500.0, "late": 11000.0, "dma": 3000.0},
+         {"cy": 1.1, "pec": 0.555, "gam": 2.0, "scat": 5.0, "fv": 15.0, "fa": 15.0, "wake": 170.0, "net": 5500.0, "big": 5500.0, "late": 6500.0, "big2": 9500.0}]
 ORDER = {}
 
 
 def price(w, E):
-    k, n = w
+    k, m = w
     cy = E["cy"]
     if k == "v":
-        return E["fv"] + cy * max(64.0, n)
+        return E["fv"] + cy * max(64.0, m)
     if k == "a":
-        return E["fa"] + cy * n
+        return E["fa"] + cy * m
     if k == "t":
-        return E["pec"] * n
+        return E["pec"] * m
     if k == "g":
-        return 170.0 + 2 * cy * n
+        return 170.0 + 2 * cy * m
     if k in ("vg", "ag"):
-        return (50.0 if k == "vg" else 65.0) + cy * E["gam"] * n
+        return (50.0 if k == "vg" else 65.0) + cy * E["gam"] * m
     if k == "vs":
-        return 50.0 + cy * E["scat"] * n
+        return 50.0 + cy * E["scat"] * m
     return E[k]
 
 
@@ -135,29 +118,28 @@ def place(qs, pred, cost, hold, W, pri):
     return order, fin
 
 
+def holds(ops, cost):
+    return [0.0 if o["q"] == "n" else 120.0 if o["dma"] else c for o, c in zip(ops, cost)]
+
+
 def schedule(ops, E, rounds):
     N = len(ops)
     W = E["wake"]
     qs = [o["q"] for o in ops]
     cost = [price(o["w"], E) for o in ops]
-    hold = [0.0 if qs[k] == "n" else 60.0 if qs[k] in ("s", "s2") else cost[k] for k in range(N)]
+    hold = holds(ops, cost)
     pred = [o["deps"] for o in ops]
     back = [{} for _ in range(N)]
     for k in range(N):
         for d, w in pred[k].items():
             back[d][k] = w
-    bonus = [BONUS.get(o["tag"], 0.0) + BONUS.get(o["tag"].split(":")[0], 0.0) + BONUS.get(o["uid"], 0.0) + o.get("first", 0.0) for o in ops]
     pri = [0.0] * N
     for k in range(N - 1, -1, -1):
         pri[k] = cost[k] + W + max([pri[s] for s in back[k]] + [0.0])
-    if RANK:
-        for k, o in enumerate(ops):
-            ph = o["tag"].split(":")[0]
-            pri[k] = -1e3 * (100 * o["t"] + RANK.get(ph + o["w"][0], RANK.get(ph, 0.0))) - k
-            bonus[k] = o.get("first", 0.0)
+    pri = [p + (0.0 if o["s"] else CFG["lead"]) for p, o in zip(pri, ops)]
     best = None
     for r in range(rounds + 1):
-        order, fin = place(qs, pred, cost, hold, W, [pri[k] + bonus[k] for k in range(N)])
+        order, fin = place(qs, pred, cost, hold, W, [pri[k] + ops[k].get("first", 0.0) for k in range(N)])
         if best is None or max(fin) < max(best[1]):
             best = (order, fin)
         if r < rounds:
@@ -167,7 +149,7 @@ def schedule(ops, E, rounds):
 
 def refine(ops, order, tries, heat):
     N = len(ops)
-    q = ["vatgsn".find(o["q"][0] if o["q"] != "s2" else "a") for o in ops]
+    q = ["vatgsn".find(o["q"]) for o in ops]
     above, deps = [0] * N, []
     for k in range(N):
         keep = []
@@ -180,8 +162,7 @@ def refine(ops, order, tries, heat):
     for c in CASES:
         E = dict(EST, **c)
         cost = [price(o["w"], E) for o in ops]
-        hold = [60.0 if o["q"] in ("s", "s2") else x for o, x in zip(ops, cost)]
-        cases.append((cost, hold, [[(d, E["wake"] if ops[k]["deps"][d] else 0.0) for d in deps[k]] for k in range(N)]))
+        cases.append((cost, holds(ops, cost), [[(d, E["wake"] if ops[k]["deps"][d] else 0.0) for d in deps[k]] for k in range(N)]))
 
     def times(order, first, case, old, guess=None):
         cost, hold, dw = case
@@ -245,14 +226,13 @@ def refine(ops, order, tries, heat):
 
     seed = [CFG["seed"]]
 
-    def draw(n):
+    def draw(m):
         seed[0] = (seed[0] * 6364136223846793005 + 1442695040888963407) % 2 ** 64
-        return (seed[0] >> 33) % n
+        return (seed[0] >> 33) % m
 
     fins = [times(order, 0, c, [0.0] * N) for c in cases]
     unit = [max(f) for f in fins]
-    now = 1.0
-    best = (now, order, fins[0])
+    best = (1.0, order, fins[0])
     done = 0
     while done < tries:
         i = draw(len(cases))
@@ -296,33 +276,34 @@ def refine(ops, order, tries, heat):
                     break
             if lost <= room:
                 order, fins = new, f2 if draw(100) else [times(new, 0, c, f) for c, f in zip(cases, fins)]
-                s = now = sum(max(f) / u for f, u in zip(fins, unit)) / len(unit)
+                s = sum(max(f) / u for f, u in zip(fins, unit)) / len(unit)
                 if s < best[0]:
                     best = (s, order, fins[0])
                 break
-    return best[1:]
+    order = best[1]
+    fins = [times(order, 0, c, [0.0] * N) for c in cases]
+    ORDER["ends"] = [max(f) for f in fins]
+    return order, fins[0]
 
 
 def rank_program(g, core, T, topo):
     rank = T.rank_of(core)
     if rank is None:
         return
-    CH = CFG["ch"]
-    NCH = len(CH)
-    OFF = [sum(CH[:j]) for j in range(NCH)]
     ops = []
     hist = {}
+    closer = {}
     cur = ["c", 0, 0]
 
-    def phase(name, j):
-        cur[0], cur[1] = "%s%d" % (name, j), 0
+    def phase(name):
+        cur[0] = name
 
     def meet(a, b):
         if a[0] >= b[1] or b[0] >= a[1]:
             return False
         return not (a[2] == b[2] > 1 and a[0] % a[2] != b[0] % a[2])
 
-    def add(q, fn, rd, wr, w, sem=None, inc=1, after=()):
+    def add(q, fn, rd, wr, w, sem=None, inc=1, after=(), free=None, dma=False):
         k = len(ops)
         deps = {}
         for isw, regs in ((False, rd), (True, wr)):
@@ -333,7 +314,8 @@ def rank_program(g, core, T, topo):
                     if bank and not same:
                         deps[d] = True
                     elif bank and q == "t":
-                        deps[d] = deps.get(d, False)
+                        if free is None or ops[d]["free"] != free:
+                            deps[d] = deps.get(d, False)
                     elif (isw or dw) and meet(r[1:], dr):
                         deps[d] = True
         for d in after:
@@ -343,18 +325,22 @@ def rank_program(g, core, T, topo):
                 lst = hist.setdefault(r[0], [])
                 if isw:
                     if SCRATCH[r[0]][0] == "psum":
-                        lst = lst[-30:]
+                        lst = lst[-40:]
                     else:
                         lst = [e for e in lst if not (r[1] <= e[1][0] and e[1][1] <= r[2] and (r[3] == 1 or r[1:] == e[1]))]
                     hist[r[0]] = lst
-                lst.append((k, r[1:], isw))
+                if not (q == "t" and isw and lst and lst[-1][0] == k):
+                    lst.append((k, r[1:], isw))
         deps.pop(k, None)
-        ops.append({"q": q, "fn": fn, "deps": deps, "w": w, "sem": sem, "inc": inc, "tag": "%s:%d" % (cur[0], cur[1]), "uid": k, "t": cur[2]})
-        cur[1] += 1
+        ops.append({"q": q, "fn": fn, "deps": deps, "w": w, "sem": sem, "inc": inc, "tag": cur[0], "t": cur[1], "s": cur[2],
+                    "free": free, "dma": dma, "out": wr[0] if wr else None})
         return k
 
     def V(name, a, b, step=1):
         return (name, a, b, step, (b - a + step - 1) // step, (slice(None), slice(a, b, step)), None)
+
+    def rows(v, a, b):
+        return v[:5] + ((slice(a, b), v[5][1]), None)
 
     def ap(v):
         if not isinstance(v, tuple):
@@ -376,7 +362,10 @@ def rank_program(g, core, T, topo):
         return r
 
     def sub(v, a, b, k=1):
-        return V(v[0], v[1] + k * a, v[1] + k * b)
+        return V(v[0], v[1] + k * a * v[3], v[1] + k * b * v[3] - v[3] + 1, v[3])
+
+    def col(v, b, a0=0, a1=n):
+        return V(v[0], 16 * a0 + b, 16 * a1, 16)
 
     def half(*vs):
         return 0.5 if all(SCRATCH[v[0]][2] in ("bfloat16", "uint16", "float16") for v in vs) else 1.0
@@ -402,7 +391,8 @@ def rank_program(g, core, T, topo):
         return add("v", fn, regs(in_), regs(out), ("vg", out[4]) if in_[6] is not None else ("v", out[4] * half(out, in_)))
 
     def scan(out, d0, d1, o0, o1):
-        return add("v", lambda: g.vector.tensor_tensor_scan(ap(out), ap(d0), ap(d1), 0.0, o0, o1), regs(d0, d1), regs(out), ("v", 0.5 * out[4]))
+        return add("v", lambda: g.vector.tensor_tensor_scan(ap(out), ap(d0), ap(d1), 0.0, o0, o1), regs(d0, d1), regs(out),
+                   ("v", half(out, d0, d1) * out[4]))
 
     def fill(out, c):
         return add("v", lambda: g.vector.memset(ap(out), c), [], regs(out), ("v", out[4] * half(out)))
@@ -410,23 +400,39 @@ def rank_program(g, core, T, topo):
     def act(out, in_, func, bias=0.0, scale=1.0, acc=None):
         def emit():
             if acc is not None:
-                return g.scalar.activation(ap(out), ap(in_), func, bias=bias, scale=scale, accum_out=ap(acc))
-            return g.scalar.activation(ap(out), ap(in_), func, bias=bias, scale=scale)
-        return add("a", emit, regs(in_), regs(out, acc), ("a" if in_[6] is None else "ag", out[4]))
+                return g.scalar.activation(ap(out), ap(in_), func, bias=ap(bias), scale=scale, accum_out=ap(acc))
+            return g.scalar.activation(ap(out), ap(in_), func, bias=ap(bias), scale=scale)
+        return add("a", emit, regs(in_, bias), regs(out, acc), ("a" if in_[6] is None else "ag", out[4]))
 
-    def mm(groups, first=True, final=True):
+    def mm(terms, first=True, final=True, free=None):
+        rd, wr, c = [], [], 0.0
+        for out, l, r in terms:
+            wr += regs(out)
+            rd += regs(l, r)
+            c += max(min(64, l[4]), r[4]) * (4 if SCRATCH[r[0]][2] == "float32" else 1)
+
+        me = len(ops)
+
+        def emit():
+            last, stop = None, final or closer.get(free) == me
+            for k, (out, l, r) in enumerate(terms):
+                last = g.tensor.matmul(ap(out), ap(l), ap(r), first and k == 0, stop and k == len(terms) - 1)
+            return last
+        return add("t", emit, sorted(set(rd)), sorted(set(wr)), ("t", c), free=free)
+
+    def mms(groups):
         rd, wr, c = [], [], 0.0
         for out, lst in groups:
             wr += regs(out)
             for l, r in lst:
                 rd += regs(l, r)
-                c += max(64, r[4]) * (4 if SCRATCH[r[0]][2] == "float32" else 1)
+                c += max(min(64, l[4]), r[4]) * (4 if SCRATCH[r[0]][2] == "float32" else 1)
 
         def emit():
             last = None
             for out, lst in groups:
                 for k, (l, r) in enumerate(lst):
-                    last = g.tensor.matmul(ap(out), ap(l), ap(r), first and k == 0, final and k == len(lst) - 1)
+                    last = g.tensor.matmul(ap(out), ap(l), ap(r), k == 0, k == len(lst) - 1)
             return last
         return add("t", emit, sorted(set(rd)), wr, ("t", c))
 
@@ -439,416 +445,313 @@ def rank_program(g, core, T, topo):
     def E(b, nm="Eb"):
         return V(nm, 15 - b, 15 - b + 128)
 
-    def load(q, dst, src, sem, w="dma"):
-        add(q, lambda: (g.sync if q == "s" else g.scalar).dma_start(ap(dst), src), [], regs(dst), (w, 0), sem, 16)
+    def dma2(q, pairs, rd, wr, sem, w):
+        fn = lambda: [(g.sync if q == "s" else g.scalar).dma_start(o, i) for o, i in pairs]
+        return add(q, fn, rd, wr, (w, 0), sem, 32, dma=True)
 
-    for a, b in ((0, CH[0]), (CH[0], 256)):
-        w = "late" if a else "dma"
-        load("s", V("li", a, b), T.ba[:, a:b], "la%d" % min(a, 1), w)
-        load("s2" if a == 0 else "s", V("li", 256 + a, 256 + b), T.bb[:, a:b], "lb%d" % min(a, 1), w)
-        load("s", V("mz0", a, b), T.zp[:, a:b], "lz%d" % min(a, 1), w)
-        if a == 0:
-            load("s2", V("X", 0, 4096), T.xt[:], "lx", "big")
-    load("s", V("wcol", 0, 1), T.wl[:], "lw", "late")
+    def load(q, dst, src, s, sem, w, split=True):
+        m = src.shape[1] // 2 if split else 0
+        dma2(q, [(ap(rows(dst, 64 * h, 64 * h + 64)), src[64 * s:64 * s + 64, m * h:m * h + dst[4]]) for h in range(2)], [], regs(dst), sem, w)
+
+    load("a", V("X0", 0, 4096), T.xt, 0, "lx0", "big", False)
+    for s in range(2):
+        w = "late" if s else "dma"
+        load("s", V("li%d" % s, 0, n), T.ba, s, "la%d" % s, w)
+        load("s", V("li%d" % s, n, 2 * n), T.bb, s, "lb%d" % s, w)
+        load("s", V("mz0", 384 * s, 384 * s + n), T.zp, s, "lz%d" % s, w)
+        load("s", V("wcol", 8 * s, 8 * s + 1), T.wl, s, "lw%d" % s, "late", False)
+        if s == 0:
+            load("s", V("X1", 0, 4096), T.xt, 1, "lx1", "big2", False)
     for k in range(len(ops)):
         ops[k]["first"] = 1e9 - 1e6 * k
 
     fill(V("ones", 0, 144), 1.0)
-    gp(lambda: g.iota(T.bi[:, 0:16], [[0, 16]], 0, 16), [], [V("bi", 0, 16)])
-    gp(lambda: g.iota(T.bi[:, 16:32], [[256, 16]], 0, 0), [], [V("bi", 16, 32)])
     gp(lambda: g.affine_select(T.tmpw[:], T.ones[:], [[-16, 9], [0, 16]], ALU.is_ge, 0.0, 0, 1), [V("ones", 0, 144)], [V("tmpw", 0, 144)])
     gp(lambda: g.affine_select(T.tmpw2[:], T.tmpw[:], [[16, 9], [0, 16]], ALU.is_ge, 0.0, 15, -1), [V("tmpw", 0, 144)], [V("tmpw2", 0, 144)])
+    gp(lambda: g.affine_select(T.Ib[:], T.ones[:, 0:128], [[1, 128]], ALU.is_equal, 0.0, 0, -1), [V("ones", 0, 144)], [M("Ib")])
     cp(M("GBb"), V("tmpw2", 0, 128))
-    gp(lambda: g.affine_select(T.Ib[:], T.GBb[:], [[1, 128]], ALU.is_equal, 0.0, 0, -1), [M("GBb")], [M("Ib")])
     gp(lambda: g.affine_select(T.Eb[:], T.tmpw2[:], [[0, 9], [1, 16]], ALU.is_equal, 0.0, -15, 0), [V("tmpw2", 0, 144)], [V("Eb", 0, 144)])
-    gp(lambda: g.affine_select(T.Tr1[:], T.GBb[:], [[1, 128]], ALU.is_ge, 0.0, -1, -1), [M("GBb")], [M("Tr1")])
-    modes = "".join(CFG["mode"])
-    scaled = [("H1", 1.0), ("Hn", -1.0), ("H2080", 2080.0), ("H3232", 3232.0), ("H2048", 2048.0), ("Ibn", -1.0), ("H32", 32.0),
-              ("F32", 32.0), ("F32n", -32.0), ("Ib128", 128.0), ("Ib256", 256.0), ("H256", 256.0), ("F1", 1.0)]
-    scaled += [("IbBn", -BIG), ("HBn", -BIG)]
-    scaled += [("Ibh", 0.5), ("Hh", 0.5), ("Fh", 0.5), ("IbHn", -BIG / 2)] if CFG["gj"] == "a" else []
-    scaled += [("Ib4096n", -4096.0), ("Ib144", 144 * 4096.0)] if CFG["uq"] == "a" else []
-    for nm, c in scaled:
-        ts(M(nm), M("Ib"), c, ALU.mult)
+    gp(lambda: g.iota(T.bi[:, 0:16], [[0, 16]], 0, 16), [], [V("bi", 0, 16)])
+    gp(lambda: g.iota(T.bi[:, 16:32], [[256, 16]], 0, 0), [], [V("bi", 16, 32)])
+    gp(lambda: g.iota(T.bi[:, 32:48], [[0, 16]], 0, 32), [], [V("bi", 32, 48)])
+    gp(lambda: g.affine_select(T.TrH[:], T.GBb[:], [[1, 128]], ALU.is_ge, 0.0, 0, -1), [M("GBb")], [M("TrH")])
+    gp(lambda: g.affine_select(T.tmpw[:, 0:128], T.GBb[:], [[1, 128]], ALU.is_equal, 0.0, -1, -1), [M("GBb")], [M("tmpw")])
+    I1, In, F1, H1, Hn, GB = M("Ib"), M("Ibn"), M("F1"), M("H1"), M("Hn"), M("GBb")
+    G8 = V("GBb", 0, 128, 16)
+
+    def scaled(out, in_, c):
+        if SCRATCH[out[0]][2] == "float16":
+            ts(out, in_, c, ALU.mult)
+        else:
+            act(out, in_, ACT.Copy, scale=c)
+
+    for nm, c in (("H1", 1.0), ("Hn", -1.0), ("H2080", 2080.0), ("H3232", 3232.0), ("H2048", 2048.0), ("Ibn", -1.0), ("H2n", -2.0),
+                  ("Ib2n", -2.0), ("Ib8", 8.0), ("F1", 1.0), ("Ib16n", -16.0), ("H32", 32.0), ("H256", 256.0), ("Ib256", 256.0),
+                  ("Ib512", 512.0), ("Ibh", 0.5), ("Hh", 0.5), ("Hhn", -0.5), ("Fhn", -0.5), ("Ib4096n", -4096.0), ("Ib144", 144 * 4096.0)):
+        scaled(M(nm), I1, c)
+    cp(V("on16", 0, n), V("ones", 0, n))
+    ts(V("m96", 0, n), V("ones", 0, n), -96.0, ALU.mult)
+    for k, c in enumerate((-EPS, 0.0, EPS, EPS, -1.0, 0.0, 0.0, 1.0, -EPS)):
+        scaled(V("RG", 8 * k, 8 * k + 8), G8, c)
+    scaled(V("RG", 72, 144), V("RG", 0, 72), -2.0)
+    tt(V("ZR", 128, 256), GB, E(15), ALU.subtract)
+    scaled(V("ZR", 0, 128), V("ZR", 128, 256), EPS)
+    scaled(V("ZR", 256, 384), V("ZR", 128, 256), -EPS)
+    fill(V("ZR", 128, 256), 0.0)
+    for k, c in enumerate((1.0, 0.0, -1.0 if CFG["a2"] == "a" else 0.0)):
+        fill(V("CR", 128 * k, 128 * k + 128), c / 128)
+    for k in range(3):
+        scaled(V("XA", 128 * k, 128 * k + 128), I1, 128.0)
+    fill(M("CAP"), 1.0)
+    fill(V("CAP", 0, 128, 16), 6.0)
+    fill(V("RST", 0, 1024), 1.0)
+    fill(V("RST", 0, 1024, 16), 0.0)
     ts(V("bi", 0, 16), V("bi", 0, 16), 255, ALU.bitwise_and)
-    if CFG["par"] == "a":
-        gp(lambda: g.affine_select(T.Tr2[:], T.GBb[:], [[1, 128]], ALU.is_ge, 0.0, 0, -1), [M("GBb")], [M("Tr2")])
-        gp(lambda: g.affine_select(T.tmpw[:, 0:128], T.GBb[:], [[1, 128]], ALU.is_equal, 0.0, -1, -1), [M("GBb")], [M("tmpw")])
-        ts(V("kcol", 0, 1), V("bi", 0, 1), 0.0, ALU.is_gt)
-        ts(M("Dm"), M("Ib"), V("kcol", 0, 1), ALU.mult)
-        tt(M("Dm"), M("Dm"), M("tmpw"), ALU.subtract)
-        ts(M("Dm"), M("Dm"), 0.5, ALU.mult)
-    ts(M("TrS"), M("Tr1"), 0.21875, ALU.mult)
-    cp(V("on16", 0, NM), V("ones", 0, NM))
-    ts(V("m96", 0, NM), V("ones", 0, NM), -96.0, ALU.mult)
-    fill(V("RST", 0, 16 * NM), 1.0)
-    fill(V("RST", 0, 16 * NM, 16), 0.0)
-    for p in range(2):
-        act(V("zs%d" % p, 0, 16 * NM), V("RST", 0, 16 * NM), ACT.Copy, scale=0.0)
-    ts(V("Ew", 0, 144), V("Eb", 0, 144), V("wcol", 0, 1), ALU.mult)
-    if "S" in modes:
-        ts(V("E2n", 0, 144), V("Eb", 0, 144), -2.0, ALU.mult)
-        tt(M("GB15"), M("GBb"), E(15), ALU.subtract)
-    if any(m[0] != "P" for m in CFG["mode"]):
-        ts(M("Ib16n"), M("Ib"), -16.0, ALU.mult)
-    if "R" in modes:
-        ts(V("E2", 0, 144), V("Eb", 0, 144), 2.0, ALU.mult)
-        ts(V("En", 0, 144), V("Eb", 0, 144), -1.0, ALU.mult)
-    fill(M("FK"), -0.5)
-    ts(M("Wb"), M("GBb"), V("wcol", 0, 1), ALU.mult)
-    tt(V("base", 0, 16), V("bi", 0, 16), V("bi", 16, 32), ALU.add)
+    ts(V("bi", 32, 48), V("bi", 32, 48), 2048, ALU.bitwise_and)
+    tt(V("bi", 16, 32), V("bi", 16, 32), V("bi", 32, 48), ALU.add)
+    tt(V("bi", 16, 32), V("bi", 16, 32), V("bi", 0, 16), ALU.add)
+    ts(V("bi", 16, 32), V("bi", 16, 32), 4095, ALU.bitwise_and)
+    cp(V("base", 0, 16), V("bi", 16, 32))
+    ts(V("kcol", 1, 2), V("bi", 0, 1), 0.0, ALU.is_gt)
+    ts(V("kcol", 2, 3), V("bi", 0, 1), 1.0 / 32, ALU.mult, 272.0, ALU.add)
+    ts(M("Dp"), I1, V("kcol", 1, 2), ALU.mult)
+    tt(M("Dp"), M("Dp"), M("tmpw"), ALU.subtract)
+    scaled(M("Dn"), M("Dp"), -2048.0)
+    scaled(M("Dp"), M("Dp"), 4096.0)
+    scaled(M("TrH"), M("TrH"), 0.5)
+    for h in range(2):
+        scaled(V("Sw", 64 * h, 64 * h + 64), V("Ib", 64 - 64 * h, 128 - 64 * h), 1.0)
+    scaled(M("Swh"), M("Sw"), 0.5)
+    fill(M("FK"), -8.0)
+    for s in range(2):
+        ts(V("Ew%d" % s, 0, 144), V("Eb", 0, 144), V("wcol", 8 * s, 8 * s + 1), ALU.mult)
+        ts(M("Wb%d" % s), GB, V("wcol", 8 * s, 8 * s + 1), ALU.mult)
 
     nxt = T.cores[(rank + 1) % len(T.cores)]
     sends = {}
-    turn = [0]
-    X = V("X", 0, 4096)
-    I1, In, F1, H1, Hn, GB = M("Ib"), M("Ibn"), M("F1"), M("H1"), M("Hn"), M("GBb")
 
-    def names(t, j):
-        q = t * NCH + j
-        p, o, n = q % NB, OFF[j], CH[j]
-        D = {"q": q, "p": p, "o": o, "n": n}
-        for nm in ("zr", "xc", "xo", "xh", "mc", "mo", "mh"):
-            D[nm] = V("%s%d" % (nm, p), 0, 16 * n)
-        D["ch"] = V("ch%d" % p, 0, 16 * n)
-        D["M"] = V("rm", 16 * o + 15, 16 * (o + n), 16)
+    def send(nm, t, s, src, dst):
+        rid, pid = topo.addr(nxt, core)
+        mask = sum(1 << x for x in topo.engines(core, nxt)[:NENG])
+        fn = lambda: g.remote_dma(ap(dst), ap(src), T.sem["%s%d_%d" % (nm, t + 1, s)], T.sem.left, pid, rid, mask)
+        sends[(nm, t, s)] = add("g", fn, regs(src), [], ("iss" if sends else "iss1", 0), "left", NENG)
 
-        def slot(base, k):
-            return V("%s%d" % (base, p), k * NM, k * NM + n)
-        for base, lst in (("f", ("dhs", "m1", "jd", "sOm", "sO", "m2", "HS", "CmS")), ("b", ("rec", "uq", "wa", "am", "sg", "J", "sp", "R", "eo", "ec")),
-                          ("i", ("pm", "r", "p2")), ("u", ("Cu", "chu"))):
-            for k, nm in enumerate(lst):
-                D[nm] = slot(base, k)
-        D["HO"] = V("s%d" % p, 0, 2 * n)
-        D["Hc"], D["Oc"] = V("s%d" % p, 0, n), V("s%d" % p, n, 2 * n)
-        D["stl"], D["x1"], D["chc"] = slot("s", 2), slot("s", 3), slot("s", 4)
-        lu, mz = "lu%d" % t, "mz%d" % t
-        D["LU"] = V(lu, 2 * o, 2 * o + 2 * n)
-        D["Hu"], D["Ou"] = V(lu, 2 * o, 2 * o + n), V(lu, 2 * o + n, 2 * o + 2 * n)
-        for k, nm in enumerate(("z", "G", "nI") if t == 1 else ("z", "nI", "G")):
-            D[nm] = V(mz, 3 * o + k * n, 3 * o + (k + 1) * n)
+    def pieces(cuts):
+        return list(zip(cuts[:-1], cuts[1:]))
+
+    def units(terms, first, final, free):
+        m = CFG["pt"]
+        for a in range(0, len(terms), m):
+            fi, la = first and a == 0, final and a + m >= len(terms)
+            mm(terms[a:a + m], fi, la, None if fi or la else free)
+
+    def reading(t, s):
+        cur[1], cur[2] = t, s
+        more, e = t < READS - 1, t % 2
+        X = V("X%d" % s, 0, 4096)
+        zr, xh, xo, xc, mh, mo, mc, ch, rm = [V("%s%d" % (nm, s), 0, 16 * n) for nm in ("zr", "xh", "xo", "xc", "mh", "mo", "mc", "ch", "rm")]
+        slot = lambda base, k, w=1: V("%s%d" % (base, s), k * n, (k + w) * n)
+        HS, t1, cq, jd, sOm, sO = [slot("f", k) for k in range(6)]
+        xq = slot("f", 6, 2)
+        eo, ec, a2, rec, wa, r, am, sg, uq, sp, R = [slot("b", k) for k in range(11)]
+        junk, ab = V("b%d" % s, 11 * n, 11 * n + 8), V("b%d" % s, 12 * n, 12 * n + 8)
+        AB, Hc, Oc, Cc, stl, fc = slot("s", 0, 2), slot("s", e), slot("s", 1 - e), slot("s", 2), slot("s", 3), slot("s", 4)
+        chc = slot("s", 5)
+        pm, p2, xv, ul = slot("i", 0), slot("i", 1), slot("i", 2, 2), V("i%d" % s, 4 * n, 4 * n + 8)
+        Cu, chu, nl = slot("u", 0), slot("u", 1), V("u%d" % s, 2 * n, 2 * n + 16)
+        LU = V("lu%d" % t, 2 * n * s, 2 * n * s + 2 * n)
+        Hu, Ou = sub(LU, e * n, e * n + n), sub(LU, n - e * n, 2 * n - e * n)
+        mz = lambda k, w=1, t=t: V("mz%d" % t, 384 * s + k * n, 384 * s + (k + w) * n)
+        z, G, nI = mz(0), mz(2 if t == 1 else 1), mz(1 if t == 1 else 2)
+        sz = lambda k, w=1: V("sz%d" % t, 512 * s + k * n, 512 * s + (k + w) * n)
+        Mx = V(rm[0], 15, 16 * n, 16)
+        A, B, C, D = [lambda k, w=1, b=b: V("p%d" % (4 * s + b), k * n, (k + w) * n) for b in range(4)]
+        Wb = M("Wb%d" % s)
+
+        phase("pre")
         if t == 0:
-            D["z"] = V(mz, o, o + n)
-        if t < READS - 1:
-            su, sz = "su%d" % t, "sz%d" % t
-            D["Hs"], D["Os"] = V(su, 2 * o + n, 2 * o + 2 * n), V(su, 2 * o, 2 * o + n)
-            for k, nm in enumerate(("zn", "nIn", "Gn", "J") if t else ("zn", "Gn", "J")):
-                D[nm] = V(sz, 4 * o + k * n, 4 * o + (k + 1) * n)
-            D["GJ"] = V(sz, D["Gn"][1], D["J"][2])
-
-        def ps(bk, k, w=1):
-            return V("p%d" % bk, k * n, (k + w) * n)
-        bank = {k: v[q % len(v)] for k, v in BANK.items()}
-        for bk, lst in (("L", (("OmH", 0), ("CmH", 1), ("Op", 2), ("S", 3), ("Hr", 4), ("t1", 3), ("cp", 4), ("De", 2), ("um", 3),
-                               ("Yw", 2), ("bp", 3), ("S2", 4))),
-                        ("C", (("dh", 0), ("do", 1), ("dc", 2), ("pf", 4), ("Vp", 0), ("zM", 1), ("sc", 2), ("Y", 0), ("bi", 1),
-                               ("H2", 2), ("up", 2), ("HSp", 3))),
-                        ("C" if CFG["gj"] == "a" else "L", (("X2", 3), ("X1", 4)))):
-            for nm, k in lst:
-                D[nm] = ps(bank[bk], k)
-        if CFG["uq"] == "v":
-            D["HS"] = D["HSp"]
-        D["X21"] = ps(bank["L"], 3, 2)
-        D["UB"] = "p%d" % bank["L"]
-        return D
-
-    def cut(n, w):
-        m = max(1, (n + w - 1) // w)
-        s = [2 * (n // 2 * i // m) for i in range(m + 1)]
-        return list(zip(s[:-1], s[1:]))
-
-    def pre(t, j):
-        phase("pre", j)
-        D = names(t, j)
-        n, o = D["n"], D["o"]
-        if t == 0:
-            cp(D["Hu"], V("li", o, o + n))
-            cp(D["Ou"], V("li", 256 + o, 256 + o + n))
+            cp(LU, V("li%d" % s, 0, 2 * n))
         else:
-            for nm, v in (("rl", D["LU"]), ("rz", V(D["z"][0], 3 * o, 3 * o + 3 * n))):
-                add("n", None, [], regs(v), ("net", 0), "%s%d_%d" % (nm, t, j), NENG, after=[sends[(nm, t - 1, j)]])
-        ts(D["HO"], D["LU"], -2048.0, ALU.add)
-        on = V("on16", 0, n)
-        mm([(D["Op"], [(H1, D["Oc"])]), (D["S"], [(M("H2080"), D["Hc"]), (M("H3232"), D["Oc"])]),
-            (D["OmH"], [(H1, D["Oc"]), (Hn, D["Hc"])]), (D["Hr"], [(H1, D["Hc"]), (M("H2048"), on)])])
-        tt(D["pm"], D["Hc"], D["Op"], ALU.mult)
-        tt(D["pm"], D["pm"], D["S"], ALU.add)
-        ts(D["pm"], D["pm"], 5, ALU.arith_shift_right, 4095, ALU.bitwise_and)
-        cp(D["Cu"], D["pm"])
-        ts(D["stl"], D["OmH"], 0.0, ALU.is_equal)
-        tt(D["HS"], D["stl"], D["Hr"], ALU.mult)
-        tt(D["CmH"], D["pm"], D["Hr"], ALU.subtract)
-        if t and CFG["par"] == "a":
-            act(D["CmS"], D["CmH"], ACT.Copy)
-        phase("zr", j)
-        if CFG["zq"][t][j] == "v":
-            zs = "zs%d" % (D["q"] % 2)
-            cp(V(zs, 0, 16 * n, 16), D["z"]) if CFG["zsq"] == "v" else act(V(zs, 0, 16 * n, 16), D["z"], ACT.Copy)
-            for a, b in cut(n, CFG["piece"]):
-                scan(sub(D["zr"], a, b, 16), V("RST", 16 * a, 16 * b), V(zs, 16 * a, 16 * b), ALU.mult, ALU.add)
-        else:
-            for k in range(16):
-                v = V(D["zr"][0], k, 16 * n, 16)
-                gp(lambda v=v: g.affine_select(ap(v), ap(D["z"]), [[0, n]], ALU.is_ge, 0.0, 0, 0), [D["z"]], [v])
-
-    def s1(t, j):
-        D = names(t, j)
-        n = D["n"]
-        phase("s1", j)
-        for nm in CFG["lists"]:
-            lst, mode = nm.upper() + "u", CFG["mode"][j]["hoc".find(nm)]
-            x, m = D["x" + nm], D["m" + nm]
-            for a, b in cut(n, CFG["piece" if mode in "PS" else "pv"]):
-                src = ind(X, sub(D[lst], a, b))
-                if mode in "PS":
-                    act(sub(x, a, b, 16), src, ACT.Copy)
-                else:
-                    tt(sub(x, a, b, 16), src, sub(D["zr"], a, b, 16), ALU.subtract)
-            for a, b in cut(n, CFG["ps"][j]) if mode == "S" else ():
-                end = V(x[0], 16 * a + 15, 16 * b, 16)
-                bk = V("p%d" % BANK["P"][turn[0] % len(BANK["P"])], 0, b - a)
-                turn[0] += 1
-                mm([(bk, [(In, sub(D["z"], a, b)), (I1, end)])])
-                if CFG["nil"] == "v":
-                    fill(end, 0.0)
-                elif CFG["nil"] == "a":
-                    act(end, sub(D["z"], a, b), ACT.Copy, scale=0.0)
-                else:
-                    gp(lambda end=end, a=a, b=b: g.affine_select(ap(end), ap(sub(D["z"], a, b)), [[0, b - a]], ALU.is_gt, 0.0, 0, 0), [sub(D["z"], a, b)], [end])
-                act(sub(D["e" + nm], a, b), bk, ACT.Abs)
-                scan(sub(m, a, b, 16), sub(D["zr"], a, b, 16), sub(x, a, b, 16), ALU.max, ALU.min)
-            for a, b in cut(n, CFG["pabs"]):
-                if mode == "A":
-                    act(sub(m, a, b, 16), sub(x, a, b, 16), ACT.Abs)
-                elif mode == "R":
-                    ts(sub(m, a, b, 16), sub(x, a, b, 16), 0.0, ALU.max)
-            col = lambda buf, e: [(E(b, e), V(buf[0], b, 16 * n, 16)) for b in range(16)]
-            d = D["d" + nm]
-            if mode == "P":
-                for a in range(0, 16 * n, 512):
-                    b = min(a + 512, 16 * n)
-                    bk = V("p%d" % BANK["P"][turn[0] % len(BANK["P"])], 0, b - a)
-                    turn[0] += 1
-                    mm([(bk, [(In, sub(D["zr"], a, b)), (I1, sub(x, a, b))])])
-                    act(sub(m, a, b), bk, ACT.Abs)
-            terms = col(x, "En") + col(m, "E2") if mode == "R" else col(m, "Eb")
-            if mode == "S":
-                terms = [(M("GB15"), D["z"])] + col(x, "Eb")[:15] + [(E(15), D["e" + nm])] + col(m, "E2n")[:15]
-            for a, b in cut(len(terms), CFG["pt"]):
-                mm([(d, terms[a:b])], a == 0, b == len(terms))
-            if nm == "h":
-                act(D["dhs"], d, ACT.Copy) if CFG["dcq"] == "a" else cp(D["dhs"], d)
-                if CFG["fast"][j]:
-                    mm([(D["Yw"], barred(D, t, "n"))])
-                else:
-                    mm([(D["Yw"], barred(D, t, "n") + [(F1, D["dhs"])])], True, False)
-            if nm == CFG["lists"][1] and CFG["fast"][j]:
-                tt(D["m2"], D["dhs"], D["do"], ALU.min)
-                tt(D["m2"], D["m2"], D["Yw"], ALU.add)
-
-    def barred(D, t, s):
-        if t and CFG["gj"] == "a":
-            return [(M("HB" + s), D["stl"]), (M("IbH" + s), D["G"]), (M("IbH" + s), V("ones", 0, D["n"]))]
-        return [(M("HB" + s), D["stl"])] + ([(M("IbB" + s), D["G"])] if t else [])
-
-    def choice(t, j):
-        D = names(t, j)
-        n = D["n"]
-        phase("ch", j)
-        if CFG["fast"][j]:
-            tt(D["wa"], D["m2"], D["dc"], ALU.is_gt)
-        tt(D["m1"], D["dhs"], D["dc"], ALU.min)
-        tt(D["rec"], D["m1"], D["do"], ALU.is_ge)
-        if not CFG["fast"][j]:
-            mm([(D["Yw"], [(M("IbBn"), D["rec"])])], False, True)
-            tt(D["wa"], D["m1"], D["Yw"], ALU.is_lt)
-        mm([(D["pf"], [(M("TrS"), D["wa"])])])
-        tt(D["t1"], D["rec"], D["OmH"], ALU.mult)
-        tt(D["x1"], D["Hc"], D["t1"], ALU.add)
-        tt(D["am"], D["wa"], D["pf"], ALU.is_gt)
-        tt(D["cp"], D["am"], D["CmH"], ALU.mult)
-        tt(D["chc"], D["x1"], D["cp"], ALU.add)
-        ts(D["chu"], D["chc"], 2048.0, ALU.add)
-        for (a, b), q in zip(cut(n, n // len(CFG["chq"][j])), CFG["chq"][j]):
-            src = ind(X, sub(D["chu"], a, b))
-            act(sub(D["ch"], a, b, 16), src, ACT.Copy) if q == "a" else cp(sub(D["ch"], a, b, 16), src)
-        terms = [(In, V(D["xh"][0], b, 16 * n, 16)) for b in range(16)] + [(I1, V(D["ch"][0], b, 16 * n, 16)) for b in range(16)]
-        for a, b in cut(32, CFG["pt"]):
-            mm([(D["Vp"], ([(M("Ib16n"), D["z"])] if a == 0 and CFG["mode"][j][0] != "P" else []) + terms[a:b])], a == 0, b == 32)
-        act(D["sg"], D["Vp"], ACT.Sign, bias=0.5)
-        mm([(D["De"], [(H1, D["chc"]), (Hn, D["Hc"])])])
-
-    def top(t, j):
-        D = names(t, j)
-        phase("top", j)
-        for a, b in cut(D["n"], D["n"] // len(CFG["chq"][j])):
-            scan(V("rm", 16 * (D["o"] + a), 16 * (D["o"] + b)), V("RST", 16 * a, 16 * b), sub(D["ch"], a, b, 16), ALU.mult, ALU.max)
-
-    def upd(t, j):
-        D = names(t, j)
-        phase("up", j)
-        if t < READS - 1:
-            mm([(D["zM"], [(I1, D["z"]), (In, D["M"])])])
-            act(D["zn"], D["zM"], ACT.Abs)
-        mm([(D["up"], [(M("Wb"), D["M"])])])
-        if CFG["uq"] == "a":
-            act(D["uq"], D["up"], ACT.Identity, bias=143.5 + 2.0 ** -13, scale=2.0 ** -12)
-            mm([(D["um"], [(M("Wb"), D["M"]), (M("Ib144"), V("ones", 0, D["n"])), (M("Ib4096n"), D["uq"])])])
-            tt(D["p2"], D["HS"], D["um"], ALU.mult)
-        else:
-            cp(D["p2"], D["up"])
-            ts(D["p2"], D["p2"], 4095, ALU.bitwise_and)
-            tt(D["p2"], D["p2"], D["HS"], ALU.mult)
-
-    def table(bank, o, n):
-        phase("tb", o)
-        k, c0 = n // 16, o // 16
-        U0, U1, nl = V("ul", c0, c0 + k), V("ul", 16 + c0, 16 + c0 + k), V("nl", c0, c0 + k)
-        UL = V(bank, 480, 480 + k)
-        mm([(UL, [(E(r, "Ew"), V("rm", 16 * (o + r) + 15, 16 * (o + n), 256)) for r in range(16)])])
-        cp(U0, UL)
-        ts(U1, U0, 15, ALU.bitwise_and)
-        tt(U1, U1, V("base", c0, c0 + k), ALU.add)
-        cp(nl, U1)
-        xv = V("xv", o, o + n)
-        tt(xv, ind(X, nl), V("rm", 16 * o + 15, 16 * (o + n), 16), ALU.add)
-        ts(xv, xv, 1, ALU.arith_shift_right)
-
-    def scat(o, n):
-        phase("sc", o)
-        cp(ind(X, V("nl", o // 16, (o + n) // 16)), V("xv", o, o + n))
-
-    def vote(t, j):
-        D = names(t, j)
-        n, o = D["n"], D["o"]
-        phase("vo", j)
-        sign = CFG["gj"] == "a"
-        more = t < READS - 1
-        x1 = (D["X1"], [(M("Ib128"), D["rec"]), (M("Ib128"), D["am"]), (M("H256"), D["stl"]), (GB, D["sg"])])
-        x2 = (D["X2"], [(M("Ib128"), D["am"])] + ([(M("Ib128" if sign else "Ib256"), D["G"])] if t else []) + [(GB, D["sg"])])
-        sc = (D["sc"], [(GB, D["sg"])])
-        if sign:
-            mm([x1, x2] + ([sc] if more else []))
-            act(D["J"], D["X1"], ACT.Sign, bias=-125.0)
-            if more:
-                act(D["Gn"], D["X2"], ACT.Sign, bias=3.0 if t else -125.0)
-        else:
-            mm([x1, x2])
-            if more:
-                mm([sc])
-                ts(D["GJ"], D["X21"], 126.0, ALU.is_ge)
+            for nm, v in (("rz", z), ("rl", LU), ("rg", mz(1, 2))):
+                add("n", None, [], regs(v), ("net", 0), "%s%d_%d" % (nm, t, s), NENG, after=[sends[(nm, t - 1, s)]])
+        ts(AB, LU, -2048.0, ALU.add)
+        mms([(B(0), [(H1, Oc)]), (B(1), [(M("H2080"), Hc), (M("H3232"), Oc)])])
+        tt(pm, Hc, B(0), ALU.mult)
+        tt(pm, pm, B(1), ALU.add)
+        ts(pm, pm, 5, ALU.arith_shift_right, 4095, ALU.bitwise_and)
+        cp(Cu, pm)
+        mms([(B(2), [(H1, Oc), (Hn, Hc)]), (B(3), [(H1, Hc), (M("H2048"), V("on16", 0, n))])])
+        ts(Cc, Cu, -2048.0, ALU.add)
+        ts(stl, B(2), 0.0, ALU.is_equal)
+        tt(HS, stl, B(3), ALU.mult)
+        mms([(B(0), [(Oc, H1), (Hc, Hn)]), (B(1), [(Cc, H1), (Hc, Hn)])])
+        phase("zr")
+        for k in range(16):
+            v = col(zr, k)
+            if k < CFG["zg"][t][s]:
+                gp(lambda v=v: g.affine_select(ap(v), ap(z), [[0, n]], ALU.is_ge, 0.0, 0, 0), [z], [v])
             else:
-                ts(D["J"], D["X1"], 126.0, ALU.is_ge)
+                cp(v, z)
+
+        phase("dist")
+        key = ("E", t, s)
+        mm([(A(0, 3), z, V("ZR", 0, 384)), (A(0, 3), M("ones"), V("CR", 0, 384))], True, False)
+        mm([(A(2), stl, M("H2n"))] + ([(A(2), G, M("Ib2n"))] if t else []), False, False, key)
+        term = lambda b, buf, k: (V(A(0)[0], b, 384, 16), buf, V("RG", 24 * k, 24 * k + 24))
+        for a, b in pieces(CFG["ph"]):
+            tt(sub(xh, a, b, 16), ind(X, sub(Hu, a, b)), sub(zr, a, b, 16), ALU.subtract)
+            ts(sub(mh, a, b, 16), sub(xh, a, b, 16), 0.0, ALU.min)
+        units([term(b, col(xh, b), 0) for b in range(16)], False, False, key)
+        units([term(b, col(mh, b), 3) for b in range(16)], False, False, key)
+        for k, lst, x, m, ee in ((1, Ou, xo, mo, eo), (2, Cu, xc, mc, ec)):
+            for a, b in pieces(CFG["po" if k == 1 else "pc"]):
+                for a1 in range(a, b, CFG["pg"]):
+                    act(sub(x, a1, a1 + CFG["pg"], 16), ind(X, sub(lst, a1, a1 + CFG["pg"])), ACT.Copy)
+                end = col(x, 15, a, b)
+                mm([(sub(C(k - 1), a, b), In, sub(z, a, b)), (sub(C(k - 1), a, b), I1, end)])
+                fill(end, 0.0) if CFG["nil"] == "v" else act(end, sub(z, a, b), ACT.Copy, scale=0.0)
+                scan(sub(m, a, b, 16), sub(zr, a, b, 16), sub(x, a, b, 16), ALU.max, ALU.min)
+            act(ee, C(k - 1), ACT.Abs)
+            units([term(b, col(x, b), k) for b in range(15)] + [term(15, ee, k)], False, False, key)
+            units([term(b, col(m, b), 3 + k) for b in range(15)], False, False, key)
+
+        phase("choice")
+        act(a2, A(1), ACT.Sign, bias=0.5) if CFG["a2"] == "a" else ts(a2, A(1), 0.0, ALU.is_ge)
+        tt(wa, a2, A(2), ALU.is_lt)
+        if CFG["am"] == "p":
+            scan(B(3), M("CAP"), wa, ALU.max, ALU.subtract)
+            tt(am, wa, B(3), ALU.min)
+        else:
+            scan(r, M("CAP"), wa, ALU.max, ALU.subtract)
+            mm([(B(3), I1, r), (B(3), M("Ib8"), wa)])
+            ts(am, B(3), 8.5, ALU.is_ge)
+        tt(cq, am, B(1), ALU.mult)
+        tt(rec, a2, A(0), ALU.is_ge)
+        tt(t1, rec, B(0), ALU.mult)
+        mm([(B(2), H1, Hc)], True, False)
+        mm([(B(2), t1, F1)], False, False, ("CH", t, s))
+        mm([(B(2), cq, F1)], False, False, ("CH", t, s))
+        ts(chu, B(2), 2048.0, ALU.add)
+        ts(chc, chu, -2048.0, ALU.add)
+        mm([(B(2), Hn, Hc), (B(2), H1, chc)])
+        key = ("V", t, s)
+        units([(C(2), M("Ib16n"), z)] + [(C(2), In, col(xh, b)) for b in range(16)], True, False, key)
+        for a, b, q in CFG["pch"]:
+            src = ind(X, sub(chu, a, b))
+            act(sub(ch, a, b, 16), src, ACT.Copy) if q == "a" else cp(sub(ch, a, b, 16), src)
+        for a, b in pieces(CFG["pm"]):
+            units([(sub(C(2), a, b), I1, col(ch, k, a, b)) for k in range(16)], False, False, key)
+        w = 3 if t else 2
+        I128 = V("XA", 0, 128)
+        mm([(A(0, w), am, V("XA", 0, 128 * w)), (A(0), rec, I128)] + ([(A(2), rec, I128)] if t else []), True, False)
+        mm([(A(0), M("H256"), stl)] + ([(A(2), M("H256"), stl), (A(1), M("Ib256"), G), (A(2), M("Ib512"), nI)] if t else []), False, False)
+        act(sg, C(2), ACT.Sign, bias=0.5)
+
+        phase("top")
+        HK = M("HK%d" % (t % 2))
+        mm([(D(1), M("H32"), Hc), (D(1), M("H2048"), V("m96", 0, n))] + ([(D(1), HK, stl), (D(1), HK, stl)] if t else []))
+        mm([(D(2), M("Ib144"), V("ones", 0, n))], True, False)
+        for a, b in pieces(CFG["pm"]):
+            scan(sub(rm, a, b, 16), V("RST", 0, 16 * (b - a)), sub(ch, a, b, 16), ALU.mult, ALU.max)
+        mms([(C(0), [(Wb, Mx)])] + ([(C(1), [(I1, z), (In, Mx)])] if more else []))
+        mm([(D(2), Wb, Mx)], False, False)
+        act(uq, C(0), ACT.Identity, bias=143.5 + 2.0 ** -13, scale=2.0 ** -12)
         if more:
-            act(V("junk", 0, n), D["sc"], ACT.Sign, bias=3.0, acc=V("kacc", 8 * (t % 2) + j, 8 * (t % 2) + j + 1))
-        else:
-            ts(V("oyg", o, o + n), D["X2"], -2.5 if sign else 126.0, ALU.is_ge)
-        tt(D["jd"], D["J"], D["De"], ALU.mult)
+            act(sz(0), C(1), ACT.Abs)
+            send("rz", t, s, sz(0), mz(0, 1, t + 1))
+        mm([(D(2), M("Ib4096n"), uq)], False, True)
+        UL, NL = V(D(0)[0], 384, 392), V(D(0)[0], 392, 408)
+        tt(p2, HS, D(2), ALU.mult)
+        tt(p2, p2, D(1), ALU.add)
+        ts(p2, p2, 5, ALU.arith_shift_right, 4095, ALU.bitwise_and)
+        ts(fc, p2, -2048.0, ALU.add)
+
+        phase("vote")
+        mm([(A(k), GB, sg) for k in ((2, 0, 1) if t else (0, 1))], False, True)
+        Hn_, On_ = B(e), B(1 - e)
+        oy = lambda k, w=1: V("oy%d" % s, k * n, (k + w) * n)
         if t:
-            one = 1.0 - (0.0 if not sign else 1.0 if t == 1 else 0.5)
-            mm([(D["Y"], [(M("Ibh") if sign and t == 1 else I1, D["nI"]), (M("Ibh") if sign else I1, D["J"])])])
-            act(D["sp"], D["Y"], ACT.Relu, bias=one, scale=-1.0)
+            act(sp, A(2), ACT.Sign, bias=125.5, scale=-1.0)
+            mm([(B(3), H1, Oc), (B(3), Hn, Hc)])
+            mm([(B(0, 2), M("Hh"), AB), (Hn_, M("Hh"), Hc), (On_, M("Hhn"), Hc)], True, False)
+            mm([(C(1), M("TrH"), sp)])
+            act(R, C(1), ACT.Identity, bias=V("kcol", 2, 3))
+            mm([(D(0), H1, Cc), (D(0), Hn, Hc)], True, False) if CFG["argD"] else mm([(C(3), H1, Cc), (C(3), Hn, Hc)], True, False)
+            arg = D(0) if CFG["argD"] else C(3)
+            mm([(arg, M("Dp"), R)], False, True)
+            act(sO, arg, ACT.Relu, bias=-4096.0)
+        else:
+            mm([(B(0, 2), H1, AB), (On_, Hn, Hc)], True, False)
+        if more:
+            ts(sz(1, 2), A(0, 2), 126.0, ALU.is_ge)
+        else:
+            ts(sz(1), A(0), 126.0, ALU.is_ge)
+            ts(oy(3), A(1), 126.0, ALU.is_ge)
+        tt(jd, sz(1), B(2), ALU.mult)
+        key = ("N", t, s)
+        if t:
+            tt(sOm, sp, B(3), ALU.mult)
+            mm([(On_, M("Fhn"), sOm)], False, False, key)
+            mm([(On_, M("Dn"), R), (Hn_, M("Dn"), R)], False, False, key)
+            mm([(Hn_, F1, jd)], False, False, key)
+            mm([(On_, F1, sO), (Hn_, F1, sO)], False, False, key)
+        else:
+            mm([(Hn_, F1, jd)], False, False, key)
+        mm([(On_, H1, fc)], False, False, key)
+        if more:
+            su = V("su%d" % t, 2 * n * s, 2 * n * s + 2 * n)
+            ts(su, B(0, 2), 2048.0, ALU.add)
+            send("rl", t, s, su, V("lu%d" % (t + 1), 2 * n * s, 2 * n * s + 2 * n))
+        elif CFG["outq"] == "v":
+            ts(oy(0, 2), B(0, 2), 2048.0, ALU.add)
+        else:
+            act(oy(0, 2), B(0, 2), ACT.Identity, bias=2048.0)
+        if t:
+            mm([(C(0), I1, nI), (C(0), I1, sz(1))])
             if more:
-                act(D["nIn"], D["Y"], ACT.Square, bias=one, scale=-1.0)
+                act(sz(3), C(0), ACT.Square, bias=1.0, scale=-1.0)
             else:
-                ts(V("oyi", o, o + n), D["Y"], one, ALU.is_equal)
-            if CFG["par"] == "a":
-                mm([(D["bi"], [(M("Tr2"), D["sp"])])])
-                act(D["R"], D["bi"], ACT.Identity, bias=271.5)
-                tt(D["sOm"], D["sp"], D["OmH"], ALU.mult)
-                mm([(D["bp"], [(M("Dm"), D["R"])])])
-                tt(D["sO"], D["CmS"], D["bp"], ALU.mult)
-            else:
-                mm([(D["bp"], [(M("Tr1"), D["sp"])])])
-                tt(D["r"], D["sp"], D["bp"], ALU.mult)
-                ts(D["r"], D["r"], 1, ALU.bitwise_and)
-                tt(D["sO"], D["r"], D["CmH"], ALU.mult)
-                tt(D["sOm"], D["sp"], D["OmH"], ALU.mult)
+                ts(oy(2), C(0), 1.0, ALU.is_equal)
+        if more:
+            send("rg", t, s, sz(2 if t else 1, 2), mz(1, 2, t + 1))
+            sc = V(C(0)[0], 128, 136)
+            mm([(sc, sg, G8)])
+            act(junk, sc, ACT.Sign, bias=3.0, acc=V("kacc", 2 * t + s, 2 * t + s + 1))
 
-    def post(t, j):
-        D = names(t, j)
-        n, o = D["n"], D["o"]
-        phase("po", j)
-        if CFG["gj"] == "a":
-            L = [(M("Hh"), D["Hc"]), (M("Hh"), D["chc"]), (M("Fh"), D["jd"])]
+            phase("table")
+            units([(UL, E(k, "Ew%d" % s), V(rm[0], 16 * k + 15, 16 * n, 256)) for k in range(16)], True, True, None)
+            cp(ul, UL)
+            ts(ul, ul, 15, ALU.bitwise_and)
+            cp(ab, ul)
+            mm([(NL, I1, V("base", 0, 16)), (sub(NL, 0, 8), I1, ab), (sub(NL, 8, 16), M("Sw"), ab)])
+            cp(nl, NL)
+            mms([(D(1), [(M("Ibh"), Mx)]), (D(2), [(M("Swh"), Mx)])])
+            act(xq, ind(X, nl), ACT.Identity, bias=-0.25, scale=0.5)
+            tt(xv, xq, D(1, 2), ALU.add)
+            cp(ind(X, nl), xv)
+            if s:
+                kb = V(D(0)[0], 408, 409)
+                mm([(kb, M("FK"), V("kacc", 2 * t + j, 2 * t + j + 1)) for j in range(2)])
+                ts(V("kcol", 0, 1), kb, 16384.0, ALU.add)
+                ts(M("HK%d" % (1 - t % 2)), H1, V("kcol", 0, 1), ALU.mult)
         else:
-            L = [(H1, D["Hc"]), (F1, D["jd"])]
-        L2 = [(M("H32"), D["Oc"]), (M("H2048"), V("m96", 0, n))]
-        if t:
-            mm([(D["H2"], L)], True, False)
-            mm([(D["S2"], L2 + [(M("HK"), D["stl"]), (M("HK"), D["stl"]), (M("F32n"), D["sOm"])])], True, False)
-            mm([(D["S2"], [(M("F32"), D["sO"])])], False, True)
-            mm([(D["H2"], [(F1, D["sO"])])], False, True)
-        else:
-            mm([(D["S2"], L2)])
-            mm([(D["H2"], L)])
-        tt(D["p2"], D["p2"], D["S2"], ALU.add)
-        ts(D["Hs"] if t < READS - 1 else V("oyb", o, o + n), D["H2"], 2048.0, ALU.add)
-        ts(D["p2"], D["p2"], 5, ALU.arith_shift_right, 4095, ALU.bitwise_and)
-        if t < READS - 1:
-            cp(D["Os"], D["p2"])
-            rid, pid = topo.addr(nxt, core)
-            mask = sum(1 << x for x in topo.engines(core, nxt)[:NENG])
-            for nm, src, dst in (("rz", V("sz%d" % t, 4 * o, 4 * o + 3 * n), V("mz%d" % (t + 1), 3 * o, 3 * o + 3 * n)),
-                                 ("rl", V("su%d" % t, 2 * o, 2 * o + 2 * n), V("lu%d" % (t + 1), 2 * o, 2 * o + 2 * n))):
-                fn = lambda nm=nm, src=src, dst=dst: g.remote_dma(ap(dst), ap(src), T.sem["%s%d_%d" % (nm, t + 1, j)], T.sem.left, pid, rid, mask)
-                sends[(nm, t, j)] = add("g", fn, regs(src), [], ("iss" if sends else "iss1", 0), "left", NENG)
-        else:
-            cp(V("oya", o, o + n), D["p2"])
-            for m, nm in enumerate(("yg", "yi", "yb", "ya")):
-                fn = lambda nm=nm: g.sync.dma_start(T[nm][:, o:o + n], T["o" + nm][:, o:o + n])
-                add("s", fn, regs(V("o" + nm, o, o + n)), [], ("dma", 0), "out%d" % (4 * j + m), 16)
+            for k, nm in ((3, "yg"), (2, "yi"), (0, "ya"), (1, "yb")):
+                pairs = [(T[nm][64 * s:64 * s + 64, n * h:n * h + n], ap(rows(oy(k), 64 * h, 64 * h + 64))) for h in range(2)]
+                dma2("a" if s and k == 1 else "s", pairs, regs(oy(k)), [], "out%d" % (4 * s + k), "dma")
 
-    def kcalc(t):
-        phase("kc", 0)
-        b = 8 * (t % 2)
-        kb = V(names(t, NCH - 1)["UB"], 500, 501)
-        mm([(kb, [(M("FK"), V("kacc", b + j, b + j + 1)) for j in range(NCH)])])
-        ts(V("kcol", 0, 1), kb, 16384.0, ALU.add)
-        ts(M("HK"), H1, V("kcol", 0, 1), ALU.mult)
-
-    pre(0, 0)
     for t in range(READS):
-        more = t < READS - 1
-        cur[2] = t
-        for j in range(NCH):
-            if j:
-                pre(t, j)
-            s1(t, j)
-        for j in range(NCH):
-            last = j == NCH - 1
-            choice(t, j)
-            top(t, j)
-            if more and j in CFG["tabs"]:
-                o = max([0] + [OFF[i] + CH[i] for i in CFG["tabs"] if i < j])
-                if last and o:
-                    scat(0, o)
-                table(names(t, j)["UB"], o, OFF[j] + CH[j] - o)
-                if last:
-                    scat(o, 256 - o)
-                    pre(t + 1, 0)
-            upd(t, j)
-            vote(t, j)
-            post(t, j)
-        if more:
-            kcalc(t)
-
-    for early, late in CFG["rules"]:
-        seen = []
-        for k, o in enumerate(ops):
-            if (o["tag"].split(":")[0], o["w"][0]) == early:
-                seen.append(k)
-        for k, o in enumerate(ops):
-            if (o["tag"].split(":")[0], o["w"][0]) == late:
-                for d in seen:
-                    if o["t"] == ops[d]["t"]:
-                        o["deps"].setdefault(d, False)
+        for s in range(2):
+            reading(t, s)
 
     if "it" not in ORDER:
+        ORDER["ops"] = ops
         ORDER["it"] = schedule(ops, EST, CFG["rounds"])
         if CFG["tries"]:
             ORDER["it"] = refine(ops, ORDER["it"][0], CFG["tries"], CFG["heat"])
     order, fin = ORDER["it"]
+    for k in order:
+        if ops[k]["free"] is not None and ops[k]["free"][0] != "open":
+            closer[ops[k]["free"]] = k
 
     eng = {"v": g.vector, "t": g.tensor, "a": g.scalar, "g": g, "s": g.sync}
     own = {"v": "qv", "t": "qt", "a": "qa", "g": "qg"}
@@ -858,7 +761,7 @@ def rank_program(g, core, T, topo):
     opclk = [None] * len(ops)
     for k in order:
         o = ops[k]
-        q = "a" if o["q"] == "s2" else o["q"]
+        q = o["q"]
         if q == "n":
             val[k] = (o["sem"], o["inc"])
             opclk[k] = {o["sem"]: o["inc"]}
@@ -877,9 +780,12 @@ def rank_program(g, core, T, topo):
         ins = o["fn"]()
         s = o["sem"] or own[q]
         total[s] = total.get(s, 0) + o["inc"]
-        if s != "left":
+        if o["dma"]:
+            for i in ins:
+                i.then_inc(T.sem[s], 16)
+        elif s != "left":
             ins.then_inc(T.sem[s], o["inc"])
-        val[k] = (s, o.get("need", total[s]))
+        val[k] = (s, total[s])
         opclk[k] = dict(c)
         if s != "left":
             opclk[k][s] = val[k][1]

@@ -1,4 +1,5 @@
 import math
+import numpy as np
 from concourse.mybir import dt, AluOpType as ALU, ActivationFunctionType as ACT
 
 n = 128
@@ -6,12 +7,16 @@ READS = 4
 NENG = 8
 EPS = 2.0 ** -12
 CFG = {
-    "ph": [0, 32, 64, 96, 128],
-    "po": [0, 64, 128], "pc": [0, 64, 128], "pg": 32,
+    "gh": [0, 32, 64, 96, 128],
+    "go": [0, 32, 64, 96, 128], "gc": [0, 32, 64, 96, 128], "fo": [0, 64, 128], "fc": [0, 64, 128], "HS": "a",
+    "po": [0, 64, 128], "pc": [0, 64, 128], "wait": 0.3, "margin": 500.0,
     "pch": [(0, 32, "a"), (32, 64, "a"), (64, 96, "a"), (96, 128, "v")], "pm": [0, 64, 128],
-    "zg": [[0, 8], [10, 10], [10, 10], [10, 10]],
-    "a2": "a", "am": "p", "nil": "v", "pt": 8, "outq": "v",
-    "argD": False, "lead": 9000.0, "rounds": 6, "tries": 120000, "heat": 0.0007, "seed": 1, "auto": 2, "far": 1,
+    "zg": [[0, 8], [2, 8], [8, 8], [8, 8]],
+    "za": [[8, 0], [6, 4], [4, 4], [4, 4]], "xlate": True, "ahead": [0, 0, 0, 0, 0, 0, 8],
+    "a2": "a", "nil": "vvaa", "pt": 16, "outq": "v",
+    "wide": True, "stages": [], "hord": [3, 1, 0, 0], "eo": [0, 128], "ec": [0, 128], "cool": 0.03, "mean": 2, "gaps": 10,
+    "pch3": [[(0, 32, "a"), (32, 64, "a"), (64, 96, "a"), (96, 128, "a")], [(0, 32, "a"), (32, 64, "v"), (64, 96, "a"), (96, 128, "v")]],
+    "solo": 0, "pr": [0, 64, 96, 128], "lead": 14000.0, "rounds": 6, "tries": 170000, "heat": 0.0007, "seed": 1, "auto": 2, "far": 1,
 }
 
 SCRATCH = {
@@ -23,14 +28,14 @@ SCRATCH = {
     "RST": ("sbuf", [128, 16 * 64], "bfloat16"), "CAP": ("sbuf", [128, 128], "bfloat16"),
     "kacc": ("sbuf", [128, 8], "float32"), "kcol": ("sbuf", [128, 4], "float32"),
     "RG": ("sbuf", [128, 144], "bfloat16"),
-    "ZR": ("sbuf", [128, 384], "bfloat16"), "CR": ("sbuf", [128, 384], "bfloat16"),
-    "XR": ("sbuf", [128, 384], "bfloat16"), "XA": ("sbuf", [128, 384], "bfloat16"),
+    "ZR": ("sbuf", [128, 384], "bfloat16"), "CR0": ("sbuf", [128, 384], "bfloat16"),
+    "CR1": ("sbuf", [128, 384], "bfloat16"), "XA": ("sbuf", [128, 384], "bfloat16"),
 }
-for _n in ("GBb", "Ib", "Ibn", "Ibh", "Swh", "Sw", "Ib2n", "Ib8", "Ib256", "Ib512", "Ib4096n", "Ib144", "Ib16n", "TrH", "Dp", "Dn"):
+for _n in ("GBb", "Ib", "Ibn", "Ibh", "Swh", "Sw", "Ib256", "Ib512", "Ib4096n", "Ib144", "Ib16n", "TrH", "Dp", "Dn"):
     SCRATCH[_n] = ("sbuf", [128, 128], "bfloat16")
-for _n in ("H1", "Hn", "Hh", "Hhn", "H2n", "H2080", "H3232", "H32", "H2048", "H256", "HK0", "HK1"):
+for _n in ("H1", "Hn", "Hh", "Hhn", "H2n", "H2080", "H3232", "H32", "H2048", "H4096", "H256", "HK0", "HK1"):
     SCRATCH[_n] = ("sbuf", [128, 128], "float16")
-for _n in ("F1", "Fhn", "FK"):
+for _n in ("F1", "Fh", "Fhn", "FK"):
     SCRATCH[_n] = ("sbuf", [128, 128], "float32")
 for _t in range(READS):
     SCRATCH["lu%d" % _t] = ("sbuf", [128, 512], "uint16")
@@ -60,7 +65,7 @@ SEMAPHORES += ["r%s%d_%d" % (k, t, s) for k in "lzg" for t in range(1, READS) fo
 SEMAPHORES += ["out%d" % k for k in range(8)]
 
 EST = {"cy": 0.9, "gam": 1.56, "scat": 3.0, "pec": 0.46, "fv": 20.0, "fa": 20.0, "wake": 130.0, "net": 5500.0, "dma": 2000.0,
-       "big": 7500.0, "late": 9000.0, "big2": 12000.0, "iss": 600.0, "iss1": 4500.0}
+       "big": 7500.0, "late": 9000.0, "big2": 12000.0, "big3": 5500.0, "iss": 600.0, "iss1": 4500.0}
 CASES = [{"cy": 0.9, "pec": 0.455, "fv": 15.0, "fa": 15.0, "wake": 140.0, "net": 5000.0},
          {"cy": 0.95, "pec": 0.48, "gam": 1.15, "fv": 0.0, "fa": 0.0, "wake": 110.0, "net": 6500.0, "late": 11000.0, "dma": 3000.0},
          {"cy": 1.1, "pec": 0.555, "gam": 2.0, "scat": 5.0, "fv": 15.0, "fa": 15.0, "wake": 170.0, "net": 5500.0, "big": 5500.0, "late": 6500.0, "big2": 9500.0}]
@@ -70,6 +75,8 @@ ORDER = {}
 def price(w, E):
     k, m = w
     cy = E["cy"]
+    if k in ("v2", "g2", "a2"):
+        return 2 * price((k[0], m), E)
     if k == "v":
         return E["fv"] + cy * max(64.0, m)
     if k == "a":
@@ -106,6 +113,10 @@ def place(qs, pred, cost, hold, W, pri):
                     best = (st, q, lst)
         st, q, lst = best
         k = max([k for k in lst if rt[k] <= st + 1e-9], key=lambda k: pri[k])
+        soon = [j for j in lst if rt[j] <= st + CFG["wait"] * hold[k] and pri[j] > pri[k] + CFG["margin"]]
+        if soon:
+            k = max(soon, key=lambda j: pri[j])
+            st = rt[k]
         lst.remove(k)
         free[q] = st + hold[k]
         fin[k] = st + cost[k]
@@ -118,6 +129,59 @@ def place(qs, pred, cost, hold, W, pri):
     return order, fin
 
 
+def fit(qs, pred, cost, hold, W, pri):
+    N = len(qs)
+    succ = [[] for _ in range(N)]
+    for k in range(N):
+        for d, w in pred[k].items():
+            succ[d].append((k, W if w else 0.0))
+    left = [len(p) for p in pred]
+    todo = {q: sorted([k for k in range(N) if qs[k] == q], key=lambda k: -pri[k]) for q in set(qs)}
+    free, order, rt, fin = {q: 0.0 for q in todo}, [], [0.0] * N, [None] * N
+    waits = 0
+
+    def guess(k, depth, memo):
+        if left[k] == 0:
+            return rt[k]
+        if depth == 0:
+            return 1e18
+        if k not in memo:
+            memo[k] = max([rt[k]] + [max(guess(d, depth - 1, memo), free[qs[d]]) + cost[d] + (W if w else 0.0)
+                                     for d, w in pred[k].items() if fin[d] is None])
+        return memo[k]
+
+    while len(order) < N:
+        st, q = min((max(free[q], min([rt[k] for k in lst[:CFG["see"]] if left[k] == 0] + [1e18])), q) for q, lst in todo.items() if lst)
+        if st >= 1e18:
+            st, q = min((max(free[q], min([rt[k] for k in lst if left[k] == 0] + [1e18])), q) for q, lst in todo.items() if lst)
+        memo, near, pick, first = {}, [], None, None
+        for k in todo[q]:
+            if left[k] == 0 and rt[k] <= st + 1e-9:
+                first = k if first is None else first
+                if q == "n" or not [e for j, e in near if pri[j] > pri[k] + CFG["margin"] and e < st + hold[k] - CFG["tol"]]:
+                    pick = k
+                    break
+            elif len(near) < CFG["see"]:
+                near.append((k, guess(k, 5, memo)))
+            if len(near) >= CFG["see"] and first is not None and pri[k] < pri[first] - CFG["deep"]:
+                break
+        if pick is None:
+            e = min(e for j, e in near if pri[j] > pri[first] + CFG["margin"])
+            if e - st < CFG["wait"] * hold[first] and waits < 40:
+                free[q] = max(e, st + 20.0)
+                waits += 1
+                continue
+            pick = first
+        waits = 0
+        todo[q].remove(pick)
+        free[q], fin[pick] = st + hold[pick], st + cost[pick]
+        order.append(pick)
+        for s, w in succ[pick]:
+            left[s] -= 1
+            rt[s] = max(rt[s], fin[pick] + w)
+    return order, fin
+
+
 def holds(ops, cost):
     return [0.0 if o["q"] == "n" else 120.0 if o["dma"] else c for o, c in zip(ops, cost)]
 
@@ -125,7 +189,7 @@ def holds(ops, cost):
 def schedule(ops, E, rounds):
     N = len(ops)
     W = E["wake"]
-    qs = [o["q"] for o in ops]
+    qs = [o["q"] + (str(o["s"]) if CFG["solo"] else "") for o in ops]
     cost = [price(o["w"], E) for o in ops]
     hold = holds(ops, cost)
     pred = [o["deps"] for o in ops]
@@ -134,9 +198,18 @@ def schedule(ops, E, rounds):
         for d, w in pred[k].items():
             back[d][k] = w
     pri = [0.0] * N
+    after, top = {}, {}
     for k in range(N - 1, -1, -1):
-        pri[k] = cost[k] + W + max([pri[s] for s in back[k]] + [0.0])
-    pri = [p + (0.0 if o["s"] else CFG["lead"]) for p, o in zip(pri, ops)]
+        o = ops[k]
+        pri[k] = cost[k] + W + max([pri[s] for s in back[k] if ops[s]["s"] == o["s"] or o["tag"] == "c"] + [0.0])
+        if o["w"][0] in ("ag", "vg") or (o["q"], o["tag"]) in (("v", "zr"), ("g", "zr"), ("a", "zr")):
+            key = (o["t"], o["s"], o["q"], o["tag"])
+            if key in after:
+                pri[k] = max(pri[k], cost[k] + pri[after[key]])
+            after[key] = k
+        if o["tag"] != "c":
+            top[o["t"], o["s"]] = max(top.get((o["t"], o["s"]), 0.0), pri[k] if o["q"] != "n" else 0.0)
+    pri = [p - top.get((o["t"] + 1, o["s"]), 0.0) - (2 * o["t"] + o["s"]) * CFG["lead"] for p, o in zip(pri, ops)]
     best = None
     for r in range(rounds + 1):
         order, fin = place(qs, pred, cost, hold, W, [pri[k] + ops[k].get("first", 0.0) for k in range(N)])
@@ -144,7 +217,181 @@ def schedule(ops, E, rounds):
             best = (order, fin)
         if r < rounds:
             pri = place(qs, back, cost, hold, W, fin)[1]
+    if CFG["solo"] == 2:
+        late = place(qs, back, cost, hold, W, best[1])[1]
+        mix = [CFG["mix"] * (c - f) + (1 - CFG["mix"]) * x for f, c, x in zip(best[1], cost, late)]
+        base = {(o["t"], o["s"]): mix[k] for k, o in reversed(list(enumerate(ops))) if o["tag"] == "choice"}
+        pri = [x - base[o["t"], o["s"]] - (2 * o["t"] + o["s"]) * CFG["lead"] + o.get("first", 0.0) for o, x in zip(ops, mix)]
+        best = fit([o["q"] for o in ops], pred, cost, hold, W, pri)
     return best
+
+
+def rhythm(ops, fin, tries, heat, parts, places, ncase, nudge):
+    N, L = len(ops), CFG["lead"]
+    q = ["vatgsn".find(o["q"]) for o in ops]
+    seen, kinds, kind = {}, {}, []
+    part = [-1 if o["tag"] == "c" else parts[2 * o["t"] + o["s"]] for o in ops]
+    for o, p in zip(ops, part):
+        key = (o["t"], o["s"], o["kind"])
+        seen[key] = seen.get(key, 0) + 1
+        kind.append(kinds.setdefault((o["kind"], seen[key], p), len(kinds)))
+    member = {p: {kind[k] for k in range(N) if part[k] == p} for p in set(part)}
+    turn = [(2 * o["t"] + o["s"]) * L for o in ops]
+    if places:
+        at = {kind[k]: places[k] - turn[k] + nudge.get((part[k], ops[k]["tag"]), 0.0) for k in range(N)}
+    else:
+        base, at = {}, {}
+        for k, o in enumerate(ops):
+            if o["tag"] == "choice":
+                base.setdefault((o["t"], o["s"]), fin[k])
+        for k, o in sorted(enumerate(ops), key=lambda e: (e[1]["t"], e[1]["s"]) != (2, 0)):
+            at.setdefault(kind[k], fin[k] - price(o["w"], EST) - base[o["t"], o["s"]])
+        first = min(at[kind[k]] for k, o in enumerate(ops) if o["w"][0] == "ag" and o["t"] == 2)
+        for x, o in {kind[k]: o for k, o in enumerate(ops) if o["tag"] not in ("c", "pre", "zr")}.items():
+            y, pts = at[x] - first, CFG["warp"][o["q"] == "a"]
+            more = pts[-1][1] if o["tag"] != "dist" else 0.0
+            for (a0, b0), (a1, b1) in zip(pts[:-1], pts[1:]):
+                if y >= a0 and o["tag"] == "dist":
+                    more = b0 + (b1 - b0) * min(1.0, (y - a0) / (a1 - a0))
+            at[x] += more
+    pre, suc = [{} for _ in kinds], [{} for _ in kinds]
+    for k, o in enumerate(ops):
+        for d in o["deps"]:
+            gap = turn[d] - turn[k] + 1e-3
+            pre[kind[k]][kind[d]] = max(pre[kind[k]].get(kind[d], -1e18), gap)
+            suc[kind[d]][kind[k]] = pre[kind[k]][kind[d]]
+
+    def push(at, x, v, back):
+        todo, steps = [(x, v)], 0
+        while todo:
+            x, v = todo.pop()
+            if (at[x] <= v) if back else (at[x] >= v):
+                continue
+            at[x] = v
+            steps += 1
+            if steps > 400:
+                return False
+            todo += [(y, v - gap) for y, gap in pre[x].items() if at[y] > v - gap] if back else \
+                [(y, v + gap) for y, gap in suc[x].items() if at[y] < v + gap]
+        return True
+
+    for _ in range(50):
+        for x in range(len(kinds)):
+            at[x] = max([at[x]] + [at[y] + gap for y, gap in pre[x].items()])
+    above, deps = [0] * N, []
+    for k in range(N):
+        keep = []
+        for d in sorted(ops[k]["deps"], reverse=True):
+            if not (above[k] >> d) & 1:
+                keep.append(d)
+            above[k] |= above[d] | (1 << d)
+        deps.append(keep)
+    cases = []
+    for c in CASES[:ncase]:
+        E = dict(EST, **c)
+        cost = [price(o["w"], E) for o in ops]
+        cases.append((cost, holds(ops, cost), [[(d, E["wake"] if ops[k]["deps"][d] else 0.0) for d in deps[k]] for k in range(N)], E["wake"]))
+
+    banks = [o["banks"] for o in ops]
+
+    def times(order, case):
+        cost, hold, dw, wake = case
+        fin, free, user = [0.0] * N, [0.0] * 6, [0] * 8
+        for k in order:
+            x = q[k]
+            st = free[x]
+            for b in banks[k]:
+                d = user[b]
+                user[b] = k
+                if q[d] != x and fin[d] + wake > st:
+                    st = fin[d] + wake
+            for d, w in dw[k]:
+                w += fin[d]
+                if w > st:
+                    st = w
+            fin[k] = st + cost[k]
+            if x < 5:
+                free[x] = st + hold[k]
+        return fin
+
+    def causes(order, case, fin):
+        cost, hold, dw, wake = case
+        last, why, user = [None] * 6, [None] * N, [0] * 8
+        for k in order:
+            x, st = q[k], fin[k] - cost[k] - 1e-6
+            p = last[x]
+            for b in banks[k]:
+                d, user[b] = user[b], k
+                if q[d] != x and fin[d] + wake >= st:
+                    p = d
+            for d, w in dw[k]:
+                if fin[d] + w >= st:
+                    p = d
+            why[k] = p
+            if x < 5:
+                last[x] = k
+        return why
+
+    seed = [CFG["seed"]]
+
+    def draw(m):
+        seed[0] = (seed[0] * 6364136223846793005 + 1442695040888963407) % 2 ** 64
+        return (seed[0] >> 33) % m
+
+    kinda, turna = np.array(kind), np.array(turn)
+
+    def sort(at):
+        return np.argsort(np.array([at[x] for x in range(len(kinds))])[kinda] + turna, kind="stable").tolist()
+
+    order = sort(at)
+    runs = [times(order, c) for c in cases]
+    worth = lambda fin: max(fin) + CFG["mean"] * sum(fin) / N
+    unit = [worth(r) for r in runs]
+    now, whys = 1.0, {}
+    best = (now, order, runs[0], at)
+    for done in range(tries):
+        i = draw(len(cases))
+        if i not in whys:
+            whys[i] = causes(order, cases[i], runs[i])
+        fin, why = runs[i], whys[i]
+        k, pairs = fin.index(max(fin)) if draw(4) else draw(N), []
+        while why[k] is not None:
+            if why[k] not in ops[k]["deps"]:
+                pairs.append((why[k], k))
+            k = why[k]
+        if not pairs:
+            continue
+        p, k = pairs[draw(len(pairs))]
+        new, far = dict(at), (1.0, 1.0, 300.0, 800.0, 1500.0)[draw(5)] * (1 + draw(100) / 100)
+        if kind[p] == kind[k]:
+            continue
+        if draw(100) < CFG["gaps"]:
+            v, far, mine = at[kind[k]] if draw(3) else -1e9, 50.0 + draw(1200), member[part[k]]
+            if draw(2):
+                new.update({x: at[x] + far for x in mine if at[x] >= v})
+            else:
+                new.update({x: at[x] - far if at[x] >= v else v - far + 0.001 * (at[x] - v) for x in mine if at[x] >= v - far})
+            ok = all(new[x] >= new[y] + gap - 9e-4 for x in new for y, gap in pre[x].items())
+        elif draw(2):
+            ok = push(new, kind[k], at[kind[p]] + turn[p] - turn[k] - far, True)
+        else:
+            ok = push(new, kind[p], at[kind[k]] + turn[k] - turn[p] + far, False)
+        if not ok:
+            continue
+        o2 = sort(new)
+        room = -math.log((draw(10 ** 6) + 1) / 10 ** 6) * heat * CFG["cool"] ** (done / tries)
+        r2, lost = list(runs), 0.0
+        for j in [i] + [j for j in range(len(unit)) if j != i]:
+            r2[j] = times(o2, cases[j])
+            lost += (worth(r2[j]) - worth(runs[j])) / unit[j] / len(unit)
+            if lost > room + 0.001:
+                break
+        if lost <= room:
+            at, order, runs, now, whys = new, o2, r2, now + lost, {}
+            if now < best[0]:
+                best = (now, order, runs[0], at)
+    ORDER.setdefault("rhythm", []).append([round(max(times(best[1], c))) for c in cases])
+    return best[1], best[2], [best[3][kind[k]] + turn[k] for k in range(N)]
 
 
 def refine(ops, order, tries, heat):
@@ -162,21 +409,30 @@ def refine(ops, order, tries, heat):
     for c in CASES:
         E = dict(EST, **c)
         cost = [price(o["w"], E) for o in ops]
-        cases.append((cost, holds(ops, cost), [[(d, E["wake"] if ops[k]["deps"][d] else 0.0) for d in deps[k]] for k in range(N)]))
+        cases.append((cost, holds(ops, cost), [[(d, E["wake"] if ops[k]["deps"][d] else 0.0) for d in deps[k]] for k in range(N)], E["wake"]))
+    banks = [o["banks"] for o in ops]
 
     def times(order, first, case, old, guess=None):
-        cost, hold, dw = case
-        fin, free = list(old), [None] * 5 + [0.0]
+        cost, hold, dw, wake = case
+        fin, free, user = list(old), [None] * 5 + [0.0], [None] * 8
         for k in reversed(order[:first]):
+            for b in banks[k]:
+                if user[b] is None:
+                    user[b] = k
             if free[q[k]] is None:
                 free[q[k]] = fin[k] - cost[k] + hold[k]
-                if None not in free[:4]:
-                    break
+            if None not in user and None not in free[:4]:
+                break
         free = [f or 0.0 for f in free]
         for j in range(first, N, 40):
             for k in order[j:j + 40]:
                 x = q[k]
                 st = free[x]
+                for b in banks[k]:
+                    d = user[b]
+                    user[b] = k
+                    if d is not None and q[d] != x and fin[d] + wake > st:
+                        st = fin[d] + wake
                 for d, w in dw[k]:
                     if fin[d] + w > st:
                         st = fin[d] + w
@@ -193,10 +449,14 @@ def refine(ops, order, tries, heat):
         return fin
 
     def chain(order, case, fin):
-        cost, hold, dw = case
-        before, last = [None] * N, [None] * 6
+        cost, hold, dw, wake = case
+        before, last, user, other = [None] * N, [None] * 6, [None] * 8, {}
         for k in order:
             before[k], last[q[k]] = last[q[k]], k
+            for b in banks[k]:
+                d, user[b] = user[b], k
+                if d is not None and q[d] != q[k] and fin[d] + wake >= fin[k] - cost[k] - 1e-6:
+                    other[k] = d
         k, out = fin.index(max(fin)), []
         while k is not None:
             st, p = fin[k] - cost[k], None
@@ -204,7 +464,7 @@ def refine(ops, order, tries, heat):
                 if fin[d] + w >= st - 1e-6:
                     p = d
             if p is None and q[k] < 5 and st > 0:
-                p = before[k]
+                p = other.get(k, before[k])
                 if p is not None:
                     out.append((p, k))
             k = p
@@ -291,12 +551,15 @@ def rank_program(g, core, T, topo):
     if rank is None:
         return
     ops = []
-    hist = {}
+    hist, span = {}, {}
     closer = {}
     cur = ["c", 0, 0]
 
     def phase(name):
         cur[0] = name
+
+    def plain(name):
+        return "ABCD"[int(name[1]) % 4] if SCRATCH[name][0] == "psum" else name[:-1] if name[:-1] + "0" in SCRATCH else name
 
     def meet(a, b):
         if a[0] >= b[1] or b[0] >= a[1]:
@@ -311,9 +574,7 @@ def rank_program(g, core, T, topo):
                 bank = SCRATCH[r[0]][0] == "psum"
                 for (d, dr, dw) in hist.get(r[0], ()):
                     same = ops[d]["q"] == q
-                    if bank and not same:
-                        deps[d] = True
-                    elif bank and q == "t":
+                    if bank and same and q == "t":
                         if free is None or ops[d]["free"] != free:
                             deps[d] = deps.get(d, False)
                     elif (isw or dw) and meet(r[1:], dr):
@@ -325,15 +586,16 @@ def rank_program(g, core, T, topo):
                 lst = hist.setdefault(r[0], [])
                 if isw:
                     if SCRATCH[r[0]][0] == "psum":
-                        lst = lst[-40:]
+                        lst = lst[-80:]
                     else:
                         lst = [e for e in lst if not (r[1] <= e[1][0] and e[1][1] <= r[2] and (r[3] == 1 or r[1:] == e[1]))]
                     hist[r[0]] = lst
-                if not (q == "t" and isw and lst and lst[-1][0] == k):
-                    lst.append((k, r[1:], isw))
+                lst.append((k, r[1:], isw))
         deps.pop(k, None)
         ops.append({"q": q, "fn": fn, "deps": deps, "w": w, "sem": sem, "inc": inc, "tag": cur[0], "t": cur[1], "s": cur[2],
-                    "free": free, "dma": dma, "out": wr[0] if wr else None})
+                    "free": free, "dma": dma, "out": wr[0] if wr else None,
+                    "banks": sorted({int(r[0][1]) for r in list(rd) + list(wr) if SCRATCH[r[0]][0] == "psum"}),
+                    "kind": (cur[0], q, w, tuple(sorted(plain(r[0]) for r in list(rd) + list(wr)))) if cur[0] != "c" else k})
         return k
 
     def V(name, a, b, step=1):
@@ -412,6 +674,9 @@ def rank_program(g, core, T, topo):
             c += max(min(64, l[4]), r[4]) * (4 if SCRATCH[r[0]][2] == "float32" else 1)
 
         me = len(ops)
+        if first:
+            span[wr[0][0]] = (wr[0][0], min(r[1] for r in wr), max(r[2] for r in wr), 1)
+        wr = [span[wr[0][0]]]
 
         def emit():
             last, stop = None, final or closer.get(free) == me
@@ -460,8 +725,10 @@ def rank_program(g, core, T, topo):
         load("s", V("li%d" % s, n, 2 * n), T.bb, s, "lb%d" % s, w)
         load("s", V("mz0", 384 * s, 384 * s + n), T.zp, s, "lz%d" % s, w)
         load("s", V("wcol", 8 * s, 8 * s + 1), T.wl, s, "lw%d" % s, "late", False)
-        if s == 0:
-            load("s", V("X1", 0, 4096), T.xt, 1, "lx1", "big2", False)
+    load("s", V("X1", 0, 4096), T.xt, 1, "lx1", "big2", False)
+    if CFG["xlate"]:
+        ops[-1]["deps"][0] = True
+        ops[-1]["w"] = ("big3", 0)
     for k in range(len(ops)):
         ops[k]["first"] = 1e9 - 1e6 * k
 
@@ -486,7 +753,7 @@ def rank_program(g, core, T, topo):
             act(out, in_, ACT.Copy, scale=c)
 
     for nm, c in (("H1", 1.0), ("Hn", -1.0), ("H2080", 2080.0), ("H3232", 3232.0), ("H2048", 2048.0), ("Ibn", -1.0), ("H2n", -2.0),
-                  ("Ib2n", -2.0), ("Ib8", 8.0), ("F1", 1.0), ("Ib16n", -16.0), ("H32", 32.0), ("H256", 256.0), ("Ib256", 256.0),
+                  ("Fh", 0.5), ("F1", 1.0), ("Ib16n", -16.0), ("H32", 32.0), ("H256", 256.0), ("H4096", 4096.0), ("Ib256", 256.0),
                   ("Ib512", 512.0), ("Ibh", 0.5), ("Hh", 0.5), ("Hhn", -0.5), ("Fhn", -0.5), ("Ib4096n", -4096.0), ("Ib144", 144 * 4096.0)):
         scaled(M(nm), I1, c)
     cp(V("on16", 0, n), V("ones", 0, n))
@@ -494,12 +761,12 @@ def rank_program(g, core, T, topo):
     for k, c in enumerate((-EPS, 0.0, EPS, EPS, -1.0, 0.0, 0.0, 1.0, -EPS)):
         scaled(V("RG", 8 * k, 8 * k + 8), G8, c)
     scaled(V("RG", 72, 144), V("RG", 0, 72), -2.0)
-    tt(V("ZR", 128, 256), GB, E(15), ALU.subtract)
-    scaled(V("ZR", 0, 128), V("ZR", 128, 256), EPS)
-    scaled(V("ZR", 256, 384), V("ZR", 128, 256), -EPS)
-    fill(V("ZR", 128, 256), 0.0)
+    tt(V("ZR", 256, 384), GB, E(15), ALU.subtract)
+    scaled(V("ZR", 0, 128), V("ZR", 256, 384), EPS)
+    scaled(V("ZR", 128, 256), V("ZR", 256, 384), -EPS)
     for k, c in enumerate((1.0, 0.0, -1.0 if CFG["a2"] == "a" else 0.0)):
-        fill(V("CR", 128 * k, 128 * k + 128), c / 128)
+        fill(V("CR0", 128 * k, 128 * k + 128), c / 128)
+        fill(V("CR1", 128 * k, 128 * k + 128), (c - (k == 2)) / 128)
     for k in range(3):
         scaled(V("XA", 128 * k, 128 * k + 128), I1, 128.0)
     fill(M("CAP"), 1.0)
@@ -528,13 +795,21 @@ def rank_program(g, core, T, topo):
         ts(M("Wb%d" % s), GB, V("wcol", 8 * s, 8 * s + 1), ALU.mult)
 
     nxt = T.cores[(rank + 1) % len(T.cores)]
+    prv = T.cores[(rank - 1) % len(T.cores)]
     sends = {}
+
+    def engines(src, dst, nm, t, s):
+        can = topo.engines(src, dst)
+        if not CFG["wide"]:
+            return can[:NENG]
+        return can[:NENG] if nm == "rz" or (nm, t, s) == ("rl", 0, 0) else can[-NENG:] if nm == "rg" else can
 
     def send(nm, t, s, src, dst):
         rid, pid = topo.addr(nxt, core)
-        mask = sum(1 << x for x in topo.engines(core, nxt)[:NENG])
+        use = engines(core, nxt, nm, t, s)
+        mask = sum(1 << x for x in use)
         fn = lambda: g.remote_dma(ap(dst), ap(src), T.sem["%s%d_%d" % (nm, t + 1, s)], T.sem.left, pid, rid, mask)
-        sends[(nm, t, s)] = add("g", fn, regs(src), [], ("iss" if sends else "iss1", 0), "left", NENG)
+        sends[(nm, t, s)] = add("g", fn, regs(src), [], ("iss" if sends else "iss1", 0), "left", len(use))
 
     def pieces(cuts):
         return list(zip(cuts[:-1], cuts[1:]))
@@ -573,70 +848,98 @@ def rank_program(g, core, T, topo):
             cp(LU, V("li%d" % s, 0, 2 * n))
         else:
             for nm, v in (("rz", z), ("rl", LU), ("rg", mz(1, 2))):
-                add("n", None, [], regs(v), ("net", 0), "%s%d_%d" % (nm, t, s), NENG, after=[sends[(nm, t - 1, s)]])
+                add("n", None, [], regs(v), ("net", 0), "%s%d_%d" % (nm, t, s), len(engines(prv, core, nm, t - 1, s)), after=[sends[(nm, t - 1, s)]])
         ts(AB, LU, -2048.0, ALU.add)
         mms([(B(0), [(H1, Oc)]), (B(1), [(M("H2080"), Hc), (M("H3232"), Oc)])])
         tt(pm, Hc, B(0), ALU.mult)
         tt(pm, pm, B(1), ALU.add)
         ts(pm, pm, 5, ALU.arith_shift_right, 4095, ALU.bitwise_and)
         cp(Cu, pm)
-        mms([(B(2), [(H1, Oc), (Hn, Hc)]), (B(3), [(H1, Hc), (M("H2048"), V("on16", 0, n))])])
+        mms([(B(2), [(H1, Oc), (Hn, Hc)])] + ([(B(3), [(H1, Hc), (M("H2048"), V("on16", 0, n))])] if CFG["HS"] == "v" else []))
         ts(Cc, Cu, -2048.0, ALU.add)
         ts(stl, B(2), 0.0, ALU.is_equal)
-        tt(HS, stl, B(3), ALU.mult)
+        if CFG["HS"] == "v":
+            tt(HS, stl, B(3), ALU.mult)
         mms([(B(0), [(Oc, H1), (Hc, Hn)]), (B(1), [(Cc, H1), (Hc, Hn)])])
         phase("zr")
-        for k in range(16):
-            v = col(zr, k)
+        for k in range(0, 16, 2):
+            vs = [col(zr, k), col(zr, k + 1)]
             if k < CFG["zg"][t][s]:
-                gp(lambda v=v: g.affine_select(ap(v), ap(z), [[0, n]], ALU.is_ge, 0.0, 0, 0), [z], [v])
+                add("g", lambda vs=vs: [g.affine_select(ap(v), ap(z), [[0, n]], ALU.is_ge, 0.0, 0, 0) for v in vs][-1], regs(z), regs(*vs), ("g2", n))
+            elif k < CFG["zg"][t][s] + CFG["za"][t][s]:
+                add("a", lambda vs=vs: [g.scalar.activation(ap(v), ap(z), ACT.Copy) for v in vs][-1], regs(z), regs(*vs), ("a2", n))
             else:
-                cp(v, z)
+                add("v", lambda vs=vs: [g.vector.tensor_copy(ap(v), ap(z)) for v in vs][-1], regs(z), regs(*vs), ("v2", n / 2))
 
         phase("dist")
         key = ("E", t, s)
-        mm([(A(0, 3), z, V("ZR", 0, 384)), (A(0, 3), M("ones"), V("CR", 0, 384))], True, False)
-        mm([(A(2), stl, M("H2n"))] + ([(A(2), G, M("Ib2n"))] if t else []), False, False, key)
+        mm([(A(0, 3), M("ones"), V("CR%d" % min(t, 1), 0, 384))], True, False)
+        mm([(A(0), z, V("ZR", 0, 128)), (A(2), z, V("ZR", 128, 256))], False, False, key)
+        mm([(A(2), stl, M("H2n"))] + ([(A(2), G, In)] if t else []), False, False, key)
         term = lambda b, buf, k: (V(A(0)[0], b, 384, 16), buf, V("RG", 24 * k, 24 * k + 24))
-        for a, b in pieces(CFG["ph"]):
-            tt(sub(xh, a, b, 16), ind(X, sub(Hu, a, b)), sub(zr, a, b, 16), ALU.subtract)
-            ts(sub(mh, a, b, 16), sub(xh, a, b, 16), 0.0, ALU.min)
-        units([term(b, col(xh, b), 0) for b in range(16)], False, False, key)
-        units([term(b, col(mh, b), 3) for b in range(16)], False, False, key)
-        for k, lst, x, m, ee in ((1, Ou, xo, mo, eo), (2, Cu, xc, mc, ec)):
-            for a, b in pieces(CFG["po" if k == 1 else "pc"]):
-                for a1 in range(a, b, CFG["pg"]):
-                    act(sub(x, a1, a1 + CFG["pg"], 16), ind(X, sub(lst, a1, a1 + CFG["pg"])), ACT.Copy)
+        hp = pieces(CFG["gh"])
+        lists = ((1, Ou, xo, mo, eo), (2, Cu, xc, mc, ec))
+        for k, lst, x, m, ee in lists:
+            for a, b in pieces(CFG["g" + "hoc"[k]]):
+                act(sub(x, a, b, 16), ind(X, sub(lst, a, b)), ACT.Copy)
+
+        def hpiece(m):
+            for a, b in hp[:m]:
+                tt(sub(xh, a, b, 16), ind(X, sub(Hu, a, b)), sub(zr, a, b, 16), ALU.subtract)
+                ts(sub(mh, a, b, 16), sub(xh, a, b, 16), 0.0, ALU.min)
+            del hp[:m]
+
+        turn = list(CFG["hord"])
+        for k, lst, x, m, ee in lists:
+            for a, b in pieces(CFG["f" + "hoc"[k]]):
+                hpiece(turn.pop(0))
                 end = col(x, 15, a, b)
                 mm([(sub(C(k - 1), a, b), In, sub(z, a, b)), (sub(C(k - 1), a, b), I1, end)])
-                fill(end, 0.0) if CFG["nil"] == "v" else act(end, sub(z, a, b), ACT.Copy, scale=0.0)
-                scan(sub(m, a, b, 16), sub(zr, a, b, 16), sub(x, a, b, 16), ALU.max, ALU.min)
+                nil = CFG["nil"][len(turn)]
+                if nil == "g":
+                    gp(lambda end=end: g.affine_select(ap(end), ap(end), [[0, end[4]]], ALU.is_gt, 0.0, 0, 0), [end], [end])
+                else:
+                    fill(end, 0.0) if nil == "v" else act(end, sub(z, a, b), ACT.Copy, scale=0.0)
+                for a1, b1 in pieces(CFG["p" + "hoc"[k]]):
+                    if a <= a1 < b:
+                        scan(sub(m, a1, b1, 16), sub(zr, a1, b1, 16), sub(x, a1, b1, 16), ALU.max, ALU.min)
             act(ee, C(k - 1), ACT.Abs)
-            units([term(b, col(x, b), k) for b in range(15)] + [term(15, ee, k)], False, False, key)
-            units([term(b, col(m, b), 3 + k) for b in range(15)], False, False, key)
+            if k == 2:
+                mm([term(15, ee, k)], False, False, key)
+            for a0, a1 in pieces(CFG["e" + "hoc"[k]]):
+                for buf, j in ((x, k), (m, 3 + k)):
+                    units([(rows(term(b, 0, j)[0], a0, a1), col(buf, b, a0, a1), term(b, 0, j)[2]) for b in range(15)], False, False, key)
+        hpiece(len(hp))
+        units([term(b, col(xh, b), 0) for b in range(16)], False, False, key)
+        units([term(b, col(mh, b), 3) for b in range(16)], False, False, key)
+        mm([term(15, eo, 1)], False, True)
+        if CFG["HS"] != "v":
+            mm([(C(3), H1, Hc), (C(3), M("H4096"), stl)])
+            act(HS, C(3), ACT.Relu, bias=-2048.0)
 
+        yield
+        cur[1], cur[2] = t, s
         phase("choice")
         act(a2, A(1), ACT.Sign, bias=0.5) if CFG["a2"] == "a" else ts(a2, A(1), 0.0, ALU.is_ge)
         tt(wa, a2, A(2), ALU.is_lt)
-        if CFG["am"] == "p":
-            scan(B(3), M("CAP"), wa, ALU.max, ALU.subtract)
-            tt(am, wa, B(3), ALU.min)
-        else:
-            scan(r, M("CAP"), wa, ALU.max, ALU.subtract)
-            mm([(B(3), I1, r), (B(3), M("Ib8"), wa)])
-            ts(am, B(3), 8.5, ALU.is_ge)
+        scan(B(3), M("CAP"), wa, ALU.max, ALU.subtract)
+        tt(am, wa, B(3), ALU.min)
         tt(cq, am, B(1), ALU.mult)
         tt(rec, a2, A(0), ALU.is_ge)
         tt(t1, rec, B(0), ALU.mult)
-        mm([(B(2), H1, Hc)], True, False)
-        mm([(B(2), t1, F1)], False, False, ("CH", t, s))
-        mm([(B(2), cq, F1)], False, False, ("CH", t, s))
-        ts(chu, B(2), 2048.0, ALU.add)
+        mm([(D(0), H1, Hc)], True, False)
+        mm([(D(0), t1, F1)], False, False, ("CH", t, s))
+        mm([(D(0), cq, F1)], False, False, ("CH", t, s))
+        ts(chu, D(0), 2048.0, ALU.add)
         ts(chc, chu, -2048.0, ALU.add)
-        mm([(B(2), Hn, Hc), (B(2), H1, chc)])
+        mm([(D(3), Hn, Hc), (D(3), H1, chc)])
+        HK = M("HK%d" % (t % 2))
+        mm([(D(1), M("H32"), Hc), (D(1), M("H2048"), V("m96", 0, n))] + ([(D(1), HK, stl), (D(1), HK, stl)] if t else []))
         key = ("V", t, s)
-        units([(C(2), M("Ib16n"), z)] + [(C(2), In, col(xh, b)) for b in range(16)], True, False, key)
-        for a, b, q in CFG["pch"]:
+        mm([(C(2), M("Ib16n"), z)], True, False)
+        for b in range(0, 16, 4):
+            mm([(C(2), In, col(xh, k)) for k in range(b, b + 4)], False, False, key)
+        for a, b, q in CFG["pch"] if more else CFG["pch3"][s]:
             src = ind(X, sub(chu, a, b))
             act(sub(ch, a, b, 16), src, ACT.Copy) if q == "a" else cp(sub(ch, a, b, 16), src)
         for a, b in pieces(CFG["pm"]):
@@ -644,23 +947,22 @@ def rank_program(g, core, T, topo):
         w = 3 if t else 2
         I128 = V("XA", 0, 128)
         mm([(A(0, w), am, V("XA", 0, 128 * w)), (A(0), rec, I128)] + ([(A(2), rec, I128)] if t else []), True, False)
-        mm([(A(0), M("H256"), stl)] + ([(A(2), M("H256"), stl), (A(1), M("Ib256"), G), (A(2), M("Ib512"), nI)] if t else []), False, False)
+        mm([(A(0), M("H256"), stl)] + ([(A(2), M("H256"), stl), (A(1), I128, G), (A(2), M("Ib256" if t == 1 else "Ib512"), nI)] if t else []),
+           False, False)
         act(sg, C(2), ACT.Sign, bias=0.5)
 
         phase("top")
-        HK = M("HK%d" % (t % 2))
-        mm([(D(1), M("H32"), Hc), (D(1), M("H2048"), V("m96", 0, n))] + ([(D(1), HK, stl), (D(1), HK, stl)] if t else []))
         mm([(D(2), M("Ib144"), V("ones", 0, n))], True, False)
-        for a, b in pieces(CFG["pm"]):
+        for a, b in pieces(CFG["pr"]):
             scan(sub(rm, a, b, 16), V("RST", 0, 16 * (b - a)), sub(ch, a, b, 16), ALU.mult, ALU.max)
-        mms([(C(0), [(Wb, Mx)])] + ([(C(1), [(I1, z), (In, Mx)])] if more else []))
+        mms([(B(2), [(Wb, Mx)])] + ([(B(3), [(I1, z), (In, Mx)])] if more else []))
         mm([(D(2), Wb, Mx)], False, False)
-        act(uq, C(0), ACT.Identity, bias=143.5 + 2.0 ** -13, scale=2.0 ** -12)
+        act(uq, B(2), ACT.Identity, bias=143.5 + 2.0 ** -13, scale=2.0 ** -12)
         if more:
-            act(sz(0), C(1), ACT.Abs)
+            act(sz(0), B(3), ACT.Abs)
             send("rz", t, s, sz(0), mz(0, 1, t + 1))
         mm([(D(2), M("Ib4096n"), uq)], False, True)
-        UL, NL = V(D(0)[0], 384, 392), V(D(0)[0], 392, 408)
+        UL, NL = V(D(0)[0], 0, 8), V(D(0)[0], 8, 24)
         tt(p2, HS, D(2), ALU.mult)
         tt(p2, p2, D(1), ALU.add)
         ts(p2, p2, 5, ALU.arith_shift_right, 4095, ALU.bitwise_and)
@@ -670,34 +972,31 @@ def rank_program(g, core, T, topo):
         mm([(A(k), GB, sg) for k in ((2, 0, 1) if t else (0, 1))], False, True)
         Hn_, On_ = B(e), B(1 - e)
         oy = lambda k, w=1: V("oy%d" % s, k * n, (k + w) * n)
+
         if t:
-            act(sp, A(2), ACT.Sign, bias=125.5, scale=-1.0)
+            act(sp, A(2), ACT.Sign, bias=125.5 - (256.0 if t == 1 else 0.0), scale=-1.0)
+            act(sz(1), A(0), ACT.Sign, bias=-125.5)
+            act(sz(2), A(1), ACT.Sign, bias=2.5) if more else ts(oy(3), A(1), -2.5, ALU.is_ge)
             mm([(B(3), H1, Oc), (B(3), Hn, Hc)])
-            mm([(B(0, 2), M("Hh"), AB), (Hn_, M("Hh"), Hc), (On_, M("Hhn"), Hc)], True, False)
+            mm([(B(0, 2), M("Hh"), AB), (Hn_, M("Hh"), chc), (On_, M("Hhn"), Hc)], True, False)
             mm([(C(1), M("TrH"), sp)])
             act(R, C(1), ACT.Identity, bias=V("kcol", 2, 3))
-            mm([(D(0), H1, Cc), (D(0), Hn, Hc)], True, False) if CFG["argD"] else mm([(C(3), H1, Cc), (C(3), Hn, Hc)], True, False)
-            arg = D(0) if CFG["argD"] else C(3)
-            mm([(arg, M("Dp"), R)], False, True)
-            act(sO, arg, ACT.Relu, bias=-4096.0)
+            mm([(C(3), H1, Cc), (C(3), Hn, Hc)], True, False)
+            mm([(C(3), M("Dp"), R)], False, True)
+            act(sO, C(3), ACT.Relu, bias=-4096.0)
         else:
-            mm([(B(0, 2), H1, AB), (On_, Hn, Hc)], True, False)
-        if more:
-            ts(sz(1, 2), A(0, 2), 126.0, ALU.is_ge)
-        else:
-            ts(sz(1), A(0), 126.0, ALU.is_ge)
-            ts(oy(3), A(1), 126.0, ALU.is_ge)
-        tt(jd, sz(1), B(2), ALU.mult)
+            act(sz(1, 2), A(0, 2), ACT.Sign, bias=-125.5)
+            mm([(B(0, 2), M("Hh"), AB), (Hn_, M("Hh"), chc), (On_, M("Hh"), Oc), (On_, Hn, Hc)], True, False)
+        tt(jd, sz(1), D(3), ALU.mult)
         key = ("N", t, s)
+        mm([(Hn_, M("Fh"), jd)], False, False, key)
         if t:
             tt(sOm, sp, B(3), ALU.mult)
             mm([(On_, M("Fhn"), sOm)], False, False, key)
             mm([(On_, M("Dn"), R), (Hn_, M("Dn"), R)], False, False, key)
-            mm([(Hn_, F1, jd)], False, False, key)
             mm([(On_, F1, sO), (Hn_, F1, sO)], False, False, key)
-        else:
-            mm([(Hn_, F1, jd)], False, False, key)
         mm([(On_, H1, fc)], False, False, key)
+        phase("post")
         if more:
             su = V("su%d" % t, 2 * n * s, 2 * n * s + 2 * n)
             ts(su, B(0, 2), 2048.0, ALU.add)
@@ -707,16 +1006,21 @@ def rank_program(g, core, T, topo):
         else:
             act(oy(0, 2), B(0, 2), ACT.Identity, bias=2048.0)
         if t:
-            mm([(C(0), I1, nI), (C(0), I1, sz(1))])
+            mm([(C(0), M("Ibh") if t == 1 else I1, nI), (C(0), M("Ibh"), sz(1))])
             if more:
-                act(sz(3), C(0), ACT.Square, bias=1.0, scale=-1.0)
+                act(sz(3), C(0), ACT.Square, bias=0.0 if t == 1 else 0.5, scale=-1.0)
             else:
-                ts(oy(2), C(0), 1.0, ALU.is_equal)
+                ts(oy(2), C(0), 0.5, ALU.is_equal)
         if more:
             send("rg", t, s, sz(2 if t else 1, 2), mz(1, 2, t + 1))
             sc = V(C(0)[0], 128, 136)
             mm([(sc, sg, G8)])
             act(junk, sc, ACT.Sign, bias=3.0, acc=V("kacc", 2 * t + s, 2 * t + s + 1))
+            if s:
+                kb = V(A(0)[0], 384, 385)
+                mm([(kb, M("FK"), V("kacc", 2 * t + j, 2 * t + j + 1)) for j in range(2)])
+                ts(V("kcol", 0, 1), kb, 16384.0, ALU.add)
+                ts(M("HK%d" % (1 - t % 2)), H1, V("kcol", 0, 1), ALU.mult)
 
             phase("table")
             units([(UL, E(k, "Ew%d" % s), V(rm[0], 16 * k + 15, 16 * n, 256)) for k in range(16)], True, True, None)
@@ -729,28 +1033,40 @@ def rank_program(g, core, T, topo):
             act(xq, ind(X, nl), ACT.Identity, bias=-0.25, scale=0.5)
             tt(xv, xq, D(1, 2), ALU.add)
             cp(ind(X, nl), xv)
-            if s:
-                kb = V(D(0)[0], 408, 409)
-                mm([(kb, M("FK"), V("kacc", 2 * t + j, 2 * t + j + 1)) for j in range(2)])
-                ts(V("kcol", 0, 1), kb, 16384.0, ALU.add)
-                ts(M("HK%d" % (1 - t % 2)), H1, V("kcol", 0, 1), ALU.mult)
         else:
             for k, nm in ((3, "yg"), (2, "yi"), (0, "ya"), (1, "yb")):
                 pairs = [(T[nm][64 * s:64 * s + 64, n * h:n * h + n], ap(rows(oy(k), 64 * h, 64 * h + 64))) for h in range(2)]
                 dma2("a" if s and k == 1 else "s", pairs, regs(oy(k)), [], "out%d" % (4 * s + k), "dma")
 
-    for t in range(READS):
-        for s in range(2):
-            reading(t, s)
+    turns = [reading(j // 2, j % 2) for j in range(2 * READS)]
+    for j in range(2 * READS + 1):
+        for r in turns[j:j + 1] + turns[max(j - 1, 0):j]:
+            next(r, None)
+    pick = lambda j, tag: [k for k, o in enumerate(ops) if (2 * o["t"] + o["s"], o["tag"], o["w"][0]) == (j, tag, "ag")]
+    for j, m in enumerate(CFG["ahead"]):
+        for k in pick(j, "choice"):
+            ops[k]["deps"].update({d: False for d in pick(j + 1, "dist")[:m]})
 
     if "it" not in ORDER:
         ORDER["ops"] = ops
         ORDER["it"] = schedule(ops, EST, CFG["rounds"])
-        if CFG["tries"]:
-            ORDER["it"] = refine(ops, ORDER["it"][0], CFG["tries"], CFG["heat"])
+        places = None
+        order, fin = ORDER["it"]
+        order = sorted(order, key=lambda k: fin[k] - price(ops[k]["w"], EST))
+        for tries, heat, parts, ncase, nudge in CFG["stages"]:
+            order, fin, places = rhythm(ops, ORDER["it"][1], tries, heat, parts, places, ncase, nudge)
+        ORDER["it"] = refine(ops, order, CFG["tries"], CFG["heat"])
+    user = {}
+    for k in ORDER["it"][0]:
+        for b in ops[k]["banks"]:
+            before, run = user.get(b, ([], []))
+            if run and ops[run[0]]["q"] != ops[k]["q"]:
+                before, run = run, []
+            ops[k]["deps"].update({d: True for d in before})
+            user[b] = (before, run + [k])
     order, fin = ORDER["it"]
     for k in order:
-        if ops[k]["free"] is not None and ops[k]["free"][0] != "open":
+        if ops[k]["free"] is not None and ops[k]["free"][0] != "E":
             closer[ops[k]["free"]] = k
 
     eng = {"v": g.vector, "t": g.tensor, "a": g.scalar, "g": g, "s": g.sync}

import math
import numpy as np
from concourse.mybir import dt, AluOpType as ALU, ActivationFunctionType as ACT

n = 128
READS = 4
NENG = 8
EPS = 2.0 ** -12
CFG = {
    "gh": [0, 32, 64, 96, 128],
    "go": [0, 32, 64, 96, 128], "gc": [0, 32, 64, 96, 128], "fo": [0, 64, 128], "fc": [0, 64, 128], "HS": "a",
    "po": [0, 64, 128], "pc": [0, 64, 128], "wait": 0.3, "margin": 500.0,
    "pch": [(0, 32, "a"), (32, 64, "a"), (64, 96, "a"), (96, 128, "v")], "pm": [0, 64, 128],
    "zg": [[0, 8], [2, 8], [8, 8], [8, 8]],
    "za": [[8, 0], [6, 4], [4, 4], [4, 4]], "xlate": True, "ahead": [0, 0, 0, 0, 0, 0, 8],
    "a2": "a", "nil": "vvaa", "pt": 16, "outq": "v",
    "wide": True, "stages": [], "hord": [3, 1, 0, 0], "eo": [0, 128], "ec": [0, 128], "cool": 0.03, "mean": 2, "gaps": 10,
    "pch3": [[(0, 32, "a"), (32, 64, "a"), (64, 96, "a"), (96, 128, "a")], [(0, 32, "a"), (32, 64, "v"), (64, 96, "a"), (96, 128, "v")]],
    "solo": 0, "pr": [0, 64, 96, 128], "lead": 14000.0, "rounds": 6, "tries": 170000, "heat": 0.0007, "seed": 1, "auto": 2, "far": 1,
}

SCRATCH = {
    "wcol": ("sbuf", [128, 16], "bfloat16"),
    "Eb": ("sbuf", [128, 144], "bfloat16"),
    "ones": ("sbuf", [128, 144], "bfloat16"), "tmpw": ("sbuf", [128, 144], "bfloat16"), "tmpw2": ("sbuf", [128, 144], "bfloat16"),
    "m96": ("sbuf", [128, n], "float16"), "on16": ("sbuf", [128, n], "float16"),
    "bi": ("sbuf", [128, 64], "int32"), "base": ("sbuf", [128, 16], "bfloat16"),
    "RST": ("sbuf", [128, 16 * 64], "bfloat16"), "CAP": ("sbuf", [128, 128], "bfloat16"),
    "kacc": ("sbuf", [128, 8], "float32"), "kcol": ("sbuf", [128, 4], "float32"),
    "RG": ("sbuf", [128, 144], "bfloat16"),
    "ZR": ("sbuf", [128, 384], "bfloat16"), "CR0": ("sbuf", [128, 384], "bfloat16"),
    "CR1": ("sbuf", [128, 384], "bfloat16"), "XA": ("sbuf", [128, 384], "bfloat16"),
}
for _n in ("GBb", "Ib", "Ibn", "Ibh", "Swh", "Sw", "Ib256", "Ib512", "Ib4096n", "Ib144", "Ib16n", "TrH", "Dp", "Dn"):
    SCRATCH[_n] = ("sbuf", [128, 128], "bfloat16")
for _n in ("H1", "Hn", "Hh", "Hhn", "H2n", "H2080", "H3232", "H32", "H2048", "H4096", "H256", "HK0", "HK1"):
    SCRATCH[_n] = ("sbuf", [128, 128], "float16")
for _n in ("F1", "Fh", "Fhn", "FK"):
    SCRATCH[_n] = ("sbuf", [128, 128], "float32")
for _t in range(READS):
    SCRATCH["lu%d" % _t] = ("sbuf", [128, 512], "uint16")
    SCRATCH["mz%d" % _t] = ("sbuf", [128, 768], "bfloat16")
    SCRATCH["sz%d" % _t] = ("sbuf", [128, 1024], "bfloat16")
    if _t < READS - 1:
        SCRATCH["su%d" % _t] = ("sbuf", [128, 512], "uint16")
for _p in range(2):
    SCRATCH["X%d" % _p] = ("sbuf", [128, 4096], "bfloat16")
    SCRATCH["li%d" % _p] = ("sbuf", [128, 256], "int32")
    SCRATCH["Ew%d" % _p] = ("sbuf", [128, 144], "bfloat16")
    SCRATCH["Wb%d" % _p] = ("sbuf", [128, 128], "bfloat16")
    for _n in ("zr", "xc", "xo", "xh", "mc", "mo", "mh", "ch", "rm"):
        SCRATCH["%s%d" % (_n, _p)] = ("sbuf", [128, 16 * n], "bfloat16")
    SCRATCH["f%d" % _p] = ("sbuf", [128, 8 * n], "float32")
    SCRATCH["b%d" % _p] = ("sbuf", [128, 13 * n], "bfloat16")
    SCRATCH["s%d" % _p] = ("sbuf", [128, 6 * n], "float16")
    SCRATCH["i%d" % _p] = ("sbuf", [128, 5 * n], "int32")
    SCRATCH["u%d" % _p] = ("sbuf", [128, 3 * n], "uint16")
    SCRATCH["oy%d" % _p] = ("sbuf", [128, 4 * n], "float32")
for _p in range(8):
    SCRATCH["p%d" % _p] = ("psum", [128, 512], "float32")

SEMAPHORES = ["qv", "qt", "qa", "qg", "left"]
SEMAPHORES += ["l%s%d" % (k, s) for k in "abzxw" for s in range(2)]
SEMAPHORES += ["r%s%d_%d" % (k, t, s) for k in "lzg" for t in range(1, READS) for s in range(2)]
SEMAPHORES += ["out%d" % k for k in range(8)]

EST = {"cy": 0.9, "gam": 1.56, "scat": 3.0, "pec": 0.46, "fv": 20.0, "fa": 20.0, "wake": 130.0, "net": 5500.0, "dma": 2000.0,
       "big": 7500.0, "late": 9000.0, "big2": 12000.0, "big3": 5500.0, "iss": 600.0, "iss1": 4500.0}
CASES = [{"cy": 0.9, "pec": 0.455, "fv": 15.0, "fa": 15.0, "wake": 140.0, "net": 5000.0},
         {"cy": 0.95, "pec": 0.48, "gam": 1.15, "fv": 0.0, "fa": 0.0, "wake": 110.0, "net": 6500.0, "late": 11000.0, "dma": 3000.0},
         {"cy": 1.1, "pec": 0.555, "gam": 2.0, "scat": 5.0, "fv": 15.0, "fa": 15.0, "wake": 170.0, "net": 5500.0, "big": 5500.0, "late": 6500.0, "big2": 9500.0}]
ORDER = {}


def price(w, E):
    k, m = w
    cy = E["cy"]
    if k in ("v2", "g2", "a2"):
        return 2 * price((k[0], m), E)
    if k == "v":
        return E["fv"] + cy * max(64.0, m)
    if k == "a":
        return E["fa"] + cy * m
    if k == "t":
        return E["pec"] * m
    if k == "g":
        return 170.0 + 2 * cy * m
    if k in ("vg", "ag"):
        return (50.0 if k == "vg" else 65.0) + cy * E["gam"] * m
    if k == "vs":
        return 50.0 + cy * E["scat"] * m
    return E[k]


def place(qs, pred, cost, hold, W, pri):
    N = len(qs)
    succ = [[] for _ in range(N)]
    for k in range(N):
        for d, w in pred[k].items():
            succ[d].append((k, W if w else 0.0))
    left = [len(p) for p in pred]
    ready, free, order = {q: [] for q in qs}, {q: 0.0 for q in qs}, []
    rt, fin = [0.0] * N, [0.0] * N
    for k in range(N):
        if left[k] == 0:
            ready[qs[k]].append(k)
    while len(order) < N:
        best = None
        for q, lst in ready.items():
            if lst:
                st = max(free[q], min([rt[k] for k in lst]))
                if best is None or st < best[0]:
                    best = (st, q, lst)
        st, q, lst = best
        k = max([k for k in lst if rt[k] <= st + 1e-9], key=lambda k: pri[k])
        soon = [j for j in lst if rt[j] <= st + CFG["wait"] * hold[k] and pri[j] > pri[k] + CFG["margin"]]
        if soon:
            k = max(soon, key=lambda j: pri[j])
            st = rt[k]
        lst.remove(k)
        free[q] = st + hold[k]
        fin[k] = st + cost[k]
        order.append(k)
        for s, w in succ[k]:
            left[s] -= 1
            rt[s] = max(rt[s], fin[k] + w)
            if left[s] == 0:
                ready[qs[s]].append(s)
    return order, fin


def fit(qs, pred, cost, hold, W, pri):
    N = len(qs)
    succ = [[] for _ in range(N)]
    for k in range(N):
        for d, w in pred[k].items():
            succ[d].append((k, W if w else 0.0))
    left = [len(p) for p in pred]
    todo = {q: sorted([k for k in range(N) if qs[k] == q], key=lambda k: -pri[k]) for q in set(qs)}
    free, order, rt, fin = {q: 0.0 for q in todo}, [], [0.0] * N, [None] * N
    waits = 0

    def guess(k, depth, memo):
        if left[k] == 0:
            return rt[k]
        if depth == 0:
            return 1e18
        if k not in memo:
            memo[k] = max([rt[k]] + [max(guess(d, depth - 1, memo), free[qs[d]]) + cost[d] + (W if w else 0.0)
                                     for d, w in pred[k].items() if fin[d] is None])
        return memo[k]

    while len(order) < N:
        st, q = min((max(free[q], min([rt[k] for k in lst[:CFG["see"]] if left[k] == 0] + [1e18])), q) for q, lst in todo.items() if lst)
        if st >= 1e18:
            st, q = min((max(free[q], min([rt[k] for k in lst if left[k] == 0] + [1e18])), q) for q, lst in todo.items() if lst)
        memo, near, pick, first = {}, [], None, None
        for k in todo[q]:
            if left[k] == 0 and rt[k] <= st + 1e-9:
                first = k if first is None else first
                if q == "n" or not [e for j, e in near if pri[j] > pri[k] + CFG["margin"] and e < st + hold[k] - CFG["tol"]]:
                    pick = k
                    break
            elif len(near) < CFG["see"]:
                near.append((k, guess(k, 5, memo)))
            if len(near) >= CFG["see"] and first is not None and pri[k] < pri[first] - CFG["deep"]:
                break
        if pick is None:
            e = min(e for j, e in near if pri[j] > pri[first] + CFG["margin"])
            if e - st < CFG["wait"] * hold[first] and waits < 40:
                free[q] = max(e, st + 20.0)
                waits += 1
                continue
            pick = first
        waits = 0
        todo[q].remove(pick)
        free[q], fin[pick] = st + hold[pick], st + cost[pick]
        order.append(pick)
        for s, w in succ[pick]:
            left[s] -= 1
            rt[s] = max(rt[s], fin[pick] + w)
    return order, fin


def holds(ops, cost):
    return [0.0 if o["q"] == "n" else 120.0 if o["dma"] else c for o, c in zip(ops, cost)]


def schedule(ops, E, rounds):
    N = len(ops)
    W = E["wake"]
    qs = [o["q"] + (str(o["s"]) if CFG["solo"] else "") for o in ops]
    cost = [price(o["w"], E) for o in ops]
    hold = holds(ops, cost)
    pred = [o["deps"] for o in ops]
    back = [{} for _ in range(N)]
    for k in range(N):
        for d, w in pred[k].items():
            back[d][k] = w
    pri = [0.0] * N
    after, top = {}, {}
    for k in range(N - 1, -1, -1):
        o = ops[k]
        pri[k] = cost[k] + W + max([pri[s] for s in back[k] if ops[s]["s"] == o["s"] or o["tag"] == "c"] + [0.0])
        if o["w"][0] in ("ag", "vg") or (o["q"], o["tag"]) in (("v", "zr"), ("g", "zr"), ("a", "zr")):
            key = (o["t"], o["s"], o["q"], o["tag"])
            if key in after:
                pri[k] = max(pri[k], cost[k] + pri[after[key]])
            after[key] = k
        if o["tag"] != "c":
            top[o["t"], o["s"]] = max(top.get((o["t"], o["s"]), 0.0), pri[k] if o["q"] != "n" else 0.0)
    pri = [p - top.get((o["t"] + 1, o["s"]), 0.0) - (2 * o["t"] + o["s"]) * CFG["lead"] for p, o in zip(pri, ops)]
    best = None
    for r in range(rounds + 1):
        order, fin = place(qs, pred, cost, hold, W, [pri[k] + ops[k].get("first", 0.0) for k in range(N)])
        if best is None or max(fin) < max(best[1]):
            best = (order, fin)
        if r < rounds:
            pri = place(qs, back, cost, hold, W, fin)[1]
    if CFG["solo"] == 2:
        late = place(qs, back, cost, hold, W, best[1])[1]
        mix = [CFG["mix"] * (c - f) + (1 - CFG["mix"]) * x for f, c, x in zip(best[1], cost, late)]
        base = {(o["t"], o["s"]): mix[k] for k, o in reversed(list(enumerate(ops))) if o["tag"] == "choice"}
        pri = [x - base[o["t"], o["s"]] - (2 * o["t"] + o["s"]) * CFG["lead"] + o.get("first", 0.0) for o, x in zip(ops, mix)]
        best = fit([o["q"] for o in ops], pred, cost, hold, W, pri)
    return best


def rhythm(ops, fin, tries, heat, parts, places, ncase, nudge):
    N, L = len(ops), CFG["lead"]
    q = ["vatgsn".find(o["q"]) for o in ops]
    seen, kinds, kind = {}, {}, []
    part = [-1 if o["tag"] == "c" else parts[2 * o["t"] + o["s"]] for o in ops]
    for o, p in zip(ops, part):
        key = (o["t"], o["s"], o["kind"])
        seen[key] = seen.get(key, 0) + 1
        kind.append(kinds.setdefault((o["kind"], seen[key], p), len(kinds)))
    member = {p: {kind[k] for k in range(N) if part[k] == p} for p in set(part)}
    turn = [(2 * o["t"] + o["s"]) * L for o in ops]
    if places:
        at = {kind[k]: places[k] - turn[k] + nudge.get((part[k], ops[k]["tag"]), 0.0) for k in range(N)}
    else:
        base, at = {}, {}
        for k, o in enumerate(ops):
            if o["tag"] == "choice":
                base.setdefault((o["t"], o["s"]), fin[k])
        for k, o in sorted(enumerate(ops), key=lambda e: (e[1]["t"], e[1]["s"]) != (2, 0)):
            at.setdefault(kind[k], fin[k] - price(o["w"], EST) - base[o["t"], o["s"]])
        first = min(at[kind[k]] for k, o in enumerate(ops) if o["w"][0] == "ag" and o["t"] == 2)
        for x, o in {kind[k]: o for k, o in enumerate(ops) if o["tag"] not in ("c", "pre", "zr")}.items():
            y, pts = at[x] - first, CFG["warp"][o["q"] == "a"]
            more = pts[-1][1] if o["tag"] != "dist" else 0.0
            for (a0, b0), (a1, b1) in zip(pts[:-1], pts[1:]):
                if y >= a0 and o["tag"] == "dist":
                    more = b0 + (b1 - b0) * min(1.0, (y - a0) / (a1 - a0))
            at[x] += more
    pre, suc = [{} for _ in kinds], [{} for _ in kinds]
    for k, o in enumerate(ops):
        for d in o["deps"]:
            gap = turn[d] - turn[k] + 1e-3
            pre[kind[k]][kind[d]] = max(pre[kind[k]].get(kind[d], -1e18), gap)
            suc[kind[d]][kind[k]] = pre[kind[k]][kind[d]]

    def push(at, x, v, back):
        todo, steps = [(x, v)], 0
        while todo:
            x, v = todo.pop()
            if (at[x] <= v) if back else (at[x] >= v):
                continue
            at[x] = v
            steps += 1
            if steps > 400:
                return False
            todo += [(y, v - gap) for y, gap in pre[x].items() if at[y] > v - gap] if back else \
                [(y, v + gap) for y, gap in suc[x].items() if at[y] < v + gap]
        return True

    for _ in range(50):
        for x in range(len(kinds)):
            at[x] = max([at[x]] + [at[y] + gap for y, gap in pre[x].items()])
    above, deps = [0] * N, []
    for k in range(N):
        keep = []
        for d in sorted(ops[k]["deps"], reverse=True):
            if not (above[k] >> d) & 1:
                keep.append(d)
            above[k] |= above[d] | (1 << d)
        deps.append(keep)
    cases = []
    for c in CASES[:ncase]:
        E = dict(EST, **c)
        cost = [price(o["w"], E) for o in ops]
        cases.append((cost, holds(ops, cost), [[(d, E["wake"] if ops[k]["deps"][d] else 0.0) for d in deps[k]] for k in range(N)], E["wake"]))

    banks = [o["banks"] for o in ops]

    def times(order, case):
        cost, hold, dw, wake = case
        fin, free, user = [0.0] * N, [0.0] * 6, [0] * 8
        for k in order:
            x = q[k]
            st = free[x]
            for b in banks[k]:
                d = user[b]
                user[b] = k
                if q[d] != x and fin[d] + wake > st:
                    st = fin[d] + wake
            for d, w in dw[k]:
                w += fin[d]
                if w > st:
                    st = w
            fin[k] = st + cost[k]
            if x < 5:
                free[x] = st + hold[k]
        return fin

    def causes(order, case, fin):
        cost, hold, dw, wake = case
        last, why, user = [None] * 6, [None] * N, [0] * 8
        for k in order:
            x, st = q[k], fin[k] - cost[k] - 1e-6
            p = last[x]
            for b in banks[k]:
                d, user[b] = user[b], k
                if q[d] != x and fin[d] + wake >= st:
                    p = d
            for d, w in dw[k]:
                if fin[d] + w >= st:
                    p = d
            why[k] = p
            if x < 5:
                last[x] = k
        return why

    seed = [CFG["seed"]]

    def draw(m):
        seed[0] = (seed[0] * 6364136223846793005 + 1442695040888963407) % 2 ** 64
        return (seed[0] >> 33) % m

    kinda, turna = np.array(kind), np.array(turn)

    def sort(at):
        return np.argsort(np.array([at[x] for x in range(len(kinds))])[kinda] + turna, kind="stable").tolist()

    order = sort(at)
    runs = [times(order, c) for c in cases]
    worth = lambda fin: max(fin) + CFG["mean"] * sum(fin) / N
    unit = [worth(r) for r in runs]
    now, whys = 1.0, {}
    best = (now, order, runs[0], at)
    for done in range(tries):
        i = draw(len(cases))
        if i not in whys:
            whys[i] = causes(order, cases[i], runs[i])
        fin, why = runs[i], whys[i]
        k, pairs = fin.index(max(fin)) if draw(4) else draw(N), []
        while why[k] is not None:
            if why[k] not in ops[k]["deps"]:
                pairs.append((why[k], k))
            k = why[k]
        if not pairs:
            continue
        p, k = pairs[draw(len(pairs))]
        new, far = dict(at), (1.0, 1.0, 300.0, 800.0, 1500.0)[draw(5)] * (1 + draw(100) / 100)
        if kind[p] == kind[k]:
            continue
        if draw(100) < CFG["gaps"]:
            v, far, mine = at[kind[k]] if draw(3) else -1e9, 50.0 + draw(1200), member[part[k]]
            if draw(2):
                new.update({x: at[x] + far for x in mine if at[x] >= v})
            else:
                new.update({x: at[x] - far if at[x] >= v else v - far + 0.001 * (at[x] - v) for x in mine if at[x] >= v - far})
            ok = all(new[x] >= new[y] + gap - 9e-4 for x in new for y, gap in pre[x].items())
        elif draw(2):
            ok = push(new, kind[k], at[kind[p]] + turn[p] - turn[k] - far, True)
        else:
            ok = push(new, kind[p], at[kind[k]] + turn[k] - turn[p] + far, False)
        if not ok:
            continue
        o2 = sort(new)
        room = -math.log((draw(10 ** 6) + 1) / 10 ** 6) * heat * CFG["cool"] ** (done / tries)
        r2, lost = list(runs), 0.0
        for j in [i] + [j for j in range(len(unit)) if j != i]:
            r2[j] = times(o2, cases[j])
            lost += (worth(r2[j]) - worth(runs[j])) / unit[j] / len(unit)
            if lost > room + 0.001:
                break
        if lost <= room:
            at, order, runs, now, whys = new, o2, r2, now + lost, {}
            if now < best[0]:
                best = (now, order, runs[0], at)
    ORDER.setdefault("rhythm", []).append([round(max(times(best[1], c))) for c in cases])
    return best[1], best[2], [best[3][kind[k]] + turn[k] for k in range(N)]


def refine(ops, order, tries, heat):
    N = len(ops)
    q = ["vatgsn".find(o["q"]) for o in ops]
    above, deps = [0] * N, []
    for k in range(N):
        keep = []
        for d in sorted(ops[k]["deps"], reverse=True):
            if not (above[k] >> d) & 1:
                keep.append(d)
            above[k] |= above[d] | (1 << d)
        deps.append(keep)
    cases = []
    for c in CASES:
        E = dict(EST, **c)
        cost = [price(o["w"], E) for o in ops]
        cases.append((cost, holds(ops, cost), [[(d, E["wake"] if ops[k]["deps"][d] else 0.0) for d in deps[k]] for k in range(N)], E["wake"]))
    banks = [o["banks"] for o in ops]

    def times(order, first, case, old, guess=None):
        cost, hold, dw, wake = case
        fin, free, user = list(old), [None] * 5 + [0.0], [None] * 8
        for k in reversed(order[:first]):
            for b in banks[k]:
                if user[b] is None:
                    user[b] = k
            if free[q[k]] is None:
                free[q[k]] = fin[k] - cost[k] + hold[k]
            if None not in user and None not in free[:4]:
                break
        free = [f or 0.0 for f in free]
        for j in range(first, N, 40):
            for k in order[j:j + 40]:
                x = q[k]
                st = free[x]
                for b in banks[k]:
                    d = user[b]
                    user[b] = k
                    if d is not None and q[d] != x and fin[d] + wake > st:
                        st = fin[d] + wake
                for d, w in dw[k]:
                    if fin[d] + w > st:
                        st = fin[d] + w
                fin[k] = st + cost[k]
                if x < 5:
                    free[x] = st + hold[k]
            if guess is not None and j > guess + 80 and j + 40 < N:
                gap = [fin[k] - old[k] for k in order[j - 80:j + 40]]
                if max(gap) - min(gap) < 1e-3:
                    if abs(gap[0]) > 1e-3:
                        for k in order[j + 40:]:
                            fin[k] += gap[0]
                    break
        return fin

    def chain(order, case, fin):
        cost, hold, dw, wake = case
        before, last, user, other = [None] * N, [None] * 6, [None] * 8, {}
        for k in order:
            before[k], last[q[k]] = last[q[k]], k
            for b in banks[k]:
                d, user[b] = user[b], k
                if d is not None and q[d] != q[k] and fin[d] + wake >= fin[k] - cost[k] - 1e-6:
                    other[k] = d
        k, out = fin.index(max(fin)), []
        while k is not None:
            st, p = fin[k] - cost[k], None
            for d, w in dw[k]:
                if fin[d] + w >= st - 1e-6:
                    p = d
            if p is None and q[k] < 5 and st > 0:
                p = other.get(k, before[k])
                if p is not None:
                    out.append((p, k))
            k = p
        return out

    def shift(order, a, b, back):
        seg = order[a:b + 1]
        me = seg[-1] if back else seg[0]
        take, mask, qs = {me}, above[me] if back else 1 << me, set()
        for x in (reversed(seg[:-1]) if back else seg[1:]):
            if ((mask >> x) & 1 if back else above[x] & mask) or q[x] in qs:
                if q[x] == q[me]:
                    return None
                take.add(x)
                mask |= above[x] if back else 1 << x
                if q[x] < 5:
                    qs.add(q[x])
        return order[:a] + [x for x in seg if (x in take) == back] + [x for x in seg if (x in take) != back] + order[b + 1:]

    seed = [CFG["seed"]]

    def draw(m):
        seed[0] = (seed[0] * 6364136223846793005 + 1442695040888963407) % 2 ** 64
        return (seed[0] >> 33) % m

    fins = [times(order, 0, c, [0.0] * N) for c in cases]
    unit = [max(f) for f in fins]
    best = (1.0, order, fins[0])
    done = 0
    while done < tries:
        i = draw(len(cases))
        pairs = chain(order, cases[i], fins[i])
        pos = [0] * N
        for j, x in enumerate(order):
            pos[x] = j
        for _ in range(6):
            done += 1
            p, k = pairs[draw(len(pairs))]
            a, b, back, more = pos[p], pos[k], draw(5) < 3, (0, 0, 1, 2, 3, 5, 8)[draw(7)]
            j = a if back else b
            ready = max([0.0] + [fins[i][d] + w for d, w in cases[i][2][k]]) if back and more > CFG["auto"] else None
            while more and 0 < j < N - 1:
                j += -1 if back else 1
                x = order[j]
                if q[x] == q[k]:
                    if ready is not None and fins[i][x] - 0.5 * cases[i][0][x] < ready:
                        break
                    a, b, more = min(a, j), max(b, j), more - (ready is None)
            if draw(10) < CFG["far"]:
                run = {x: y for x, y in pairs} if not back else {y: x for x, y in pairs}
                stops = [p if back else k]
                while stops[-1] in run:
                    stops.append(run[stops[-1]])
                a, b, new = pos[p], pos[k], None
                while new is None and stops:
                    a, b = (pos[stops[-1]], b) if back else (a, pos[stops[-1]])
                    new = shift(order, a, b, back)
                    stops = stops[:len(stops) * 2 // 3]
            else:
                new = shift(order, a, b, back)
            if new is None:
                continue
            room = -math.log((draw(10 ** 6) + 1) / 10 ** 6) * heat * 0.1 ** (done / tries) * len(unit)
            lost, f2 = 0.0, list(fins)
            for c in [i] + [c for c in range(len(unit)) if c != i]:
                f2[c] = times(new, a, cases[c], fins[c], b)
                lost += (max(f2[c]) - max(fins[c])) / unit[c]
                if lost > room + 0.002:
                    break
            if lost <= room:
                order, fins = new, f2 if draw(100) else [times(new, 0, c, f) for c, f in zip(cases, fins)]
                s = sum(max(f) / u for f, u in zip(fins, unit)) / len(unit)
                if s < best[0]:
                    best = (s, order, fins[0])
                break
    order = best[1]
    fins = [times(order, 0, c, [0.0] * N) for c in cases]
    ORDER["ends"] = [max(f) for f in fins]
    return order, fins[0]


def rank_program(g, core, T, topo):
    rank = T.rank_of(core)
    if rank is None:
        return
    ops = []
    hist, span = {}, {}
    closer = {}
    cur = ["c", 0, 0]

    def phase(name):
        cur[0] = name

    def plain(name):
        return "ABCD"[int(name[1]) % 4] if SCRATCH[name][0] == "psum" else name[:-1] if name[:-1] + "0" in SCRATCH else name

    def meet(a, b):
        if a[0] >= b[1] or b[0] >= a[1]:
            return False
        return not (a[2] == b[2] > 1 and a[0] % a[2] != b[0] % a[2])

    def add(q, fn, rd, wr, w, sem=None, inc=1, after=(), free=None, dma=False):
        k = len(ops)
        deps = {}
        for isw, regs in ((False, rd), (True, wr)):
            for r in regs:
                bank = SCRATCH[r[0]][0] == "psum"
                for (d, dr, dw) in hist.get(r[0], ()):
                    same = ops[d]["q"] == q
                    if bank and same and q == "t":
                        if free is None or ops[d]["free"] != free:
                            deps[d] = deps.get(d, False)
                    elif (isw or dw) and meet(r[1:], dr):
                        deps[d] = True
        for d in after:
            deps[d] = True
        for isw, regs in ((False, rd), (True, wr)):
            for r in regs:
                lst = hist.setdefault(r[0], [])
                if isw:
                    if SCRATCH[r[0]][0] == "psum":
                        lst = lst[-80:]
                    else:
                        lst = [e for e in lst if not (r[1] <= e[1][0] and e[1][1] <= r[2] and (r[3] == 1 or r[1:] == e[1]))]
                    hist[r[0]] = lst
                lst.append((k, r[1:], isw))
        deps.pop(k, None)
        ops.append({"q": q, "fn": fn, "deps": deps, "w": w, "sem": sem, "inc": inc, "tag": cur[0], "t": cur[1], "s": cur[2],
                    "free": free, "dma": dma, "out": wr[0] if wr else None,
                    "banks": sorted({int(r[0][1]) for r in list(rd) + list(wr) if SCRATCH[r[0]][0] == "psum"}),
                    "kind": (cur[0], q, w, tuple(sorted(plain(r[0]) for r in list(rd) + list(wr)))) if cur[0] != "c" else k})
        return k

    def V(name, a, b, step=1):
        return (name, a, b, step, (b - a + step - 1) // step, (slice(None), slice(a, b, step)), None)

    def rows(v, a, b):
        return v[:5] + ((slice(a, b), v[5][1]), None)

    def ap(v):
        if not isinstance(v, tuple):
            return v
        if v[6] is not None:
            return T[v[0]][v[5]].indirect(ap(v[6]))
        return T[v[0]][v[5]]

    def ind(win, off):
        return win[:4] + (16 * off[4], win[5], off)

    def regs(*vs):
        r = []
        for v in vs:
            if isinstance(v, tuple):
                r.append(v[:4])
                if v[6] is not None:
                    r.append(v[6][:4])
        return r

    def sub(v, a, b, k=1):
        return V(v[0], v[1] + k * a * v[3], v[1] + k * b * v[3] - v[3] + 1, v[3])

    def col(v, b, a0=0, a1=n):
        return V(v[0], 16 * a0 + b, 16 * a1, 16)

    def half(*vs):
        return 0.5 if all(SCRATCH[v[0]][2] in ("bfloat16", "uint16", "float16") for v in vs) else 1.0

    def tt(out, in0, in1, op):
        if in0[6] is not None:
            c = ("vg", out[4])
        else:
            c = ("v", out[4] * (1.0 if "psum" in (SCRATCH[in0[0]][0], SCRATCH[in1[0]][0]) else 2.0))
        return add("v", lambda: g.vector.tensor_tensor(ap(out), ap(in0), ap(in1), op), regs(in0, in1), regs(out), c)

    def ts(out, in0, s1, op0, s2=None, op1=None):
        def emit():
            if op1 is None:
                return g.vector.tensor_scalar(ap(out), ap(in0), ap(s1), None, op0)
            return g.vector.tensor_scalar(ap(out), ap(in0), ap(s1), ap(s2), op0, op1)
        return add("v", emit, regs(in0, s1, s2), regs(out), ("v", out[4] * half(out, in0)))

    def cp(out, in_):
        fn = lambda: g.vector.tensor_copy(ap(out), ap(in_))
        if out[6] is not None:
            return add("v", fn, regs(in_, out[6]), [out[:4]], ("vs", in_[4]))
        return add("v", fn, regs(in_), regs(out), ("vg", out[4]) if in_[6] is not None else ("v", out[4] * half(out, in_)))

    def scan(out, d0, d1, o0, o1):
        return add("v", lambda: g.vector.tensor_tensor_scan(ap(out), ap(d0), ap(d1), 0.0, o0, o1), regs(d0, d1), regs(out),
                   ("v", half(out, d0, d1) * out[4]))

    def fill(out, c):
        return add("v", lambda: g.vector.memset(ap(out), c), [], regs(out), ("v", out[4] * half(out)))

    def act(out, in_, func, bias=0.0, scale=1.0, acc=None):
        def emit():
            if acc is not None:
                return g.scalar.activation(ap(out), ap(in_), func, bias=ap(bias), scale=scale, accum_out=ap(acc))
            return g.scalar.activation(ap(out), ap(in_), func, bias=ap(bias), scale=scale)
        return add("a", emit, regs(in_, bias), regs(out, acc), ("a" if in_[6] is None else "ag", out[4]))

    def mm(terms, first=True, final=True, free=None):
        rd, wr, c = [], [], 0.0
        for out, l, r in terms:
            wr += regs(out)
            rd += regs(l, r)
            c += max(min(64, l[4]), r[4]) * (4 if SCRATCH[r[0]][2] == "float32" else 1)

        me = len(ops)
        if first:
            span[wr[0][0]] = (wr[0][0], min(r[1] for r in wr), max(r[2] for r in wr), 1)
        wr = [span[wr[0][0]]]

        def emit():
            last, stop = None, final or closer.get(free) == me
            for k, (out, l, r) in enumerate(terms):
                last = g.tensor.matmul(ap(out), ap(l), ap(r), first and k == 0, stop and k == len(terms) - 1)
            return last
        return add("t", emit, sorted(set(rd)), sorted(set(wr)), ("t", c), free=free)

    def mms(groups):
        rd, wr, c = [], [], 0.0
        for out, lst in groups:
            wr += regs(out)
            for l, r in lst:
                rd += regs(l, r)
                c += max(min(64, l[4]), r[4]) * (4 if SCRATCH[r[0]][2] == "float32" else 1)

        def emit():
            last = None
            for out, lst in groups:
                for k, (l, r) in enumerate(lst):
                    last = g.tensor.matmul(ap(out), ap(l), ap(r), k == 0, k == len(lst) - 1)
            return last
        return add("t", emit, sorted(set(rd)), wr, ("t", c))

    def gp(fn, rd, wr):
        return add("g", fn, regs(*rd), regs(*wr), ("g", wr[0][4]))

    def M(name):
        return V(name, 0, 128)

    def E(b, nm="Eb"):
        return V(nm, 15 - b, 15 - b + 128)

    def dma2(q, pairs, rd, wr, sem, w):
        fn = lambda: [(g.sync if q == "s" else g.scalar).dma_start(o, i) for o, i in pairs]
        return add(q, fn, rd, wr, (w, 0), sem, 32, dma=True)

    def load(q, dst, src, s, sem, w, split=True):
        m = src.shape[1] // 2 if split else 0
        dma2(q, [(ap(rows(dst, 64 * h, 64 * h + 64)), src[64 * s:64 * s + 64, m * h:m * h + dst[4]]) for h in range(2)], [], regs(dst), sem, w)

    load("a", V("X0", 0, 4096), T.xt, 0, "lx0", "big", False)
    for s in range(2):
        w = "late" if s else "dma"
        load("s", V("li%d" % s, 0, n), T.ba, s, "la%d" % s, w)
        load("s", V("li%d" % s, n, 2 * n), T.bb, s, "lb%d" % s, w)
        load("s", V("mz0", 384 * s, 384 * s + n), T.zp, s, "lz%d" % s, w)
        load("s", V("wcol", 8 * s, 8 * s + 1), T.wl, s, "lw%d" % s, "late", False)
    load("s", V("X1", 0, 4096), T.xt, 1, "lx1", "big2", False)
    if CFG["xlate"]:
        ops[-1]["deps"][0] = True
        ops[-1]["w"] = ("big3", 0)
    for k in range(len(ops)):
        ops[k]["first"] = 1e9 - 1e6 * k

    fill(V("ones", 0, 144), 1.0)
    gp(lambda: g.affine_select(T.tmpw[:], T.ones[:], [[-16, 9], [0, 16]], ALU.is_ge, 0.0, 0, 1), [V("ones", 0, 144)], [V("tmpw", 0, 144)])
    gp(lambda: g.affine_select(T.tmpw2[:], T.tmpw[:], [[16, 9], [0, 16]], ALU.is_ge, 0.0, 15, -1), [V("tmpw", 0, 144)], [V("tmpw2", 0, 144)])
    gp(lambda: g.affine_select(T.Ib[:], T.ones[:, 0:128], [[1, 128]], ALU.is_equal, 0.0, 0, -1), [V("ones", 0, 144)], [M("Ib")])
    cp(M("GBb"), V("tmpw2", 0, 128))
    gp(lambda: g.affine_select(T.Eb[:], T.tmpw2[:], [[0, 9], [1, 16]], ALU.is_equal, 0.0, -15, 0), [V("tmpw2", 0, 144)], [V("Eb", 0, 144)])
    gp(lambda: g.iota(T.bi[:, 0:16], [[0, 16]], 0, 16), [], [V("bi", 0, 16)])
    gp(lambda: g.iota(T.bi[:, 16:32], [[256, 16]], 0, 0), [], [V("bi", 16, 32)])
    gp(lambda: g.iota(T.bi[:, 32:48], [[0, 16]], 0, 32), [], [V("bi", 32, 48)])
    gp(lambda: g.affine_select(T.TrH[:], T.GBb[:], [[1, 128]], ALU.is_ge, 0.0, 0, -1), [M("GBb")], [M("TrH")])
    gp(lambda: g.affine_select(T.tmpw[:, 0:128], T.GBb[:], [[1, 128]], ALU.is_equal, 0.0, -1, -1), [M("GBb")], [M("tmpw")])
    I1, In, F1, H1, Hn, GB = M("Ib"), M("Ibn"), M("F1"), M("H1"), M("Hn"), M("GBb")
    G8 = V("GBb", 0, 128, 16)

    def scaled(out, in_, c):
        if SCRATCH[out[0]][2] == "float16":
            ts(out, in_, c, ALU.mult)
        else:
            act(out, in_, ACT.Copy, scale=c)

    for nm, c in (("H1", 1.0), ("Hn", -1.0), ("H2080", 2080.0), ("H3232", 3232.0), ("H2048", 2048.0), ("Ibn", -1.0), ("H2n", -2.0),
                  ("Fh", 0.5), ("F1", 1.0), ("Ib16n", -16.0), ("H32", 32.0), ("H256", 256.0), ("H4096", 4096.0), ("Ib256", 256.0),
                  ("Ib512", 512.0), ("Ibh", 0.5), ("Hh", 0.5), ("Hhn", -0.5), ("Fhn", -0.5), ("Ib4096n", -4096.0), ("Ib144", 144 * 4096.0)):
        scaled(M(nm), I1, c)
    cp(V("on16", 0, n), V("ones", 0, n))
    ts(V("m96", 0, n), V("ones", 0, n), -96.0, ALU.mult)
    for k, c in enumerate((-EPS, 0.0, EPS, EPS, -1.0, 0.0, 0.0, 1.0, -EPS)):
        scaled(V("RG", 8 * k, 8 * k + 8), G8, c)
    scaled(V("RG", 72, 144), V("RG", 0, 72), -2.0)
    tt(V("ZR", 256, 384), GB, E(15), ALU.subtract)
    scaled(V("ZR", 0, 128), V("ZR", 256, 384), EPS)
    scaled(V("ZR", 128, 256), V("ZR", 256, 384), -EPS)
    for k, c in enumerate((1.0, 0.0, -1.0 if CFG["a2"] == "a" else 0.0)):
        fill(V("CR0", 128 * k, 128 * k + 128), c / 128)
        fill(V("CR1", 128 * k, 128 * k + 128), (c - (k == 2)) / 128)
    for k in range(3):
        scaled(V("XA", 128 * k, 128 * k + 128), I1, 128.0)
    fill(M("CAP"), 1.0)
    fill(V("CAP", 0, 128, 16), 6.0)
    fill(V("RST", 0, 1024), 1.0)
    fill(V("RST", 0, 1024, 16), 0.0)
    ts(V("bi", 0, 16), V("bi", 0, 16), 255, ALU.bitwise_and)
    ts(V("bi", 32, 48), V("bi", 32, 48), 2048, ALU.bitwise_and)
    tt(V("bi", 16, 32), V("bi", 16, 32), V("bi", 32, 48), ALU.add)
    tt(V("bi", 16, 32), V("bi", 16, 32), V("bi", 0, 16), ALU.add)
    ts(V("bi", 16, 32), V("bi", 16, 32), 4095, ALU.bitwise_and)
    cp(V("base", 0, 16), V("bi", 16, 32))
    ts(V("kcol", 1, 2), V("bi", 0, 1), 0.0, ALU.is_gt)
    ts(V("kcol", 2, 3), V("bi", 0, 1), 1.0 / 32, ALU.mult, 272.0, ALU.add)
    ts(M("Dp"), I1, V("kcol", 1, 2), ALU.mult)
    tt(M("Dp"), M("Dp"), M("tmpw"), ALU.subtract)
    scaled(M("Dn"), M("Dp"), -2048.0)
    scaled(M("Dp"), M("Dp"), 4096.0)
    scaled(M("TrH"), M("TrH"), 0.5)
    for h in range(2):
        scaled(V("Sw", 64 * h, 64 * h + 64), V("Ib", 64 - 64 * h, 128 - 64 * h), 1.0)
    scaled(M("Swh"), M("Sw"), 0.5)
    fill(M("FK"), -8.0)
    for s in range(2):
        ts(V("Ew%d" % s, 0, 144), V("Eb", 0, 144), V("wcol", 8 * s, 8 * s + 1), ALU.mult)
        ts(M("Wb%d" % s), GB, V("wcol", 8 * s, 8 * s + 1), ALU.mult)

    nxt = T.cores[(rank + 1) % len(T.cores)]
    prv = T.cores[(rank - 1) % len(T.cores)]
    sends = {}

    def engines(src, dst, nm, t, s):
        can = topo.engines(src, dst)
        if not CFG["wide"]:
            return can[:NENG]
        return can[:NENG] if nm == "rz" or (nm, t, s) == ("rl", 0, 0) else can[-NENG:] if nm == "rg" else can

    def send(nm, t, s, src, dst):
        rid, pid = topo.addr(nxt, core)
        use = engines(core, nxt, nm, t, s)
        mask = sum(1 << x for x in use)
        fn = lambda: g.remote_dma(ap(dst), ap(src), T.sem["%s%d_%d" % (nm, t + 1, s)], T.sem.left, pid, rid, mask)
        sends[(nm, t, s)] = add("g", fn, regs(src), [], ("iss" if sends else "iss1", 0), "left", len(use))

    def pieces(cuts):
        return list(zip(cuts[:-1], cuts[1:]))

    def units(terms, first, final, free):
        m = CFG["pt"]
        for a in range(0, len(terms), m):
            fi, la = first and a == 0, final and a + m >= len(terms)
            mm(terms[a:a + m], fi, la, None if fi or la else free)

    def reading(t, s):
        cur[1], cur[2] = t, s
        more, e = t < READS - 1, t % 2
        X = V("X%d" % s, 0, 4096)
        zr, xh, xo, xc, mh, mo, mc, ch, rm = [V("%s%d" % (nm, s), 0, 16 * n) for nm in ("zr", "xh", "xo", "xc", "mh", "mo", "mc", "ch", "rm")]
        slot = lambda base, k, w=1: V("%s%d" % (base, s), k * n, (k + w) * n)
        HS, t1, cq, jd, sOm, sO = [slot("f", k) for k in range(6)]
        xq = slot("f", 6, 2)
        eo, ec, a2, rec, wa, r, am, sg, uq, sp, R = [slot("b", k) for k in range(11)]
        junk, ab = V("b%d" % s, 11 * n, 11 * n + 8), V("b%d" % s, 12 * n, 12 * n + 8)
        AB, Hc, Oc, Cc, stl, fc = slot("s", 0, 2), slot("s", e), slot("s", 1 - e), slot("s", 2), slot("s", 3), slot("s", 4)
        chc = slot("s", 5)
        pm, p2, xv, ul = slot("i", 0), slot("i", 1), slot("i", 2, 2), V("i%d" % s, 4 * n, 4 * n + 8)
        Cu, chu, nl = slot("u", 0), slot("u", 1), V("u%d" % s, 2 * n, 2 * n + 16)
        LU = V("lu%d" % t, 2 * n * s, 2 * n * s + 2 * n)
        Hu, Ou = sub(LU, e * n, e * n + n), sub(LU, n - e * n, 2 * n - e * n)
        mz = lambda k, w=1, t=t: V("mz%d" % t, 384 * s + k * n, 384 * s + (k + w) * n)
        z, G, nI = mz(0), mz(2 if t == 1 else 1), mz(1 if t == 1 else 2)
        sz = lambda k, w=1: V("sz%d" % t, 512 * s + k * n, 512 * s + (k + w) * n)
        Mx = V(rm[0], 15, 16 * n, 16)
        A, B, C, D = [lambda k, w=1, b=b: V("p%d" % (4 * s + b), k * n, (k + w) * n) for b in range(4)]
        Wb = M("Wb%d" % s)

        phase("pre")
        if t == 0:
            cp(LU, V("li%d" % s, 0, 2 * n))
        else:
            for nm, v in (("rz", z), ("rl", LU), ("rg", mz(1, 2))):
                add("n", None, [], regs(v), ("net", 0), "%s%d_%d" % (nm, t, s), len(engines(prv, core, nm, t - 1, s)), after=[sends[(nm, t - 1, s)]])
        ts(AB, LU, -2048.0, ALU.add)
        mms([(B(0), [(H1, Oc)]), (B(1), [(M("H2080"), Hc), (M("H3232"), Oc)])])
        tt(pm, Hc, B(0), ALU.mult)
        tt(pm, pm, B(1), ALU.add)
        ts(pm, pm, 5, ALU.arith_shift_right, 4095, ALU.bitwise_and)
        cp(Cu, pm)
        mms([(B(2), [(H1, Oc), (Hn, Hc)])] + ([(B(3), [(H1, Hc), (M("H2048"), V("on16", 0, n))])] if CFG["HS"] == "v" else []))
        ts(Cc, Cu, -2048.0, ALU.add)
        ts(stl, B(2), 0.0, ALU.is_equal)
        if CFG["HS"] == "v":
            tt(HS, stl, B(3), ALU.mult)
        mms([(B(0), [(Oc, H1), (Hc, Hn)]), (B(1), [(Cc, H1), (Hc, Hn)])])
        phase("zr")
        for k in range(0, 16, 2):
            vs = [col(zr, k), col(zr, k + 1)]
            if k < CFG["zg"][t][s]:
                add("g", lambda vs=vs: [g.affine_select(ap(v), ap(z), [[0, n]], ALU.is_ge, 0.0, 0, 0) for v in vs][-1], regs(z), regs(*vs), ("g2", n))
            elif k < CFG["zg"][t][s] + CFG["za"][t][s]:
                add("a", lambda vs=vs: [g.scalar.activation(ap(v), ap(z), ACT.Copy) for v in vs][-1], regs(z), regs(*vs), ("a2", n))
            else:
                add("v", lambda vs=vs: [g.vector.tensor_copy(ap(v), ap(z)) for v in vs][-1], regs(z), regs(*vs), ("v2", n / 2))

        phase("dist")
        key = ("E", t, s)
        mm([(A(0, 3), M("ones"), V("CR%d" % min(t, 1), 0, 384))], True, False)
        mm([(A(0), z, V("ZR", 0, 128)), (A(2), z, V("ZR", 128, 256))], False, False, key)
        mm([(A(2), stl, M("H2n"))] + ([(A(2), G, In)] if t else []), False, False, key)
        term = lambda b, buf, k: (V(A(0)[0], b, 384, 16), buf, V("RG", 24 * k, 24 * k + 24))
        hp = pieces(CFG["gh"])
        lists = ((1, Ou, xo, mo, eo), (2, Cu, xc, mc, ec))
        for k, lst, x, m, ee in lists:
            for a, b in pieces(CFG["g" + "hoc"[k]]):
                act(sub(x, a, b, 16), ind(X, sub(lst, a, b)), ACT.Copy)

        def hpiece(m):
            for a, b in hp[:m]:
                tt(sub(xh, a, b, 16), ind(X, sub(Hu, a, b)), sub(zr, a, b, 16), ALU.subtract)
                ts(sub(mh, a, b, 16), sub(xh, a, b, 16), 0.0, ALU.min)
            del hp[:m]

        turn = list(CFG["hord"])
        for k, lst, x, m, ee in lists:
            for a, b in pieces(CFG["f" + "hoc"[k]]):
                hpiece(turn.pop(0))
                end = col(x, 15, a, b)
                mm([(sub(C(k - 1), a, b), In, sub(z, a, b)), (sub(C(k - 1), a, b), I1, end)])
                nil = CFG["nil"][len(turn)]
                if nil == "g":
                    gp(lambda end=end: g.affine_select(ap(end), ap(end), [[0, end[4]]], ALU.is_gt, 0.0, 0, 0), [end], [end])
                else:
                    fill(end, 0.0) if nil == "v" else act(end, sub(z, a, b), ACT.Copy, scale=0.0)
                for a1, b1 in pieces(CFG["p" + "hoc"[k]]):
                    if a <= a1 < b:
                        scan(sub(m, a1, b1, 16), sub(zr, a1, b1, 16), sub(x, a1, b1, 16), ALU.max, ALU.min)
            act(ee, C(k - 1), ACT.Abs)
            if k == 2:
                mm([term(15, ee, k)], False, False, key)
            for a0, a1 in pieces(CFG["e" + "hoc"[k]]):
                for buf, j in ((x, k), (m, 3 + k)):
                    units([(rows(term(b, 0, j)[0], a0, a1), col(buf, b, a0, a1), term(b, 0, j)[2]) for b in range(15)], False, False, key)
        hpiece(len(hp))
        units([term(b, col(xh, b), 0) for b in range(16)], False, False, key)
        units([term(b, col(mh, b), 3) for b in range(16)], False, False, key)
        mm([term(15, eo, 1)], False, True)
        if CFG["HS"] != "v":
            mm([(C(3), H1, Hc), (C(3), M("H4096"), stl)])
            act(HS, C(3), ACT.Relu, bias=-2048.0)

        yield
        cur[1], cur[2] = t, s
        phase("choice")
        act(a2, A(1), ACT.Sign, bias=0.5) if CFG["a2"] == "a" else ts(a2, A(1), 0.0, ALU.is_ge)
        tt(wa, a2, A(2), ALU.is_lt)
        scan(B(3), M("CAP"), wa, ALU.max, ALU.subtract)
        tt(am, wa, B(3), ALU.min)
        tt(cq, am, B(1), ALU.mult)
        tt(rec, a2, A(0), ALU.is_ge)
        tt(t1, rec, B(0), ALU.mult)
        mm([(D(0), H1, Hc)], True, False)
        mm([(D(0), t1, F1)], False, False, ("CH", t, s))
        mm([(D(0), cq, F1)], False, False, ("CH", t, s))
        ts(chu, D(0), 2048.0, ALU.add)
        ts(chc, chu, -2048.0, ALU.add)
        mm([(D(3), Hn, Hc), (D(3), H1, chc)])
        HK = M("HK%d" % (t % 2))
        mm([(D(1), M("H32"), Hc), (D(1), M("H2048"), V("m96", 0, n))] + ([(D(1), HK, stl), (D(1), HK, stl)] if t else []))
        key = ("V", t, s)
        mm([(C(2), M("Ib16n"), z)], True, False)
        for b in range(0, 16, 4):
            mm([(C(2), In, col(xh, k)) for k in range(b, b + 4)], False, False, key)
        for a, b, q in CFG["pch"] if more else CFG["pch3"][s]:
            src = ind(X, sub(chu, a, b))
            act(sub(ch, a, b, 16), src, ACT.Copy) if q == "a" else cp(sub(ch, a, b, 16), src)
        for a, b in pieces(CFG["pm"]):
            units([(sub(C(2), a, b), I1, col(ch, k, a, b)) for k in range(16)], False, False, key)
        w = 3 if t else 2
        I128 = V("XA", 0, 128)
        mm([(A(0, w), am, V("XA", 0, 128 * w)), (A(0), rec, I128)] + ([(A(2), rec, I128)] if t else []), True, False)
        mm([(A(0), M("H256"), stl)] + ([(A(2), M("H256"), stl), (A(1), I128, G), (A(2), M("Ib256" if t == 1 else "Ib512"), nI)] if t else []),
           False, False)
        act(sg, C(2), ACT.Sign, bias=0.5)

        phase("top")
        mm([(D(2), M("Ib144"), V("ones", 0, n))], True, False)
        for a, b in pieces(CFG["pr"]):
            scan(sub(rm, a, b, 16), V("RST", 0, 16 * (b - a)), sub(ch, a, b, 16), ALU.mult, ALU.max)
        mms([(B(2), [(Wb, Mx)])] + ([(B(3), [(I1, z), (In, Mx)])] if more else []))
        mm([(D(2), Wb, Mx)], False, False)
        act(uq, B(2), ACT.Identity, bias=143.5 + 2.0 ** -13, scale=2.0 ** -12)
        if more:
            act(sz(0), B(3), ACT.Abs)
            send("rz", t, s, sz(0), mz(0, 1, t + 1))
        mm([(D(2), M("Ib4096n"), uq)], False, True)
        UL, NL = V(D(0)[0], 0, 8), V(D(0)[0], 8, 24)
        tt(p2, HS, D(2), ALU.mult)
        tt(p2, p2, D(1), ALU.add)
        ts(p2, p2, 5, ALU.arith_shift_right, 4095, ALU.bitwise_and)
        ts(fc, p2, -2048.0, ALU.add)

        phase("vote")
        mm([(A(k), GB, sg) for k in ((2, 0, 1) if t else (0, 1))], False, True)
        Hn_, On_ = B(e), B(1 - e)
        oy = lambda k, w=1: V("oy%d" % s, k * n, (k + w) * n)

        if t:
            act(sp, A(2), ACT.Sign, bias=125.5 - (256.0 if t == 1 else 0.0), scale=-1.0)
            act(sz(1), A(0), ACT.Sign, bias=-125.5)
            act(sz(2), A(1), ACT.Sign, bias=2.5) if more else ts(oy(3), A(1), -2.5, ALU.is_ge)
            mm([(B(3), H1, Oc), (B(3), Hn, Hc)])
            mm([(B(0, 2), M("Hh"), AB), (Hn_, M("Hh"), chc), (On_, M("Hhn"), Hc)], True, False)
            mm([(C(1), M("TrH"), sp)])
            act(R, C(1), ACT.Identity, bias=V("kcol", 2, 3))
            mm([(C(3), H1, Cc), (C(3), Hn, Hc)], True, False)
            mm([(C(3), M("Dp"), R)], False, True)
            act(sO, C(3), ACT.Relu, bias=-4096.0)
        else:
            act(sz(1, 2), A(0, 2), ACT.Sign, bias=-125.5)
            mm([(B(0, 2), M("Hh"), AB), (Hn_, M("Hh"), chc), (On_, M("Hh"), Oc), (On_, Hn, Hc)], True, False)
        tt(jd, sz(1), D(3), ALU.mult)
        key = ("N", t, s)
        mm([(Hn_, M("Fh"), jd)], False, False, key)
        if t:
            tt(sOm, sp, B(3), ALU.mult)
            mm([(On_, M("Fhn"), sOm)], False, False, key)
            mm([(On_, M("Dn"), R), (Hn_, M("Dn"), R)], False, False, key)
            mm([(On_, F1, sO), (Hn_, F1, sO)], False, False, key)
        mm([(On_, H1, fc)], False, False, key)
        phase("post")
        if more:
            su = V("su%d" % t, 2 * n * s, 2 * n * s + 2 * n)
            ts(su, B(0, 2), 2048.0, ALU.add)
            send("rl", t, s, su, V("lu%d" % (t + 1), 2 * n * s, 2 * n * s + 2 * n))
        elif CFG["outq"] == "v":
            ts(oy(0, 2), B(0, 2), 2048.0, ALU.add)
        else:
            act(oy(0, 2), B(0, 2), ACT.Identity, bias=2048.0)
        if t:
            mm([(C(0), M("Ibh") if t == 1 else I1, nI), (C(0), M("Ibh"), sz(1))])
            if more:
                act(sz(3), C(0), ACT.Square, bias=0.0 if t == 1 else 0.5, scale=-1.0)
            else:
                ts(oy(2), C(0), 0.5, ALU.is_equal)
        if more:
            send("rg", t, s, sz(2 if t else 1, 2), mz(1, 2, t + 1))
            sc = V(C(0)[0], 128, 136)
            mm([(sc, sg, G8)])
            act(junk, sc, ACT.Sign, bias=3.0, acc=V("kacc", 2 * t + s, 2 * t + s + 1))
            if s:
                kb = V(A(0)[0], 384, 385)
                mm([(kb, M("FK"), V("kacc", 2 * t + j, 2 * t + j + 1)) for j in range(2)])
                ts(V("kcol", 0, 1), kb, 16384.0, ALU.add)
                ts(M("HK%d" % (1 - t % 2)), H1, V("kcol", 0, 1), ALU.mult)

            phase("table")
            units([(UL, E(k, "Ew%d" % s), V(rm[0], 16 * k + 15, 16 * n, 256)) for k in range(16)], True, True, None)
            cp(ul, UL)
            ts(ul, ul, 15, ALU.bitwise_and)
            cp(ab, ul)
            mm([(NL, I1, V("base", 0, 16)), (sub(NL, 0, 8), I1, ab), (sub(NL, 8, 16), M("Sw"), ab)])
            cp(nl, NL)
            mms([(D(1), [(M("Ibh"), Mx)]), (D(2), [(M("Swh"), Mx)])])
            act(xq, ind(X, nl), ACT.Identity, bias=-0.25, scale=0.5)
            tt(xv, xq, D(1, 2), ALU.add)
            cp(ind(X, nl), xv)
        else:
            for k, nm in ((3, "yg"), (2, "yi"), (0, "ya"), (1, "yb")):
                pairs = [(T[nm][64 * s:64 * s + 64, n * h:n * h + n], ap(rows(oy(k), 64 * h, 64 * h + 64))) for h in range(2)]
                dma2("a" if s and k == 1 else "s", pairs, regs(oy(k)), [], "out%d" % (4 * s + k), "dma")

    turns = [reading(j // 2, j % 2) for j in range(2 * READS)]
    for j in range(2 * READS + 1):
        for r in turns[j:j + 1] + turns[max(j - 1, 0):j]:
            next(r, None)
    pick = lambda j, tag: [k for k, o in enumerate(ops) if (2 * o["t"] + o["s"], o["tag"], o["w"][0]) == (j, tag, "ag")]
    for j, m in enumerate(CFG["ahead"]):
        for k in pick(j, "choice"):
            ops[k]["deps"].update({d: False for d in pick(j + 1, "dist")[:m]})

    if "it" not in ORDER:
        ORDER["ops"] = ops
        ORDER["it"] = schedule(ops, EST, CFG["rounds"])
        places = None
        order, fin = ORDER["it"]
        order = sorted(order, key=lambda k: fin[k] - price(ops[k]["w"], EST))
        for tries, heat, parts, ncase, nudge in CFG["stages"]:
            order, fin, places = rhythm(ops, ORDER["it"][1], tries, heat, parts, places, ncase, nudge)
        ORDER["it"] = refine(ops, order, CFG["tries"], CFG["heat"])
    user = {}
    for k in ORDER["it"][0]:
        for b in ops[k]["banks"]:
            before, run = user.get(b, ([], []))
            if run and ops[run[0]]["q"] != ops[k]["q"]:
                before, run = run, []
            ops[k]["deps"].update({d: True for d in before})
            user[b] = (before, run + [k])
    order, fin = ORDER["it"]
    for k in order:
        if ops[k]["free"] is not None and ops[k]["free"][0] != "E":
            closer[ops[k]["free"]] = k

    eng = {"v": g.vector, "t": g.tensor, "a": g.scalar, "g": g, "s": g.sync}
    own = {"v": "qv", "t": "qt", "a": "qa", "g": "qg"}
    total = {}
    clk = {q: {} for q in eng}
    val = [None] * len(ops)
    opclk = [None] * len(ops)
    for k in order:
        o = ops[k]
        q = o["q"]
        if q == "n":
            val[k] = (o["sem"], o["inc"])
            opclk[k] = {o["sem"]: o["inc"]}
            total[o["sem"]] = o["inc"]
            continue
        c = clk[q]
        ds = [d for d, w in o["deps"].items() if w and ops[d]["sem"] != "left"]
        ds.sort(key=lambda d: -fin[d])
        for d in ds:
            s, v = val[d]
            if c.get(s, 0) < v:
                eng[q].wait_ge(T.sem[s], v)
                for s2, v2 in opclk[d].items():
                    if c.get(s2, 0) < v2:
                        c[s2] = v2
        ins = o["fn"]()
        s = o["sem"] or own[q]
        total[s] = total.get(s, 0) + o["inc"]
        if o["dma"]:
            for i in ins:
                i.then_inc(T.sem[s], 16)
        elif s != "left":
            ins.then_inc(T.sem[s], o["inc"])
        val[k] = (s, total[s])
        opclk[k] = dict(c)
        if s != "left":
            opclk[k][s] = val[k][1]
    for s in sorted(total):
        g.wait_ge(T.sem[s], total[s])
